import numpy as np, ml_dtypes
CORES = [36,164,52,180,100,228,116,244]
N = 8
BF = ml_dtypes.bfloat16
def gentries(a):
    return np.ascontiguousarray(a.reshape(8, 16, -1).transpose(0, 2, 1)).reshape(8, -1)
def gtable(e):
    e = np.asarray(e); return np.ascontiguousarray(e.reshape(8, -1, 16).transpose(0, 2, 1)).reshape(128, -1).astype(np.int32)
C, K, A, V, S = 1536, 512, 2, 3, 3
L = V * S
E = (V - 1) * S
def rock(rng, big=False):
    Q = C // 4; o = np.argsort(rng.random((N, 8, C)), axis=-1)
    a = np.where(rng.random((N, 8, 16, Q)) < 0.25, rng.integers(1, 3, (N, 8, 16, Q)), 0); a[:, :, 0] = rng.integers(0, 3, (N, 8, Q)); a[..., :Q // 16] = 0
    lv = [a]; pp = [rng.integers(0, Q // 16, (N, 8, Q))]
    for i in range(1, 4):
        j = rng.integers(0, Q, (N, 8, Q)); up = np.where(rng.random((N, 8, 16, Q)) < 0.15, rng.integers(1, 3, (N, 8, 16, Q)), 0); up[:, :, 0] = rng.integers(0, 3, (N, 8, Q))
        if big: up = up * rng.choice(np.array([1, 1, 2, 4]), (N, 8, 1, Q))
        lv.append(np.minimum(7, np.take_along_axis(lv[-1], j[:, :, None, :], 3) + up)); pp.append(j + (i - 1) * Q)
    fp = np.concatenate(lv, axis=3); pp = np.concatenate(pp, axis=2); inv = np.argsort(o, axis=-1)
    fm = np.ascontiguousarray(np.take_along_axis(fp, inv[:, :, None, :], 3)); nx = rng.integers(0, C, (N, 8, 16, C))
    nx[:, :, 0] = np.take_along_axis(o, np.take_along_axis(pp, inv, 2), 2)
    return fm, nx
def melts(rng):
    b = np.where(rng.random((N, 8, 16, K)) < 0.1, rng.integers(0, 4, (N, 8, 16, K)), rng.integers(4, 44, (N, 8, 16, K))); b[:, :, 0] = rng.integers(0, 16, (N, 8, K))
    w = np.where(rng.random((N, 8, 16, A * K)) < 0.5, rng.integers(0, 9, (N, 8, 16, A * K)), 0); w[:, :, 0] = rng.integers(0, 9, (N, 8, A * K))
    return b, w, rng.integers(0, C, (N, 8, K))
def link(fm, nx, g, a, form, row, after, partner):
    fm[:, g, :, a] = form; nx[:, g, row, a] = after; nx[:, g, 0, a] = partner
def mend(fm, nx, zs):
    low = np.take_along_axis(fm, nx[:, :, :1], 3)
    nx[:, :, 0] = np.where(np.any(low > fm, axis=2), np.array(zs).reshape(1, 8, 1), nx[:, :, 0])
def pack(fm, nx, w, b, m):
    return {"fm": np.ascontiguousarray(fm.reshape(N, 128, C)).astype(BF), "nx": np.ascontiguousarray(nx.reshape(N, 128, C)).astype(np.int32), "wl": np.ascontiguousarray(w.reshape(N, 128, A * K)).astype(BF),
            "b0": np.ascontiguousarray(b.reshape(N, 128, K)).astype(BF), "m0": np.stack([gtable(a) for a in m])}
def setup_inputs(rng):
    fm, nx = rock(rng); b, w, m = melts(rng)
    return pack(fm, nx, w, b, m)
def setup_inputs_spread(rng):
    fm, nx = rock(rng, True); b, w, m = melts(rng)
    b = np.minimum(255, (np.exp2(8 * rng.random((N, 8, 1, K))) * rng.random((N, 8, 16, K))).astype(np.int64))
    b[:, :, 0] = np.minimum(255, (np.exp2(8 * rng.random((N, 8, K)) * rng.random((N, 8, K))) - 1).astype(np.int64))
    w = np.minimum(255, (np.exp2(8 * rng.random((N, 8, 1, A * K))) * rng.random((N, 8, 16, A * K)) * rng.random((N, 8, 16, A * K))).astype(np.int64)) * (rng.random((N, 8, 1, A * K)) > 0.125)
    return pack(fm, nx, w, b, m)
def setup_inputs_ends(rng):
    full = rng.random((N, 8, 1, C)) < 0.3
    fm = 7 * (full | (rng.random((N, 8, 16, C)) < 0.3)).astype(np.int64)
    nx = np.where(rng.random((N, 8, 16, C)) < 0.75, (C - 1) * rng.integers(0, 2, (N, 8, 16, C)), rng.integers(0, C, (N, 8, 16, C))); nx[:, :, 0] = (C - 1) * rng.integers(0, 2, (N, 8, C))
    style = rng.integers(0, 4, (N, 8, 1, K)); rich = (np.arange(16) > 0).astype(np.int64).reshape(1, 1, 16, 1)
    b = 255 * np.where(style == 0, 0, np.where(style == 1, 1, np.where(style == 2, rng.integers(0, 2, (N, 8, 16, K)), rich)))
    w = 255 * rng.integers(0, 2, (N, 8, 16, A * K))
    m = np.where(rng.random((N, 8, K)) < 0.7, (C - 1) * rng.integers(0, 2, (N, 8, K)), rng.integers(0, C, (N, 8, K)))
    form = 7 * rich.reshape(16); zs = []
    for g in range(8):
        ch = [C - 1 - 2 * i for i in range(E - 1)] + [C - 2, 1]; z = 0; h = 1; half = 2
        idle = [3 + i for i in range((V - 3) * S)]
        if g % 2 == 1:
            ch = [C - 1 - a for a in ch]; z = C - 1; h = C - 2; half = C - 3; idle = [C - 1 - a for a in idle]
        for i in range(E): link(fm, nx, g, ch[i], form, 15, ch[i + 1], z)
        link(fm, nx, g, z, np.zeros(16, np.int64), 15, rng.integers(0, C, N), z)
        link(fm, nx, g, h, np.full(16, 7), 15, z, z)
        link(fm, nx, g, half, 7 * (np.arange(16) > 7), 15, ch[0], z)
        nx[:, g, 0, ch[E - 1]] = half; zs.append(z)
        way = idle + [ch[E - S]]
        for i in range(len(idle)): link(fm, nx, g, way[i], np.full(16, 7), 15, z, way[i + 1])
        pk = rng.permutation(K)
        ks = np.unique(np.concatenate([np.array([0, K // 2, K - 1]), pk[:K // 4]]))
        kc = np.setdiff1d(pk[K // 4:K // 4 + K // 16], ks); ka = np.concatenate([ks, kc])
        b[:, g, 0, ka] = 0; b[:, g, 1:, ka] = 255; m[:, g, ks] = ch[0]; m[:, g, kc] = way[0]
        for j in range(A):
            w[:, g, 0, j * K + ka] = 0; w[:, g, 1:, j * K + ka] = 255
    mend(fm, nx, zs)
    return pack(fm, nx, w, b, m)
def setup_inputs_corners(rng):
    fm, nx = rock(rng); b, w, m = melts(rng)
    u = rng.random(nx.shape); nx = np.where(u < 0.04, np.arange(C), np.where(u < 0.08, 0, np.where(u < 0.12, C - 1, nx)))
    kind = rng.integers(0, 3, (N, 8, 1, A * K)); w = np.where(kind == 0, 0, np.where(kind == 1, 255, rng.integers(0, 256, (N, 8, 16, A * K)))); w[:, :, 0] = rng.integers(0, 2, (N, 8, A * K))
    cls = rng.integers(0, 6, (N, 8, K)); cls[:, 7] = 4; cls[:, 7, 0] = 5; cls[:, 6] = 0; cls[:, 5] = 1; cls[:, :, K - 1] = np.arange(8) % 6
    rich = (np.arange(16) > 0).astype(np.int64).reshape(1, 1, 16, 1); c4 = cls[:, :, None, :]
    b = np.where(c4 == 0, 255, np.where(c4 == 1, 0, np.where(c4 == 2, b, 255 * rich)))
    m[:, 4] = rng.integers(0, C, (N, 1)); m[:, 5] = rng.integers(0, C, (N, 1)); m[:, 3, ::2] = 0; m[:, 3, 1::2] = C - 1; zs = []
    for g in range(8):
        nm = [int(a) for a in rng.permutation(C)[:L + 1]]; z = nm[L]; h = nm[L - 1]
        for i in range(L - 1): link(fm, nx, g, nm[i], rich.reshape(16), 15, nm[i + 1], z)
        link(fm, nx, g, h, 7 * (np.arange(16) == 0), 15, nm[0], z)
        link(fm, nx, g, z, np.zeros(16, np.int64), 15, rng.integers(0, C, N), z)
        zs.append(z); m[:, g] = np.where(cls[:, g] == 4, nm[0], np.where(cls[:, g] == 5, nm[1], m[:, g]))
    mend(fm, nx, zs)
    return pack(fm, nx, w, b, m)
def setup_inputs_calm(rng):
    fm, nx = rock(rng); b, w, m = melts(rng); w[:, :, 0] = rng.integers(0, 2, (N, 8, A * K)); zs = []
    part = rng.random((N, 8, K)); part[:, :, 0] = 0.0; part[:, :, K - 1] = 0.0
    still = rng.integers(20, 61, (N, 8, 16, K)); still[:, :, 0] = 0; still[:, :, 5] = 0
    b = np.where((part < 0.8)[:, :, None, :], still, b); r16 = np.arange(16)
    for g in range(8):
        j = g % 4; nm = [int(a) for a in rng.permutation(C)[:E + 3]]; h, q, z = nm[E], nm[E + 1], nm[E + 2]
        for i in range(E):
            if i < E - j: link(fm, nx, g, nm[i], 3 * (r16 == 5), 5, nm[i + 1], z)
            else: link(fm, nx, g, nm[i], ((r16 != 0) & (r16 != 5)).astype(np.int64), 15, nm[i + 1], z)
        link(fm, nx, g, h, 7 * (r16 == 0), 15, nm[0], q)
        link(fm, nx, g, q, 3 * (r16 == 0), 15, nm[0], z)
        link(fm, nx, g, z, np.zeros(16, np.int64), 15, rng.integers(0, C, N), z)
        zs.append(z); any_ = np.array(nm)[rng.integers(0, E + 1, (N, K))]
        m[:, g] = np.where(part[:, g] < 0.6, nm[0], np.where(part[:, g] < 0.8, any_, m[:, g]))
    mend(fm, nx, zs)
    return pack(fm, nx, w, b, m)
def check_inputs(d):
    bad = []
    for k, lo, hi in (("fm", 0, 7), ("nx", 0, C - 1), ("wl", 0, 255), ("b0", 0, 255), ("m0", 0, C - 1)):
        v = np.asarray(d[k]).astype(np.float64)
        if not (np.min(v) >= lo and np.max(v) <= hi): bad.append("range of " + k)
        if np.any(v != np.floor(v)): bad.append("whole numbers of " + k)
    fm = np.asarray(d["fm"]).astype(np.float32).reshape(N, 8, 16, C); p0 = np.clip(np.asarray(d["nx"]).astype(np.int64).reshape(N, 8, 16, C)[:, :, :1], 0, C - 1)
    if np.any(np.take_along_axis(fm, p0, 3) > fm): bad.append("partners in nx that are richer than their minerals in fm")
    return bad
def at(a, ix):
    return np.take_along_axis(a, ix[:, :, None, :], 3)
def one(a, ix):
    return np.take_along_axis(a, ix[:, :, None, :], 2)[:, :, 0]
def reference(fm, nx, wl, b0, m0):
    F = fm.astype(np.int64).reshape(N, 8, 16, C); X = nx.astype(np.int64).reshape(N, 8, 16, C); wall = wl.astype(np.int64).reshape(N, 8, 16, A * K)
    B = b0.astype(np.int64).reshape(N, 8, 16, K); m = np.stack([gentries(a) for a in m0]).astype(np.int64)
    lg = np.full((N, 8, L, K), -1, np.int64); n = np.zeros((N, 8, K), np.int64); c = np.full((N, 8, K), -1, np.int64)
    for v in range(V):
        if v > 0:
            B, m, lg, n, c = [np.roll(a, 1, axis=0) for a in (B, m, lg, n, c)]
            has = c >= 0; col = (one(lg, np.maximum(c, 0)) & (A - 1)) * K + np.arange(K)
            B = np.minimum(255, B + np.where(has[:, :, None, :], at(wall, col), 0))
            if v < V - 1:
                keep = np.ones((N, 8, A * K), np.int64); np.put_along_axis(keep, col, np.where(has, 0, 1), 2)
                wall = wall * keep[:, :, None, :]
        for s in range(S):
            f = at(F, m); short = B < f
            ok = ~np.any(short, axis=2); back = short[:, :, 0] & ~np.any(short[:, :, 1:], axis=2) & (c >= 0)
            B = B - np.where(ok[:, :, None, :], f, 0)
            low = B < f; p = np.where(np.any(low, axis=2), np.argmax(low, axis=2), 15)
            after = one(at(X, m), p)
            t = np.where(back, one(lg, np.maximum(c, 0)), m); pi = np.take_along_axis(X[:, :, 0], t, 2)
            B = B + np.where(back[:, :, None, :], at(F, t) - at(F, pi), 0)
            slot = np.where(ok, n, np.maximum(c, 0)); new = np.where(ok, m, np.where(back, pi, one(lg, slot)))
            np.put_along_axis(lg, slot[:, :, None, :], new[:, :, None, :], 2)
            c = np.where(ok, n, np.where(back, c - 1, c)); n = n + ok; m = np.where(back, m, after)
    return {"yb": B.reshape(N, 128, K).astype(np.float32), "yl": np.stack([gtable(a.reshape(8, L * K)) for a in lg]).astype(np.float32),
            "ym": np.stack([gtable(a) for a in m]).astype(np.float32), "yc": np.stack([gtable(a) for a in c]).astype(np.float32)}

@@ -1,0 +1,526 @@
+from concourse.mybir import AluOpType as ALU, ActivationFunctionType as AF
+
+C, K, V_, S_ = 1536, 512, 3, 3
+NST = V_ * S_
+NH = 2
+NHD = 2
+REV = True
+
+SCRATCH = {
+    "F": ("sbuf", [128, C], "bfloat16"),
+    "fg0": ("sbuf", [128, K], "bfloat16"), "fg1": ("sbuf", [128, K], "bfloat16"),
+    "dg0": ("sbuf", [128, K], "bfloat16"), "dg1": ("sbuf", [128, K], "bfloat16"),
+    "wg": ("sbuf", [128, K], "bfloat16"), "ex": ("sbuf", [128, K], "bfloat16"), "top": ("sbuf", [128, K], "bfloat16"),
+    "Bs0": ("sbuf", [128, K], "bfloat16"), "Bs1": ("sbuf", [128, K], "bfloat16"),
+    "IB": ("sbuf", [128, 128], "bfloat16"), "IH": ("sbuf", [128, 128], "bfloat16"), "NB": ("sbuf", [128, 128], "bfloat16"),
+    "NC": ("sbuf", [128, 128], "bfloat16"),
+    "X": ("sbuf", [128, C], "int32"), "DT": ("sbuf", [128, 2 * C + 16], "bfloat16"),
+    "U": ("sbuf", [128, C + 16], "bfloat16"), "W": ("sbuf", [128, 2 * K + 16], "bfloat16"),
+    "Bi": ("sbuf", [128, K], "bfloat16"), "mi": ("sbuf", [128, 32], "int32"),
+    "Bf": ("sbuf", [128, K], "float32"),
+    "SU0": ("sbuf", [128, 2 * K], "bfloat16"), "SU1": ("sbuf", [128, 2 * K], "bfloat16"),
+    "lw0": ("sbuf", [128, K], "bfloat16"), "lw1": ("sbuf", [128, K], "bfloat16"),
+    "mk0": ("sbuf", [128, K], "bfloat16"), "mk1": ("sbuf", [128, K], "bfloat16"),
+    "xs0": ("sbuf", [128, K], "float16"), "xs1": ("sbuf", [128, K], "float16"),
+    "sm": ("sbuf", [128, 32 * 170], "float32"), "sb": ("sbuf", [128, 32 * 90], "bfloat16"),
+    "sh": ("sbuf", [128, 32 * 90], "float16"), "su": ("sbuf", [128, 32 * 40], "uint16"),
+    "si": ("sbuf", [128, 32 * 8], "int32"),
+    "lB1": ("sbuf", [128, K], "bfloat16"), "lB2": ("sbuf", [128, K], "bfloat16"),
+    "lS1": ("sbuf", [128, 32 * 6], "float32"), "lS2": ("sbuf", [128, 32 * 9], "float32"),
+    "lm1": ("sbuf", [128, 32], "uint16"), "lm2": ("sbuf", [128, 32], "uint16"),
+    "lI1": ("sbuf", [128, 96], "uint16"), "lI2": ("sbuf", [128, 96], "uint16"),
+    "lD1": ("sbuf", [128, K], "bfloat16"), "lD2": ("sbuf", [128, K], "bfloat16"), "ug": ("sbuf", [128, K], "bfloat16"),
+    "xa": ("sbuf", [128, 96], "int32"), "xf": ("sbuf", [128, 96], "float32"), "xt": ("sbuf", [128, 96], "float32"),
+    "xu": ("sbuf", [128, 96], "uint16"), "xc": ("sbuf", [128, 96], "int32"), "xy": ("sbuf", [128, 96], "float32"),
+    "xh": ("sbuf", [128, 96], "bfloat16"), "xl": ("sbuf", [128, 96], "bfloat16"),
+    "pi": ("sbuf", [128, 8], "int32"), "pc": ("sbuf", [128, 16], "float32"),
+    "xi": ("sbuf", [128, 144], "float32"), "dd": ("sbuf", [128, 144], "float32"), "rel": ("sbuf", [128, 128], "float32"),
+    "EA": ("sbuf", [128, 144], "float16"), "EB": ("sbuf", [128, 144], "bfloat16"),
+    "cl": ("sbuf", [128, 128], "float32"), "SG": ("sbuf", [128, 128], "float32"), "I32": ("sbuf", [128, 128], "float32"),
+    "g0": ("sbuf", [128, 128], "float32"), "T2b": ("sbuf", [128, 128], "float32"), "T1b": ("sbuf", [128, 128], "float32"),
+    "T1": ("sbuf", [128, 128], "bfloat16"), "T2": ("sbuf", [128, 128], "bfloat16"),
+    "I16": ("sbuf", [128, 128], "float16"), "NI": ("sbuf", [128, 128], "bfloat16"),
+    "PLC": ("sbuf", [128, 288], "float32"), "ri": ("sbuf", [128, 32], "float32"), "rep": ("sbuf", [128, 32], "uint16"),
+    "rf": ("sbuf", [128, 32], "float32"), "ki": ("sbuf", [128, 32], "float32"), "kk": ("sbuf", [128, 32], "float32"),
+    "yo": ("sbuf", [128, 288], "float32"),
+    "z0": ("psum", [128, 512], "float32"), "z1": ("psum", [128, 512], "float32"),
+    "BA": ("psum", [128, 512], "float32"), "BB": ("psum", [128, 512], "float32"),
+    "PB": ("psum", [128, 512], "float32"), "PA": ("psum", [128, 512], "float32"),
+    "PL": ("psum", [128, 512], "float32"), "PT": ("psum", [128, 512], "float32"),
+}
+O0A, BFA = False, True
+MERGE = True
+BSV = False
+NHG = 1
+UMODE = ["none", "next", "sep", "next", "next", "sep", "next", "next", "sep"]
+PSUM = ("z0", "z1", "BA", "BB", "PB", "PA", "PL", "PT")
+NDMA = 40
+SEMAPHORES = ["eV", "eA", "eP", "eG"] + ["d%d" % i for i in range(NDMA)] + ["r%d" % i for i in range(12)] + ["l%d" % i for i in range(12)]
+
+CY, PCY = 0.83e-3, 0.6e-3
+HOP, SAME = 0.12, 0.07
+
+
+def plan(T, g, dst_addr, mask, neng):
+    ops = []
+    used = {"sm": 0, "sb": 0, "sh": 0, "su": 0, "si": 0}
+
+    def new(buf, blocks=1):
+        a = used[buf]; used[buf] += 32 * blocks
+        return (buf, a, a + 32 * blocks)
+
+    def ap(r):
+        return T[r[0]][:, r[1]:r[2]]
+
+    def whole(n):
+        return (n, 0, SCRATCH[n][1][1])
+
+    def sub(r, a, b):
+        return (r[0], r[1] + a, r[1] + b)
+
+    def add(eng, fn, rd, wr, cost, kind="c", lat=0.0):
+        ops.append({"e": eng, "fn": fn, "rd": rd, "wr": wr, "cost": cost, "kind": kind, "lat": lat})
+
+    def two(r):
+        return SCRATCH[r[0]][2] in ("bfloat16", "float16", "uint16")
+
+    def n_of(r):
+        return r[2] - r[1]
+
+    def ts(o, i, s1, op0, s2=None, op1=None, cols=()):
+        c = max(64, n_of(o) * (0.5 if two(o) and two(i) else 1)) * CY
+        if op1 is None:
+            add("V", lambda: g.vector.tensor_scalar(ap(o), ap(i), s1, None, op0), [i] + list(cols), [o], c)
+        else:
+            add("V", lambda: g.vector.tensor_scalar(ap(o), ap(i), s1, s2, op0, op1), [i] + list(cols), [o], c)
+
+    def tt(o, a, b, op):
+        c = max(64, n_of(o) * (1 if a[0] in PSUM or b[0] in PSUM else 2)) * CY
+        add("V", lambda: g.vector.tensor_tensor(ap(o), ap(a), ap(b), op), [a, b], [o], c)
+
+    def cp(o, i):
+        add("V", lambda: g.vector.tensor_copy(ap(o), ap(i)), [i], [o], max(64, n_of(o)) * CY)
+
+    def gt(o, win, off, b, op, oap=None):
+        oa = ap(o) if oap is None else oap
+        add("V", lambda: g.vector.tensor_tensor(oa, ap(win).indirect(ap(off)), ap(b), op), [win, off, b], [o],
+            0.05 + 1.5 * n_of(o) * CY)
+
+    def act(o, i, func=AF.Identity, bias=0.0, scale=1.0, cols=()):
+        add("A", lambda: g.scalar.activation(ap(o), ap(i), func, bias=bias, scale=scale), [i] + list(cols), [o],
+            max(64, n_of(o)) * CY + 0.03)
+
+    def agather(o, win, off, bias=0.0):
+        add("A", lambda: g.scalar.activation(ap(o), ap(win).indirect(ap(off)), AF.Identity, bias=bias), [win, off], [o],
+            0.065 + 1.5 * n_of(o) * CY)
+
+    def mm(o, items, rd, start=True, stop=True):
+        def fn():
+            for i, (l, r, _) in enumerate(items):
+                ins = g.tensor.matmul(ap(o), l, r, start and i == 0, stop and i == len(items) - 1)
+            return ins
+        add("P", fn, rd, [o], sum(x[2] for x in items) * PCY, kind="c" if start else "acc")
+
+    def dma(q, o, i, rd, wr, kb):
+        eng = g.sync if q == "S" else (g.scalar if q == "A" else g)
+        add(q, lambda: eng.dma_start(o, i), rd, wr, 0.06, kind="dma", lat=1.8 + kb / 250.0)
+
+    def remote(land, src):
+        kb = n_of(src) * (2 if two(src) else 4) / 8.0
+        add("G", lambda rs, ls: g.remote_dma(ap(land), ap(src), rs, ls, dst_addr[1], dst_addr[0], mask), [src], [land], 0.5,
+            kind="rem", lat=2.0 + kb / 100.0)
+
+    def iota(o, pattern, base, cm):
+        if SCRATCH[o[0]][2] == "int32":
+            add("G", lambda: g.iota(ap(o), pattern, base, cm), [], [o], 0.13 + 2 * n_of(o) * CY)
+        else:
+            add("G", lambda: g.iota(ap(o), pattern, base, cm, allow_small_or_imprecise_dtypes=True), [], [o], 0.13 + 2 * n_of(o) * CY)
+
+    def col(j):
+        return ("pc", j, j + 1)
+
+    dma("S", T.mi[:, :], T.m0[:, :], [], [whole("mi")], 16)
+    dma("S", T.F[:, :], T.fm[:, :], [], [whole("F")], 384)
+    dma("A", T.Bi[:, :], T.b0[:, :], [], [whole("Bi")], 128)
+    dma("S", T.xc[:, :], T.nx[0::16, :], [], [whole("xc")], 450)
+    for blk in range(3):
+        for gg in range(2):
+            a = 32 * blk + 16 * gg
+            dma("S", T.xa[:, a:a + 16], T.nx[16 * gg::32, 512 * blk:512 * blk + 512], [], [("xa", a, a + 16)], 500)
+    dma("S", T.X[:, :], T.nx[:, :], [], [whole("X")], 1000)
+    for i, o in enumerate(ops):
+        o["first"] = 100.0 - i
+    iota(("pi", 0, 1), [[0, 1]], 0, 1)
+    iota(whole("xi"), [[1, 144]], 0, 0)
+    iota(whole("rel"), [[1, 128]], 0, -1)
+    ts(("pi", 4, 5), ("pi", 0, 1), 112, ALU.bitwise_and)
+    cp(col(0), ("pi", 4, 5))
+    tt(col(1), ("pi", 0, 1), ("pi", 4, 5), ALU.subtract)
+    ts(col(2), col(1), 1.0, ALU.min, 3.0, ALU.mult)
+    ts(col(3), col(2), -1.0, ALU.add)
+    ts(col(4), col(1), 15.0, ALU.is_equal, 2048.0, ALU.mult)
+    ts(whole("dd"), whole("xi"), ap(col(0)), ALU.subtract, cols=[col(0)])
+    ts(whole("EB"), whole("dd"), 15.0, ALU.is_equal, ap(col(3)), ALU.mult, cols=[col(3)])
+    ts(whole("EA"), whole("dd"), 15.0, ALU.is_equal)
+    ts(whole("cl"), ("dd", 0, 128), 0.0, ALU.max, 15.0, ALU.min)
+    tt(whole("SG"), whole("cl"), ("dd", 0, 128), ALU.is_equal)
+    ts(whole("I32"), whole("rel"), 0.0, ALU.is_equal)
+    ts(whole("g0"), whole("rel"), 0.0, ALU.is_gt, -2.0, ALU.mult)
+    tt(whole("T2b"), whole("I32"), whole("g0"), ALU.add)
+    tt(whole("T2"), whole("T2b"), whole("SG"), ALU.mult)
+    act(whole("T1b"), whole("T2b"), bias=-4.0, scale=512.0)
+    tt(whole("T1"), whole("T1b"), whole("SG"), ALU.mult)
+    cp(whole("I16"), whole("I32"))
+    act(whole("NI"), whole("I32"), scale=-4096.0)
+    iota(whole("PLC"), [[1, 9], [0, 32]], 1, 0)
+    iota(("ri", 0, 18), [[0, 9], [16, 2]], 0, 1)
+    ts(("rep", 0, 18), ("ri", 0, 18), ap(col(0)), ALU.subtract, cols=[col(0)])
+    iota(whole("ki"), [[16, 32]], 16 + K, 1)
+    ts(whole("kk"), whole("ki"), ap(col(0)), ALU.subtract, cols=[col(0)])
+    act(whole("IB"), whole("I32"))
+    act(whole("IH"), whole("I32"), scale=0.5)
+    act(whole("NB"), whole("I32"), scale=-1.0)
+    act(whole("NC"), whole("I32"), scale=-0.5)
+    add("V", lambda: g.vector.memset(T.top[:, :], 255.0), [], [whole("top")], 256 * CY)
+    add("V", lambda: g.vector.memset(T.DT[:, C:C + 1] if REV else T.DT[:, 0:1], 0.0), [], [("DT", C, C + 1) if REV else ("DT", 0, 1)], 64 * CY)
+    NF = ("DT", C + 1, 2 * C + 1)
+    ts(NF, whole("F"), -1.0, ALU.mult)
+    ts(whole("xf"), whole("xa"), 1.0 if REV else 0.0, ALU.add)
+    add("V", lambda: g.vector.transpose(T.xt[:, :], T.xf[:, :]), [whole("xf")], [whole("xt")], 96 * CY)
+    cp(whole("xu"), whole("xt"))
+    for i in range(3):
+        hi = C - 1 - 512 * i
+        gt(("DT", hi - 511, hi + 1), ("DT", C, 2 * C + 1), ("xu", 32 * i, 32 * i + 32), ("F", 512 * i, 512 * i + 512), ALU.add,
+           oap=T.DT[:, hi:hi - 512:-1] if i < 2 else T.DT[:, hi::-1])
+    add("V", lambda: g.vector.memset(T.U[:, :], 0.0), [], [whole("U")], 776 * CY)
+    ts(whole("xy"), whole("xc"), 1.0, ALU.add, 0.5, ALU.mult)
+    act(whole("xh"), whole("xy"))
+    tt(whole("xl"), whole("xy"), whole("xh"), ALU.subtract)
+    dma("S", T.U[1::16, 1:C + 1], T.xh[:, :], [whole("xh"), ("U", 0, 1)], [("U", 1, 2)], 64)
+    dma("S", T.U[2::16, 1:C + 1], T.xl[:, :], [whole("xl"), ("U", 0, 1)], [("U", 2, 3)], 64)
+    add("V", lambda: g.vector.memset(T.W[:, 0:16], 0.0), [], [("W", 0, 16)], 64 * CY)
+    DTW = ("DT", 0, 2 * C + 1)
+    UW = ("U", 0, C + 1)
+
+    mu = new("su"); cp(mu, whole("mi"))
+    m = new("sm"); cp(m, whole("mi"))
+    mm(whole("BA"), [(T.IB[:, :], T.Bi[:, :], K)], [whole("IB"), whole("Bi")])
+    mm(whole("BB"), [(T.IH[:, :], T.Bi[:, :], K)], [whole("IH"), whole("Bi")])
+    parts = []
+    t1 = c1 = n1 = amp = OCp = th = wprev = pend = None
+
+    def write(s, o0, q, place, uq, stop):
+        bu = new("sm"); tt(bu, uq, o0, ALU.mult)
+        dv = new("sm"); tt(dv, q, bu, ALU.add)
+        M2 = new("sh", s); gt(M2, dv, ("rep", 0, 2 * s), place, ALU.mult)
+        parts.insert(0, M2)
+        if s < NST - 2:
+            logsum()
+
+    def logsum():
+        now = list(parts)
+
+        def fn():
+            for i, x in enumerate(now):
+                ins = g.tensor.matmul(T.PL[:, 0:n_of(x)], T.I16[:, :], ap(x), i == 0, i == len(now) - 1)
+            return ins
+        add("P", fn, [whole("I16")] + now, [("PL", 0, n_of(now[0]))], sum(max(64, n_of(x)) for x in now) * PCY)
+
+    for s in range(NST):
+        last = s == NST - 1
+        vend = s % S_ == S_ - 1 and not last
+        SU, lw, mk, xs = whole("SU%d" % (s % 2)), whole("lw%d" % (s % 2)), whole("mk%d" % (s % 2)), whole("xs%d" % (s % 2))
+        h = K // NH; hl = h // 16
+        m1 = new("sm"); act(m1, m, bias=1.0)
+        fg = whole("fg%d" % (s % 2))
+        for i in range(NH):
+            agather(sub(fg, i * h, i * h + h), whole("F"), sub(mu, i * hl, i * hl + hl))
+        for i in range(NH):
+            tt(sub(SU, i * h, i * h + h), sub(fg, i * h, i * h + h), ("BA", i * h, i * h + h), ALU.is_gt)
+            tt(sub(lw, i * h, i * h + h), sub(fg, i * h, i * h + h), ("BB", i * h, i * h + h), ALU.is_gt)
+        if s == 0:
+            Bs, shift, LA, LB = whole("Bi"), 0.0, "IB", "IH"
+        elif s % S_ == 0:
+            Bs, shift, LA, LB = whole("ex"), 127.5, "NB", "NC"
+            act(Bs, whole("BA"), AF.Relu, bias=255.0, scale=-1.0)
+        else:
+            Bs, shift, LA, LB = whole("Bs%d" % (s % 2)), 128.0, "IB", "IH"
+            if BSV:
+                ts(Bs, whole("BA"), -128.0, ALU.add)
+            else:
+                act(Bs, whole("BA"), bias=-128.0)
+        if not vend:
+            mm(whole("BA"), [(T[LA][:, :], ap(Bs), K)] + ([(T.IB[:, :], T.top[:, :], K)] if LA == "NB" else []),
+               [whole(LA), whole("IB"), whole("top"), Bs], stop=False)
+        if not (last or vend):
+            mm(whole("BB"), [(T[LB][:, :], ap(Bs), K)] + ([(T.IH[:, :], T.top[:, :], K)] if LA == "NB" else []),
+               [whole(LB), whole("IH"), whole("top"), Bs], stop=False)
+        if LA == "NB":
+            shift = 0.0
+        if s == 0:
+            dma("S", T.W[:, 16:16 + 2 * K], T.wl[:, :], [sub(lw, 0, 1)], [("W", 16, 16 + 2 * K)], 256)
+        if vend:
+            remote(whole("lB%d" % (s // S_ + 1)), Bs)
+        nb = 64 if UMODE[s] == "now" or pend is not None else 32
+        if UMODE[s] == "now":
+            agather(sub(SU, K, 2 * K), UW, th)
+        if UMODE[s] == "next":
+            agather(("SU%d" % ((s + 1) % 2), K, 2 * K), UW, th)
+        mm(("PB", 0, nb), [(T.EB[:, 15 - j:143 - j], T[SU[0]][:, j:16 * nb:16], 64) for j in range(16)],
+           [whole("EB"), sub(SU, 0, 16 * nb)])
+        for i in range(NH):
+            z = ("z%d" % i, 0, h)
+            mm(z, [(T.T1[:, :], ap(sub(SU, i * h, i * h + h)), max(64, h))], [whole("T1"), sub(SU, i * h, i * h + h)], stop=False)
+            mm(z, [(T.T2[:, :], ap(sub(lw, i * h, i * h + h)), max(64, h))], [whole("T2"), sub(lw, i * h, i * h + h)], start=False)
+            act(sub(mk, i * h, i * h + h), z, AF.Relu, bias=ap(col(4)), scale=2048.0, cols=[col(4)])
+            gt(sub(xs, i * h, i * h + h), whole("X"), sub(mu, i * hl, i * hl + hl), sub(mk, i * h, i * h + h), ALU.min)
+        Cq, Uq = ("PB", 0, 32), ("PB", 32, 64)
+        if vend:
+            msg = new("sm", 4 + s)
+            t1n, c1n, n1n, am = sub(msg, 0, 32), sub(msg, 32, 64), sub(msg, 64, 96), sub(msg, 96, 128)
+        else:
+            t1n, c1n, n1n, am = new("sm"), new("sm"), new("sm"), new("sm" if last or s == 0 else "sh")
+        ok = new("sm"); ts(ok, Cq, 0.0, ALU.is_equal)
+        tt(am, ok, m1, ALU.mult)
+        idx = new("su")
+        items = [(T.EA[:, 15 - j:143 - j], T[xs[0]][:, j:K:16], 64) for j in range(16)]
+        mn = new("sm"); mun = new("su")
+        if s == 0:
+            cp(idx, am)
+            c1n = ok
+            ts(n1n, ok, 1.0, ALU.add)
+            t1n = am
+            OC = ok
+            thn = idx
+            mm(("PA", 0, 32), items, [whole("EA"), xs])
+            cp(mun, ("PA", 0, 32))
+            act(mn, ("PA", 0, 32))
+        else:
+            o0 = new("sm")
+            if O0A:
+                act(o0, Cq, AF.Relu, scale=-1.0)
+            else:
+                ts(o0, Cq, -1.0, ALU.is_equal)
+            if not last:
+                rs = new("sm"); ts(rs, Cq, 1.0, ALU.is_ge)
+            if pend is not None:
+                write(pend[0], pend[1], pend[2], pend[3], Uq, False)
+                pend = None
+            bt = new("sm"); tt(bt, o0, t1, ALU.mult)
+            r = new("sm"); tt(r, am, bt, ALU.subtract)
+            ts(idx, r, float(C), ALU.add)
+            bf = new("sb")
+            if BFA:
+                act(bf, bt, AF.Sign)
+            else:
+                ts(bf, bt, 1.0, ALU.min)
+            w = new("sm"); tt(w, bf, m, ALU.mult)
+            mm(("PA", 0, 32), [(T.NI[:, :], ap(bf), 64)] + items, [whole("EA"), whole("NI"), xs, bf])
+            tt(mn, ("PA", 0, 32), w, ALU.max)
+            if not (last or vend):
+                cp(mun, mn)
+            an = new("sm"); tt(an, ok, n1, ALU.mult)
+            y = new("sm"); tt(y, c1, o0, ALU.subtract)
+            tt(c1n, y, an, ALU.max)
+            if not last:
+                tt(n1n, n1, ok, ALU.add)
+            q = new("sm"); tt(q, amp, bt, ALU.subtract)
+            nw = s - 1 if vend else s + 1
+            OC = new("sb", nw); gt(OC, n1 if last else c1n, ("rep", 0, 2 * nw), ("PLC", 0, 32 * nw), ALU.is_equal)
+            if not last:
+                ra = new("sh"); tt(ra, rs, amp, ALU.mult)
+                if s == 1:
+                    tt(t1n, ra, am, ALU.add)
+                    thn = new("su"); cp(thn, t1n)
+                else:
+                    M4 = new("sh", s - 1); tt(M4, ("PL", 0, 32 * s - 32), sub(OC, 0, 32 * s - 32), ALU.mult)
+                    mm(("PT", 0, 32), [(T.I32[:, :], ap(am), 256) if vend else (T.I16[:, :], ap(am), 64), (T.I16[:, :], ap(ra), 64)]
+                       + [(T.I16[:, :], ap(sub(M4, 32 * i, 32 * i + 32)), 64) for i in range(s - 1)],
+                       [whole("I32"), whole("I16"), am, ra, M4])
+                    if vend:
+                        imsg = new("su", 3)
+                        ti = new("si"); ts(ti, ("PT", 0, 32), 2048.0, ALU.mult)
+                        cp(sub(imsg, 32, 64), ("PT", 0, 32))
+                    else:
+                        thn = new("su"); cp(thn, ("PT", 0, 32))
+                    act(t1n, ("PT", 0, 32))
+            if UMODE[s] == "next":
+                pend = (s, o0, q, OCp)
+            else:
+                if UMODE[s] == "sep":
+                    ug = whole("ug")
+                    agather(ug, UW, th)
+                    Uq = ("PB", 64, 96)
+                    mm(Uq, [(T.EB[:, 15 - j:143 - j], T.ug[:, j:K:16], 64) for j in range(16)], [whole("EB"), ug])
+                write(s, o0, q, OCp, Uq, vend)
+            if vend:
+                act(sub(msg, 128, 128 + 32 * s), ("PL", 0, 32 * s))
+        dg = whole("dg%d" % (s % 2))
+        hg = K // NHG
+        for i in range(NHG):
+            part = sub(dg, i * hg, i * hg + hg)
+            agather(part, DTW if s else ("DT", C, 2 * C + 1), sub(idx, i * hg // 16, (i + 1) * hg // 16), bias=shift)
+            if not vend:
+                mm(("BA", i * hg, i * hg + hg), [(T.IB[:, :], ap(part), hg)], [whole("IB"), part], start=False, stop=(i == NHG - 1))
+            if not (last or vend):
+                mm(("BB", i * hg, i * hg + hg), [(T.IH[:, :], ap(part), hg)], [whole("IH"), part], start=False, stop=(i == NHG - 1))
+        if last:
+            hd = K // NHD
+            for i in range(NHD):
+                part = ("Bf", i * hd, i * hd + hd)
+                act(part, ("BA", i * hd, i * hd + hd))
+                dma("S", T.yb[:, i * hd:i * hd + hd], ap(part), [part], [], 256 // NHD)
+            M5 = new("sh", 9); gt(M5, am, ("rep", 0, 18), OC, ALU.mult)
+            parts.insert(0, M5)
+            logsum()
+            act(whole("yo"), ("PL", 0, 288), bias=-1.0)
+            yc = new("sm"); act(yc, c1n, bias=-1.0)
+            dma("S", T.yc[:, :], ap(yc), [yc], [], 16)
+            dma("S", T.yl[:, :], T.yo[:, :], [whole("yo")], [], 144)
+            dma("S", T.ym[:, :], ap(mn), [mn], [], 16)
+            break
+        if vend:
+            v = s // S_ + 1
+            lB, lD, lS, lI, lm = (whole(x + str(v)) for x in ("lB", "lD", "lS", "lI", "lm"))
+            pa = new("si"); ts(pa, ti, 2, ALU.arith_shift_right, 512, ALU.bitwise_and)
+            x2 = new("sm"); tt(x2, whole("kk"), pa, ALU.subtract)
+            x3 = new("sm"); tt(x3, x2, ti, ALU.min)
+            if wprev is not None:
+                ne = new("sm"); tt(ne, x3, wprev, ALU.not_equal)
+                x4 = new("sm"); tt(x4, x3, ne, ALU.mult)
+            else:
+                x4 = x3
+            wprev = x3
+            cp(sub(imsg, 0, 32), x4)
+            cp(sub(imsg, 64, 96), mn)
+            remote(lD, dg)
+            if MERGE:
+                remote(lI, imsg)
+                mun = sub(lI, 64, 96)
+            else:
+                remote(sub(lI, 0, 64), sub(imsg, 0, 64)); remote(lm, sub(imsg, 64, 96))
+                mun = lm
+            remote(lS, msg)
+            t1n, c1n, n1n, am = sub(lS, 0, 32), sub(lS, 32, 64), sub(lS, 64, 96), sub(lS, 96, 128)
+            thn = sub(lI, 32, 64)
+            mn = new("sm"); cp(mn, mun)
+            wg = whole("wg")
+            add("V", lambda a=sub(lI, 0, 32): g.vector.tensor_copy(T.wg[:, :], T.W[:, :].indirect(ap(a))),
+                [whole("W"), sub(lI, 0, 32)], [wg], 0.05 + 1.5 * n_of(wg) * CY)
+            for i, x in enumerate((lB, lD, wg)):
+                mm(whole("BA"), [(T.IB[:, :], ap(x), K)], [whole("IB"), x], start=(i == 0), stop=(i == 2))
+                mm(whole("BB"), [(T.IH[:, :], ap(x), K)], [whole("IH"), x], start=(i == 0), stop=(i == 2))
+            OC = new("sb", s + 1); gt(OC, c1n, ("rep", 0, 2 * s + 2), ("PLC", 0, 32 * s + 32), ALU.is_equal)
+            Ll = sub(lS, 128, 128 + 32 * s)
+            Lh = new("sh", s); cp(Lh, Ll)
+            parts[:] = [Lh]
+            logsum()
+        m, mu, t1, c1, n1, amp, OCp, th = mn, mun, t1n, c1n, n1n, am, OC, thn
+    return ops
+
+
+def depend(ops):
+    def meet(a, b):
+        return a[0] == b[0] and (a[0] in PSUM or (a[1] < b[2] and b[1] < a[2]))
+    deps = []
+    for i, o in enumerate(ops):
+        d = {}
+        for j in range(i):
+            p = ops[j]
+            raw = any(meet(a, b) for a in o["rd"] + o["wr"] for b in p["wr"])
+            war = any(meet(a, b) for a in o["wr"] for b in p["rd"])
+            rar = o["e"] != p["e"] and any(a[0] == b[0] and a[0] in PSUM for a in o["rd"] for b in p["rd"])
+            if raw or rar:
+                d[j] = "done"
+            elif war:
+                d[j] = "left" if p["kind"] == "rem" else "done"
+        deps.append(d)
+    return deps
+
+
+def order(ops, deps, bump=None):
+    n = len(ops)
+    succ = [[] for _ in ops]
+    for i, d in enumerate(deps):
+        for j in d:
+            succ[j].append(i)
+    tail = [0.0] * n
+    for i in range(n - 1, -1, -1):
+        tail[i] = ops[i]["cost"] + ops[i]["lat"] + max([HOP + tail[k] for k in succ[i]] + [0.0])
+    tail = [tail[i] + ops[i].get("first", 0.0) + (bump[i] if bump is not None else 0.0) for i in range(n)]
+    free = {e: 0.0 for e in "VAPGS"}
+    end = [None] * n; left = [len(d) for d in deps]; ready = [0.0] * n
+    cand = [i for i in range(n) if left[i] == 0]; out = []
+    while cand:
+        t0 = min(max(ready[i], free[ops[i]["e"]]) for i in cand)
+        near = [i for i in cand if max(ready[i], free[ops[i]["e"]]) <= t0 + 1e-9]
+        e = ops[near[0]]["e"]
+        pool = [i for i in cand if ops[i]["e"] == e and max(ready[i], free[e]) <= t0 + SLACK]
+        i = max(pool, key=lambda k: tail[k])
+        st = max(ready[i], free[e]); free[e] = st + ops[i]["cost"]; end[i] = free[e] + ops[i]["lat"]
+        ops[i]["st"] = st
+        cand.remove(i); out.append(i)
+        for k in succ[i]:
+            same = ops[k]["e"] == e and ops[i]["kind"] in ("c", "acc")
+            hop = (0.0 if e == "P" else SAME) if same else HOP
+            ready[k] = max(ready[k], end[i] + hop); left[k] -= 1
+            if left[k] == 0:
+                cand.append(k)
+    return out, max(end)
+
+
+SLACK = 0.08
+LOADS = [0, 1, 2, 10, 4, 5, 6, 7, 8, 9, 3]
+
+
+ORDER = [13,12,11,42,57,51,14,15,25,43,20,16,26,36,23,24,27,2,10,1,3,4,0,5,6,7,8,9,38,60,39,19,34,37,59,35,17,22,58,31,29,30,18,28,21,44,63,65,61,66,71,73,74,64,67,72,45,52,68,53,32,62,46,47,54,56,55,77,78,81,82,83,75,76,69,70,79,80,41,40,88,48,85,86,50,89,92,94,90,95,103,104,93,96,87,101,84,97,49,102,113,111,105,106,115,91,112,98,107,108,109,110,116,117,114,129,118,119,123,130,100,120,99,126,121,122,124,132,133,136,125,131,138,137,180,135,140,127,142,134,139,33,128,141,145,144,155,153,156,157,149,150,151,146,147,161,164,169,154,168,158,162,170,159,163,187,173,152,174,160,175,176,148,177,178,179,165,188,189,190,172,166,167,191,192,171,181,182,183,184,185,186,143,198,193,194,197,209,199,200,201,196,202,208,210,203,211,219,220,212,223,218,213,224,195,205,204,217,221,214,207,222,206,215,229,227,231,228,242,232,225,226,234,233,250,235,239,240,241,236,237,238,243,230,245,254,244,246,216,251,256,252,257,255,258,253,247,265,248,259,266,267,268,264,275,269,270,273,249,281,290,277,274,260,261,262,271,272,282,283,278,284,286,279,293,289,285,276,287,291,288,263,295,280,294,296,292,300,304,301,306,302,307,305,308,297,298,309,303,313,314,315,316,312,325,321,323,324,299,310,348,311,326,322,336,337,327,317,318,319,329,332,338,330,341,331,355,363,342,328,343,344,320,345,333,346,356,347,357,340,358,359,360,334,335,361,362,364,349,350,351,352,339,353,354,368,369,371,367,370,372,378,373,380,389,379,382,388,387,366,377,384,381,390,391,383,397,399,398,393,394,395,365,401,402,404,409,403,420,392,386,385,396,406,421,405,400,410,412,411,415,414,407,408,423,375,413,374,376,416,424,426,422,427,425,428,417,418,429,435,436,437,438,419,430,434,445,439,440,441,443,451,454,433,431,432,444,447,452,442,456,460,453,470,455,463,448,459,449,450,446,457,461,458,464,465,466,462,474,471,476,475,478,472,467,468,508,477,479,483,482,491,493,473,492,480,487,481,469,497,494,498,495,507,499,520,496,509,510,511,512,505,513,514,484,488,489,490,485,500,486,515,518,516,517,519,521,522,525,501,504,506,523,524,502,503,526]
+
+
+def rank_program(g, core, T, topo):
+    rank = T.rank_of(core)
+    if rank is None:
+        return
+    dst = T.cores[(rank + 1) % len(T.cores)]
+    mask = topo.mask(core, dst); neng = len(topo.engines(core, dst))
+    ops = plan(T, g, topo.addr(dst, core), mask, neng)
+    deps = depend(ops)
+    seq = LOADS + [i for i in ORDER if i not in LOADS]
+    for k, i in enumerate(seq):
+        ops[i]["st"] = k
+    queue = {"V": g.vector, "A": g.scalar, "P": g.tensor, "G": g, "S": g.sync}
+    count = {e: 0 for e in "VAPG"}
+    know = {e: {} for e in "VAPGS"}
+    token = {}; clock = {}; nd = 0; nr = 0; total = {}
+    for i in seq:
+        o = ops[i]; e = o["e"]; kn = know[e]
+        need = {}
+        for j, how in deps[i].items():
+            p = ops[j]
+            if e == "P" and p["e"] == "P":
+                continue
+            sem, val = token[(j, how)]
+            if kn.get(sem, 0) < val and need.get(sem, (0, 0))[0] < val:
+                need[sem] = (val, j)
+        for sem, (val, j) in sorted(need.items(), key=lambda x: -ops[x[1][1]]["st"]):
+            if kn.get(sem, 0) >= val:
+                continue
+            queue[e].wait_ge(T.sem[sem], val)
+            kn[sem] = val
+            if not sem.startswith("r"):
+                for s2, v2 in clock[j].items():
+                    if kn.get(s2, 0) < v2:
+                        kn[s2] = v2
+        clock[i] = dict(kn)
+        if o["kind"] == "dma":
+            sem = "d%d" % nd; nd += 1
+            o["fn"]().then_inc(T.sem[sem], 16); token[(i, "done")] = (sem, 16); total[sem] = 16
+        elif o["kind"] == "rem":
+            rs, ls = "r%d" % nr, "l%d" % nr; nr += 1
+            o["fn"](T.sem[rs], T.sem[ls])
+            token[(i, "done")] = (rs, neng); token[(i, "left")] = (ls, neng); total[rs] = neng; total[ls] = neng
+        else:
+            count[e] += 1
+            o["fn"]().then_inc(T.sem["e" + e], 1); token[(i, "done")] = ("e" + e, count[e]); total["e" + e] = count[e]
+    for sem, val in total.items():
+        if know["G"].get(sem, 0) < val or True:
+            g.wait_ge(T.sem[sem], val)

@@ -9,13 +9,15 @@ REV = True
 SCRATCH = {
     "F": ("sbuf", [128, C], "bfloat16"),
     "fg0": ("sbuf", [128, K], "bfloat16"), "fg1": ("sbuf", [128, K], "bfloat16"),
-    "dg0": ("sbuf", [128, K], "bfloat16"), "dg1": ("sbuf", [128, K], "bfloat16"),
+    "dg0": ("sbuf", [128, K], "bfloat16"), "dg1": ("sbuf", [128, K], "bfloat16"), "dg2": ("sbuf", [128, K], "bfloat16"),
+    "lE0": ("sbuf", [128, K], "bfloat16"), "lE1": ("sbuf", [128, K], "bfloat16"),
+    "one": ("sbuf", [128, 32], "float16"),
     "wg": ("sbuf", [128, K], "bfloat16"), "ex": ("sbuf", [128, K], "bfloat16"), "top": ("sbuf", [128, K], "bfloat16"),
     "Bs0": ("sbuf", [128, K], "bfloat16"), "Bs1": ("sbuf", [128, K], "bfloat16"),
     "IB": ("sbuf", [128, 128], "bfloat16"), "IH": ("sbuf", [128, 128], "bfloat16"), "NB": ("sbuf", [128, 128], "bfloat16"),
     "NC": ("sbuf", [128, 128], "bfloat16"),
     "X": ("sbuf", [128, C], "int32"), "DT": ("sbuf", [128, 2 * C + 16], "bfloat16"),
-    "U": ("sbuf", [128, C + 16], "bfloat16"), "W": ("sbuf", [128, 2 * K + 16], "bfloat16"),
+    "U": ("sbuf", [128, C + 16], "bfloat16"), "W": ("sbuf", [128, 3 * K], "bfloat16"),
     "Bi": ("sbuf", [128, K], "bfloat16"), "mi": ("sbuf", [128, 32], "int32"),
     "Bf": ("sbuf", [128, K], "float32"),
     "SU0": ("sbuf", [128, 2 * K], "bfloat16"), "SU1": ("sbuf", [128, 2 * K], "bfloat16"),
@@ -23,7 +25,7 @@ SCRATCH = {
     "mk0": ("sbuf", [128, K], "bfloat16"), "mk1": ("sbuf", [128, K], "bfloat16"),
     "xs0": ("sbuf", [128, K], "float16"), "xs1": ("sbuf", [128, K], "float16"),
     "sm": ("sbuf", [128, 32 * 170], "float32"), "sb": ("sbuf", [128, 32 * 90], "bfloat16"),
-    "sh": ("sbuf", [128, 32 * 90], "float16"), "su": ("sbuf", [128, 32 * 40], "uint16"),
+    "sh": ("sbuf", [128, 32 * 130], "float16"), "su": ("sbuf", [128, 32 * 40], "uint16"),
     "si": ("sbuf", [128, 32 * 8], "int32"),
     "lB1": ("sbuf", [128, K], "bfloat16"), "lB2": ("sbuf", [128, K], "bfloat16"),
     "lS1": ("sbuf", [128, 32 * 6], "float32"), "lS2": ("sbuf", [128, 32 * 9], "float32"),
@@ -48,11 +50,17 @@ SCRATCH = {
     "PB": ("psum", [128, 512], "float32"), "PA": ("psum", [128, 512], "float32"),
     "PL": ("psum", [128, 512], "float32"), "PT": ("psum", [128, 512], "float32"),
 }
-O0A, BFA = False, True
+BFA = False
 MERGE = True
-BSV = False
+FCUT = CUT = XCUT = (0, 160, 352, 512)
+COPY = (4, 7)
+WCUT = 288
+XA, XX = 500, 1150
+TQ = ("PL", 320, 352)
+PEO = ()
+PEM = ()
 NHG = 1
-UMODE = ["none", "next", "sep", "next", "next", "sep", "next", "next", "sep"]
+UMODE = ["none", "next", "sep", "sep", "sep", "sep", "sep", "sep", "sep"]
 PSUM = ("z0", "z1", "BA", "BB", "PB", "PA", "PL", "PT")
 NDMA = 40
 SEMAPHORES = ["eV", "eA", "eP", "eG"] + ["d%d" % i for i in range(NDMA)] + ["r%d" % i for i in range(12)] + ["l%d" % i for i in range(12)]
@@ -142,12 +150,9 @@ def plan(T, g, dst_addr, mask, neng):
     dma("S", T.mi[:, :], T.m0[:, :], [], [whole("mi")], 16)
     dma("S", T.F[:, :], T.fm[:, :], [], [whole("F")], 384)
     dma("A", T.Bi[:, :], T.b0[:, :], [], [whole("Bi")], 128)
-    dma("S", T.xc[:, :], T.nx[0::16, :], [], [whole("xc")], 450)
-    for blk in range(3):
-        for gg in range(2):
-            a = 32 * blk + 16 * gg
-            dma("S", T.xa[:, a:a + 16], T.nx[16 * gg::32, 512 * blk:512 * blk + 512], [], [("xa", a, a + 16)], 500)
-    dma("S", T.X[:, :], T.nx[:, :], [], [whole("X")], 1000)
+    for gg in range(2):
+        dma("S", T.xa[:, 48 * gg:48 * gg + 48], T.nx[16 * gg::32, :], [], [("xa", 48 * gg, 48 * gg + 48)], XA)
+    dma("S", T.X[:, :], T.nx[:, :], [], [whole("X")], XX)
     for i, o in enumerate(ops):
         o["first"] = 100.0 - i
     iota(("pi", 0, 1), [[0, 1]], 0, 1)
@@ -156,8 +161,8 @@ def plan(T, g, dst_addr, mask, neng):
     ts(("pi", 4, 5), ("pi", 0, 1), 112, ALU.bitwise_and)
     cp(col(0), ("pi", 4, 5))
     tt(col(1), ("pi", 0, 1), ("pi", 4, 5), ALU.subtract)
-    ts(col(2), col(1), 1.0, ALU.min, 3.0, ALU.mult)
-    ts(col(3), col(2), -1.0, ALU.add)
+    ts(col(2), col(1), 1.0, ALU.min, 3.0 * 4096, ALU.mult)
+    ts(col(3), col(2), -4096.0, ALU.add)
     ts(col(4), col(1), 15.0, ALU.is_equal, 2048.0, ALU.mult)
     ts(whole("dd"), whole("xi"), ap(col(0)), ALU.subtract, cols=[col(0)])
     ts(whole("EB"), whole("dd"), 15.0, ALU.is_equal, ap(col(3)), ALU.mult, cols=[col(3)])
@@ -175,7 +180,7 @@ def plan(T, g, dst_addr, mask, neng):
     iota(whole("PLC"), [[1, 9], [0, 32]], 1, 0)
     iota(("ri", 0, 18), [[0, 9], [16, 2]], 0, 1)
     ts(("rep", 0, 18), ("ri", 0, 18), ap(col(0)), ALU.subtract, cols=[col(0)])
-    iota(whole("ki"), [[16, 32]], 16 + K, 1)
+    iota(whole("ki"), [[16, 32]], 0, 1)
     ts(whole("kk"), whole("ki"), ap(col(0)), ALU.subtract, cols=[col(0)])
     act(whole("IB"), whole("I32"))
     act(whole("IH"), whole("I32"), scale=0.5)
@@ -183,27 +188,34 @@ def plan(T, g, dst_addr, mask, neng):
     act(whole("NC"), whole("I32"), scale=-0.5)
     add("V", lambda: g.vector.memset(T.top[:, :], 255.0), [], [whole("top")], 256 * CY)
     add("V", lambda: g.vector.memset(T.DT[:, C:C + 1] if REV else T.DT[:, 0:1], 0.0), [], [("DT", C, C + 1) if REV else ("DT", 0, 1)], 64 * CY)
+    add("V", lambda: g.vector.memset(T.DT[:, 2 * C + 1:2 * C + 2], 0.0), [], [("DT", 2 * C + 1, 2 * C + 2)], 64 * CY)
     NF = ("DT", C + 1, 2 * C + 1)
     ts(NF, whole("F"), -1.0, ALU.mult)
-    ts(whole("xf"), whole("xa"), 1.0 if REV else 0.0, ALU.add)
+    ts(whole("xy"), whole("xa"), 1.0, ALU.add, 1.0 / 8192, ALU.mult)
+    for blk in range(3):
+        for gg in range(2):
+            act(("xf", 32 * blk + 16 * gg, 32 * blk + 16 * gg + 16), ("xy", 48 * gg + 16 * blk, 48 * gg + 16 * blk + 16), scale=8192.0)
     add("V", lambda: g.vector.transpose(T.xt[:, :], T.xf[:, :]), [whole("xf")], [whole("xt")], 96 * CY)
-    cp(whole("xu"), whole("xt"))
+    for blk in range(3):
+        add("V", lambda b=blk: g.vector.tensor_copy(T.xu[:, b:96:3], T.xt[:, 32 * b:32 * b + 32]), [whole("xt")], [("xu", 32 * blk, 32 * blk + 32)], 64 * CY)
     for i in range(3):
         hi = C - 1 - 512 * i
         gt(("DT", hi - 511, hi + 1), ("DT", C, 2 * C + 1), ("xu", 32 * i, 32 * i + 32), ("F", 512 * i, 512 * i + 512), ALU.add,
            oap=T.DT[:, hi:hi - 512:-1] if i < 2 else T.DT[:, hi::-1])
+        ops[-1]["rd"].append(whole("xu"))
     add("V", lambda: g.vector.memset(T.U[:, :], 0.0), [], [whole("U")], 776 * CY)
-    ts(whole("xy"), whole("xc"), 1.0, ALU.add, 0.5, ALU.mult)
     act(whole("xh"), whole("xy"))
     tt(whole("xl"), whole("xy"), whole("xh"), ALU.subtract)
-    dma("S", T.U[1::16, 1:C + 1], T.xh[:, :], [whole("xh"), ("U", 0, 1)], [("U", 1, 2)], 64)
-    dma("S", T.U[2::16, 1:C + 1], T.xl[:, :], [whole("xl"), ("U", 0, 1)], [("U", 2, 3)], 64)
-    add("V", lambda: g.vector.memset(T.W[:, 0:16], 0.0), [], [("W", 0, 16)], 64 * CY)
-    DTW = ("DT", 0, 2 * C + 1)
+    for gg in range(2):
+        dma("S", T.U[16 * gg + 1::32, 1:C + 1], T.xh[:, 48 * gg:48 * gg + 48], [whole("xh"), ("U", 0, 1)], [("U", 1 + gg, 2 + gg)], 300)
+        dma("S", T.U[16 * gg + 2::32, 1:C + 1], T.xl[:, 48 * gg:48 * gg + 48], [whole("xl"), ("U", 0, 1)], [("U", 3 + gg, 4 + gg)], 300)
+    add("V", lambda: g.vector.memset(T.W[:, K:2 * K], 0.0), [], [("W", K, 2 * K)], 256 * CY)
+    DTW = ("DT", 0, 2 * C + 2)
     UW = ("U", 0, C + 1)
 
     mu = new("su"); cp(mu, whole("mi"))
-    m = new("sm"); cp(m, whole("mi"))
+    m = new("sh"); ts(m, whole("mi"), 1.0, ALU.add)
+    add("V", lambda: g.vector.memset(T.one[:, :], 1.0), [], [whole("one")], 64 * CY)
     mm(whole("BA"), [(T.IB[:, :], T.Bi[:, :], K)], [whole("IB"), whole("Bi")])
     mm(whole("BB"), [(T.IH[:, :], T.Bi[:, :], K)], [whole("IH"), whole("Bi")])
     parts = []
@@ -211,18 +223,31 @@ def plan(T, g, dst_addr, mask, neng):
 
     def write(s, o0, q, place, uq, stop):
         bu = new("sm"); tt(bu, uq, o0, ALU.mult)
-        dv = new("sm"); tt(dv, q, bu, ALU.add)
-        M2 = new("sh", s); gt(M2, dv, ("rep", 0, 2 * s), place, ALU.mult)
+        M2 = new("sh", s)
+        if s in PEM:
+            dv = new("sh"); tt(dv, q, bu, ALU.add)
+            spread(dv, s)
+            tt(M2, ("PT", 32, 32 + 32 * s), place, ALU.mult)
+        else:
+            dv = new("sm"); tt(dv, q, bu, ALU.add)
+            gt(M2, dv, ("rep", 0, 2 * s), place, ALU.mult)
         parts.insert(0, M2)
         if s < NST - 2:
             logsum()
 
-    def logsum():
+    def spread(x, k):
+        def fn():
+            for i in range(k):
+                ins = g.tensor.matmul(T.PT[:, 32 + 32 * i:64 + 32 * i], T.I16[:, :], ap(x), True, True)
+            return ins
+        add("P", fn, [whole("I16"), x], [("PT", 32, 32 + 32 * k)], 64 * k * PCY)
+
+    def logsum(stop=True):
         now = list(parts)
 
         def fn():
             for i, x in enumerate(now):
-                ins = g.tensor.matmul(T.PL[:, 0:n_of(x)], T.I16[:, :], ap(x), i == 0, i == len(now) - 1)
+                ins = g.tensor.matmul(T.PL[:, 0:n_of(x)], T.I16[:, :], ap(x), i == 0, stop and i == len(now) - 1)
             return ins
         add("P", fn, [whole("I16")] + now, [("PL", 0, n_of(now[0]))], sum(max(64, n_of(x)) for x in now) * PCY)
 
@@ -231,35 +256,42 @@ def plan(T, g, dst_addr, mask, neng):
         vend = s % S_ == S_ - 1 and not last
         SU, lw, mk, xs = whole("SU%d" % (s % 2)), whole("lw%d" % (s % 2)), whole("mk%d" % (s % 2)), whole("xs%d" % (s % 2))
         h = K // NH; hl = h // 16
-        m1 = new("sm"); act(m1, m, bias=1.0)
+        m1 = m
+        if last:
+            m = new("sm"); ts(m, m1, -1.0, ALU.add)
         fg = whole("fg%d" % (s % 2))
-        for i in range(NH):
-            agather(sub(fg, i * h, i * h + h), whole("F"), sub(mu, i * hl, i * hl + hl))
-        for i in range(NH):
-            tt(sub(SU, i * h, i * h + h), sub(fg, i * h, i * h + h), ("BA", i * h, i * h + h), ALU.is_gt)
-            tt(sub(lw, i * h, i * h + h), sub(fg, i * h, i * h + h), ("BB", i * h, i * h + h), ALU.is_gt)
+        for i in range(len(FCUT) - 1):
+            a, b = FCUT[i], FCUT[i + 1]
+            agather(sub(fg, a, b), whole("F"), sub(mu, a // 16, b // 16))
+        for i in range(len(CUT) - 1):
+            a, b = CUT[i], CUT[i + 1]
+            tt(sub(SU, a, b), sub(fg, a, b), ("BA", a, b), ALU.is_gt)
+            tt(sub(lw, a, b), sub(fg, a, b), ("BB", a, b), ALU.is_gt)
+        shift = 0.0
         if s == 0:
-            Bs, shift, LA, LB = whole("Bi"), 0.0, "IB", "IH"
+            terms = [("IB", "IH", whole("Bi"))]
         elif s % S_ == 0:
-            Bs, shift, LA, LB = whole("ex"), 127.5, "NB", "NC"
-            act(Bs, whole("BA"), AF.Relu, bias=255.0, scale=-1.0)
-        else:
-            Bs, shift, LA, LB = whole("Bs%d" % (s % 2)), 128.0, "IB", "IH"
-            if BSV:
-                ts(Bs, whole("BA"), -128.0, ALU.add)
-            else:
-                act(Bs, whole("BA"), bias=-128.0)
-        if not vend:
-            mm(whole("BA"), [(T[LA][:, :], ap(Bs), K)] + ([(T.IB[:, :], T.top[:, :], K)] if LA == "NB" else []),
-               [whole(LA), whole("IB"), whole("top"), Bs], stop=False)
-        if not (last or vend):
-            mm(whole("BB"), [(T[LB][:, :], ap(Bs), K)] + ([(T.IH[:, :], T.top[:, :], K)] if LA == "NB" else []),
-               [whole(LB), whole("IH"), whole("top"), Bs], stop=False)
-        if LA == "NB":
-            shift = 0.0
+            act(whole("ex"), whole("BA"), AF.Relu, bias=255.0, scale=-1.0)
+            terms = [("NB", "NC", whole("ex")), ("IB", "IH", whole("top"))]
+        elif vend and s > S_:
+            Bs, shift = whole("Bs%d" % (s % 2)), 128.0
+            act(Bs, whole("BA"), bias=-128.0)
+        elif s in COPY:
+            shift = 128.0
+            act(whole("Bs%d" % (s % 2)), whole("BA"), bias=-128.0)
+            terms = [("IB", "IH", whole("Bs%d" % (s % 2)))]
+        for i, (a, b, x) in enumerate(terms):
+            if not vend:
+                mm(whole("BA"), [(T[a][:, :], ap(x), K)], [whole(a), x], start=(i == 0), stop=False)
+            if not (last or vend):
+                mm(whole("BB"), [(T[b][:, :], ap(x), K)], [whole(b), x], start=(i == 0), stop=False)
         if s == 0:
-            dma("S", T.W[:, 16:16 + 2 * K], T.wl[:, :], [sub(lw, 0, 1)], [("W", 16, 16 + 2 * K)], 256)
-        if vend:
+            dma("S", T.W[:, 0:K], T.wl[:, K:2 * K], [whole("X")], [("W", 0, K)], 256)
+            dma("S", T.W[:, 2 * K:3 * K], T.wl[:, 0:K], [whole("X")], [("W", 2 * K, 3 * K)], 256)
+        if s == 0:
+            remote(whole("lB1"), whole("Bi"))
+            ops[-1]["rd"].append(whole("X"))
+        if vend and s > S_:
             remote(whole("lB%d" % (s // S_ + 1)), Bs)
         nb = 64 if UMODE[s] == "now" or pend is not None else 32
         if UMODE[s] == "now":
@@ -267,103 +299,116 @@ def plan(T, g, dst_addr, mask, neng):
         if UMODE[s] == "next":
             agather(("SU%d" % ((s + 1) % 2), K, 2 * K), UW, th)
         mm(("PB", 0, nb), [(T.EB[:, 15 - j:143 - j], T[SU[0]][:, j:16 * nb:16], 64) for j in range(16)],
-           [whole("EB"), sub(SU, 0, 16 * nb)])
-        for i in range(NH):
-            z = ("z%d" % i, 0, h)
-            mm(z, [(T.T1[:, :], ap(sub(SU, i * h, i * h + h)), max(64, h))], [whole("T1"), sub(SU, i * h, i * h + h)], stop=False)
-            mm(z, [(T.T2[:, :], ap(sub(lw, i * h, i * h + h)), max(64, h))], [whole("T2"), sub(lw, i * h, i * h + h)], start=False)
-            act(sub(mk, i * h, i * h + h), z, AF.Relu, bias=ap(col(4)), scale=2048.0, cols=[col(4)])
-            gt(sub(xs, i * h, i * h + h), whole("X"), sub(mu, i * hl, i * hl + hl), sub(mk, i * h, i * h + h), ALU.min)
+           [whole("EB"), sub(SU, 0, 16 * nb)], stop=False)
+        mm(("PB", 0, 32), [(T.I16[:, :], ap(m1), 64)], [whole("I16"), m1], start=False)
+        for i in range(len(CUT) - 1):
+            a, b = CUT[i], CUT[i + 1]
+            z = (("z0", "z1", "PT")[i % 3], 0, b - a)
+            mm(z, [(T.T1[:, :], ap(sub(SU, a, b)), max(64, b - a)), (T.T2[:, :], ap(sub(lw, a, b)), max(64, b - a))],
+               [whole("T1"), whole("T2"), sub(SU, a, b), sub(lw, a, b)])
+            act(sub(mk, a, b), z, AF.Relu, bias=ap(col(4)), scale=2048.0, cols=[col(4)])
+        for i in range(len(XCUT) - 1):
+            a, b = XCUT[i], XCUT[i + 1]
+            gt(sub(xs, a, b), whole("X"), sub(mu, a // 16, b // 16), sub(mk, a, b), ALU.min)
         Cq, Uq = ("PB", 0, 32), ("PB", 32, 64)
         if vend:
             msg = new("sm", 4 + s)
             t1n, c1n, n1n, am = sub(msg, 0, 32), sub(msg, 32, 64), sub(msg, 64, 96), sub(msg, 96, 128)
         else:
-            t1n, c1n, n1n, am = new("sm"), new("sm"), new("sm"), new("sm" if last or s == 0 else "sh")
-        ok = new("sm"); ts(ok, Cq, 0.0, ALU.is_equal)
-        tt(am, ok, m1, ALU.mult)
+            t1n, c1n, n1n, am = new("sm"), new("sh" if s in PEO else "sm"), new("sm"), new("sm" if last or s == 0 else "sh")
         idx = new("su")
-        items = [(T.EA[:, 15 - j:143 - j], T[xs[0]][:, j:K:16], 64) for j in range(16)]
-        mn = new("sm"); mun = new("su")
         if s == 0:
-            cp(idx, am)
+            ts(idx, Cq, C + 1.0, ALU.min)
+        else:
+            r = new("sm"); tt(r, Cq, t1, ALU.max)
+            ts(idx, r, float(C), ALU.add, 2 * C + 1.0, ALU.min)
+        ok = new("sm"); tt(ok, Cq, m1, ALU.is_equal)
+        tt(am, ok, m1, ALU.mult)
+        items = [(T.EA[:, 15 - j:143 - j], T[xs[0]][:, j:K:16], 64) for j in range(16)]
+        mn = new("sm" if last else "sh"); mun = new("su")
+        if s == 0:
             c1n = ok
             ts(n1n, ok, 1.0, ALU.add)
-            t1n = am
+            act(t1n, am, scale=-1.0)
             OC = ok
-            thn = idx
+            thn = new("su"); cp(thn, am)
             mm(("PA", 0, 32), items, [whole("EA"), xs])
             cp(mun, ("PA", 0, 32))
-            act(mn, ("PA", 0, 32))
+            ts(mn, ("PA", 0, 32), 1.0, ALU.add)
         else:
-            o0 = new("sm")
-            if O0A:
-                act(o0, Cq, AF.Relu, scale=-1.0)
-            else:
-                ts(o0, Cq, -1.0, ALU.is_equal)
+            o0 = new("sm"); ts(o0, Cq, 0.0, ALU.is_lt)
             if not last:
-                rs = new("sm"); ts(rs, Cq, 1.0, ALU.is_ge)
+                rs = new("sm"); ts(rs, r, 2048.0, ALU.is_ge)
             if pend is not None:
                 write(pend[0], pend[1], pend[2], pend[3], Uq, False)
                 pend = None
-            bt = new("sm"); tt(bt, o0, t1, ALU.mult)
-            r = new("sm"); tt(r, am, bt, ALU.subtract)
-            ts(idx, r, float(C), ALU.add)
+            bt = new("sm"); ts(bt, r, 0.0, ALU.min)
             bf = new("sb")
             if BFA:
-                act(bf, bt, AF.Sign)
+                act(bf, bt, AF.Sign, scale=-1.0)
             else:
-                ts(bf, bt, 1.0, ALU.min)
+                ts(bf, r, 0.0, ALU.is_lt)
             w = new("sm"); tt(w, bf, m, ALU.mult)
-            mm(("PA", 0, 32), [(T.NI[:, :], ap(bf), 64)] + items, [whole("EA"), whole("NI"), xs, bf])
+            mm(("PA", 0, 32), [(T.NI[:, :], ap(bf), 64)] + ([] if last else [(T.I16[:, :], T.one[:, :], 64)]),
+               [whole("NI"), whole("I16"), whole("one"), bf], stop=False)
+            mm(("PA", 0, 32), items, [whole("EA"), xs], start=False)
             tt(mn, ("PA", 0, 32), w, ALU.max)
             if not (last or vend):
-                cp(mun, mn)
+                ts(mun, mn, -1.0, ALU.add)
             an = new("sm"); tt(an, ok, n1, ALU.mult)
             y = new("sm"); tt(y, c1, o0, ALU.subtract)
             tt(c1n, y, an, ALU.max)
             if not last:
                 tt(n1n, n1, ok, ALU.add)
-            q = new("sm"); tt(q, amp, bt, ALU.subtract)
+            q = new("sm"); tt(q, amp, bt, ALU.add)
             nw = s - 1 if vend else s + 1
-            OC = new("sb", nw); gt(OC, n1 if last else c1n, ("rep", 0, 2 * nw), ("PLC", 0, 32 * nw), ALU.is_equal)
+            OC = new("sb", nw)
+            if s in PEO:
+                spread(c1n, nw)
+                tt(OC, ("PT", 32, 32 + 32 * nw), ("PLC", 0, 32 * nw), ALU.is_equal)
+            else:
+                gt(OC, n1 if last else c1n, ("rep", 0, 2 * nw), ("PLC", 0, 32 * nw), ALU.is_equal)
             if not last:
                 ra = new("sh"); tt(ra, rs, amp, ALU.mult)
                 if s == 1:
-                    tt(t1n, ra, am, ALU.add)
-                    thn = new("su"); cp(thn, t1n)
+                    tp = new("sm"); tt(tp, ra, am, ALU.add)
+                    thn = new("su"); cp(thn, tp)
+                    act(t1n, tp, scale=-1.0)
                 else:
                     M4 = new("sh", s - 1); tt(M4, ("PL", 0, 32 * s - 32), sub(OC, 0, 32 * s - 32), ALU.mult)
-                    mm(("PT", 0, 32), [(T.I32[:, :], ap(am), 256) if vend else (T.I16[:, :], ap(am), 64), (T.I16[:, :], ap(ra), 64)]
+                    mm(TQ, [(T.I32[:, :], ap(am), 256) if vend else (T.I16[:, :], ap(am), 64), (T.I16[:, :], ap(ra), 64)]
                        + [(T.I16[:, :], ap(sub(M4, 32 * i, 32 * i + 32)), 64) for i in range(s - 1)],
                        [whole("I32"), whole("I16"), am, ra, M4])
                     if vend:
                         imsg = new("su", 3)
-                        ti = new("si"); ts(ti, ("PT", 0, 32), 2048.0, ALU.mult)
-                        cp(sub(imsg, 32, 64), ("PT", 0, 32))
+                        ti = new("si"); ts(ti, TQ, 1024.0, ALU.mult, 512.0, ALU.max)
+                        cp(sub(imsg, 32, 64), TQ)
                     else:
-                        thn = new("su"); cp(thn, ("PT", 0, 32))
-                    act(t1n, ("PT", 0, 32))
+                        thn = new("su"); cp(thn, TQ)
+                    act(t1n, TQ, scale=-1.0)
             if UMODE[s] == "next":
                 pend = (s, o0, q, OCp)
             else:
                 if UMODE[s] == "sep":
                     ug = whole("ug")
                     agather(ug, UW, th)
-                    Uq = ("PB", 64, 96)
+                    Uq = ("PL", 352, 384) if last else ("PB", 64, 96)
                     mm(Uq, [(T.EB[:, 15 - j:143 - j], T.ug[:, j:K:16], 64) for j in range(16)], [whole("EB"), ug])
                 write(s, o0, q, OCp, Uq, vend)
             if vend:
                 act(sub(msg, 128, 128 + 32 * s), ("PL", 0, 32 * s))
-        dg = whole("dg%d" % (s % 2))
+        dg = whole("dg%d" % (s % 3))
+        terms.append(("IB", "IH", dg))
         hg = K // NHG
         for i in range(NHG):
             part = sub(dg, i * hg, i * hg + hg)
-            agather(part, DTW if s else ("DT", C, 2 * C + 1), sub(idx, i * hg // 16, (i + 1) * hg // 16), bias=shift)
+            agather(part, DTW if s else ("DT", C, 2 * C + 2), sub(idx, i * hg // 16, (i + 1) * hg // 16), bias=shift)
             if not vend:
                 mm(("BA", i * hg, i * hg + hg), [(T.IB[:, :], ap(part), hg)], [whole("IB"), part], start=False, stop=(i == NHG - 1))
             if not (last or vend):
                 mm(("BB", i * hg, i * hg + hg), [(T.IH[:, :], ap(part), hg)], [whole("IH"), part], start=False, stop=(i == NHG - 1))
+        if s < S_ - 1:
+            remote(whole("lE%d" % s), dg)
         if last:
             hd = K // NHD
             for i in range(NHD):
@@ -371,28 +416,30 @@ def plan(T, g, dst_addr, mask, neng):
                 act(part, ("BA", i * hd, i * hd + hd))
                 dma("S", T.yb[:, i * hd:i * hd + hd], ap(part), [part], [], 256 // NHD)
             M5 = new("sh", 9); gt(M5, am, ("rep", 0, 18), OC, ALU.mult)
+            newest = parts.pop(0)
             parts.insert(0, M5)
-            logsum()
+            logsum(stop=False)
+            mm(("PL", 0, n_of(newest)), [(T.I16[:, :], ap(newest), n_of(newest))], [whole("I16"), newest], start=False)
             act(whole("yo"), ("PL", 0, 288), bias=-1.0)
             yc = new("sm"); act(yc, c1n, bias=-1.0)
             dma("S", T.yc[:, :], ap(yc), [yc], [], 16)
-            dma("S", T.yl[:, :], T.yo[:, :], [whole("yo")], [], 144)
+            dma("A", T.yl[:, :], T.yo[:, :], [whole("yo")], [], 144)
             dma("S", T.ym[:, :], ap(mn), [mn], [], 16)
             break
         if vend:
             v = s // S_ + 1
             lB, lD, lS, lI, lm = (whole(x + str(v)) for x in ("lB", "lD", "lS", "lI", "lm"))
-            pa = new("si"); ts(pa, ti, 2, ALU.arith_shift_right, 512, ALU.bitwise_and)
-            x2 = new("sm"); tt(x2, whole("kk"), pa, ALU.subtract)
-            x3 = new("sm"); tt(x3, x2, ti, ALU.min)
+            pa = new("si"); ts(pa, ti, 3 * K, ALU.bitwise_and)
+            x4 = new("sm"); tt(x4, whole("kk"), pa, ALU.add)
             if wprev is not None:
-                ne = new("sm"); tt(ne, x3, wprev, ALU.not_equal)
-                x4 = new("sm"); tt(x4, x3, ne, ALU.mult)
+                eq = new("sm"); tt(eq, pa, wprev[0], ALU.is_equal)
+                e = new("sm"); tt(e, eq, wprev[1], ALU.mult)
+                x2, x4 = x4, new("sm"); tt(x4, x2, e, ALU.add)
             else:
-                x4 = x3
-            wprev = x3
+                gap = new("sm"); ts(gap, pa, -1.0, ALU.mult, float(K), ALU.add)
+                wprev = (pa, gap)
             cp(sub(imsg, 0, 32), x4)
-            cp(sub(imsg, 64, 96), mn)
+            ts(sub(imsg, 64, 96), mn, -1.0, ALU.add)
             remote(lD, dg)
             if MERGE:
                 remote(lI, imsg)
@@ -403,13 +450,16 @@ def plan(T, g, dst_addr, mask, neng):
             remote(lS, msg)
             t1n, c1n, n1n, am = sub(lS, 0, 32), sub(lS, 32, 64), sub(lS, 64, 96), sub(lS, 96, 128)
             thn = sub(lI, 32, 64)
-            mn = new("sm"); cp(mn, mun)
+            mn = new("sh"); ts(mn, mun, 1.0, ALU.add)
             wg = whole("wg")
-            add("V", lambda a=sub(lI, 0, 32): g.vector.tensor_copy(T.wg[:, :], T.W[:, :].indirect(ap(a))),
-                [whole("W"), sub(lI, 0, 32)], [wg], 0.05 + 1.5 * n_of(wg) * CY)
-            for i, x in enumerate((lB, lD, wg)):
-                mm(whole("BA"), [(T.IB[:, :], ap(x), K)], [whole("IB"), x], start=(i == 0), stop=(i == 2))
-                mm(whole("BB"), [(T.IH[:, :], ap(x), K)], [whole("IH"), x], start=(i == 0), stop=(i == 2))
+            o = sub(wg, 0, WCUT)
+            add("V", lambda a=sub(lI, 0, WCUT // 16): g.vector.tensor_copy(T.wg[:, 0:WCUT], T.W[:, :].indirect(ap(a))),
+                [whole("W"), sub(lI, 0, 32)], [o], 0.05 + 1.5 * n_of(o) * CY)
+            agather(sub(wg, WCUT, K), whole("W"), sub(lI, WCUT // 16, 32))
+            come = [lB] + ([whole("lE0"), whole("lE1")] if v == 1 else []) + [lD, wg]
+            for i, x in enumerate(come):
+                mm(whole("BA"), [(T.IB[:, :], ap(x), K)], [whole("IB"), x], start=(i == 0), stop=(x == wg))
+                mm(whole("BB"), [(T.IH[:, :], ap(x), K)], [whole("IH"), x], start=(i == 0), stop=(x == wg))
             OC = new("sb", s + 1); gt(OC, c1n, ("rep", 0, 2 * s + 2), ("PLC", 0, 32 * s + 32), ALU.is_equal)
             Ll = sub(lS, 128, 128 + 32 * s)
             Lh = new("sh", s); cp(Lh, Ll)
@@ -470,10 +520,10 @@ def order(ops, deps, bump=None):
 
 
 SLACK = 0.08
-LOADS = [0, 1, 2, 10, 4, 5, 6, 7, 8, 9, 3]
+LOADS = [0, 1, 2, 3, 4, 5]
 
 
-ORDER = [13,12,11,42,57,51,14,15,25,43,20,16,26,36,23,24,27,2,10,1,3,4,0,5,6,7,8,9,38,60,39,19,34,37,59,35,17,22,58,31,29,30,18,28,21,44,63,65,61,66,71,73,74,64,67,72,45,52,68,53,32,62,46,47,54,56,55,77,78,81,82,83,75,76,69,70,79,80,41,40,88,48,85,86,50,89,92,94,90,95,103,104,93,96,87,101,84,97,49,102,113,111,105,106,115,91,112,98,107,108,109,110,116,117,114,129,118,119,123,130,100,120,99,126,121,122,124,132,133,136,125,131,138,137,180,135,140,127,142,134,139,33,128,141,145,144,155,153,156,157,149,150,151,146,147,161,164,169,154,168,158,162,170,159,163,187,173,152,174,160,175,176,148,177,178,179,165,188,189,190,172,166,167,191,192,171,181,182,183,184,185,186,143,198,193,194,197,209,199,200,201,196,202,208,210,203,211,219,220,212,223,218,213,224,195,205,204,217,221,214,207,222,206,215,229,227,231,228,242,232,225,226,234,233,250,235,239,240,241,236,237,238,243,230,245,254,244,246,216,251,256,252,257,255,258,253,247,265,248,259,266,267,268,264,275,269,270,273,249,281,290,277,274,260,261,262,271,272,282,283,278,284,286,279,293,289,285,276,287,291,288,263,295,280,294,296,292,300,304,301,306,302,307,305,308,297,298,309,303,313,314,315,316,312,325,321,323,324,299,310,348,311,326,322,336,337,327,317,318,319,329,332,338,330,341,331,355,363,342,328,343,344,320,345,333,346,356,347,357,340,358,359,360,334,335,361,362,364,349,350,351,352,339,353,354,368,369,371,367,370,372,378,373,380,389,379,382,388,387,366,377,384,381,390,391,383,397,399,398,393,394,395,365,401,402,404,409,403,420,392,386,385,396,406,421,405,400,410,412,411,415,414,407,408,423,375,413,374,376,416,424,426,422,427,425,428,417,418,429,435,436,437,438,419,430,434,445,439,440,441,443,451,454,433,431,432,444,447,452,442,456,460,453,470,455,463,448,459,449,450,446,457,461,458,464,465,466,462,474,471,476,475,478,472,467,468,508,477,479,483,482,491,493,473,492,480,487,481,469,497,494,498,495,507,499,520,496,509,510,511,512,505,513,514,484,488,489,490,485,500,486,515,518,516,517,519,521,522,525,501,504,506,523,524,502,503,526]
+ORDER = [31,8,55,0,2,1,3,4,5,6,21,29,20,9,10,36,33,34,66,7,81,28,32,26,22,24,35,11,15,37,12,17,18,14,63,19,65,13,39,62,69,70,23,38,25,40,41,64,73,16,75,68,71,43,42,47,56,46,44,67,72,60,79,80,57,58,59,30,74,45,27,48,76,82,83,84,85,86,87,88,89,50,49,51,93,94,102,53,105,95,97,91,90,92,96,98,52,78,104,99,100,107,54,77,103,111,112,106,109,110,108,113,114,101,124,125,129,122,123,128,126,127,130,61,119,120,121,131,138,115,116,132,133,134,154,135,136,145,139,150,151,140,141,137,142,143,147,152,148,144,146,149,117,118,158,155,161,156,162,169,160,165,166,173,159,163,167,168,164,153,170,175,174,177,178,184,171,172,180,182,189,185,179,213,194,186,195,176,225,191,187,227,196,183,197,181,199,200,192,201,202,188,190,193,203,198,214,204,215,218,217,206,207,208,216,209,205,210,211,212,226,228,157,230,229,219,232,220,223,224,222,231,233,239,243,238,241,234,244,256,240,245,252,247,242,254,246,258,221,235,236,237,257,261,255,253,263,260,270,249,251,248,250,259,262,264,268,265,267,282,276,271,277,269,272,278,273,274,280,275,281,287,288,289,290,266,283,293,297,294,301,295,284,302,312,296,299,300,310,298,303,308,285,313,291,304,314,286,311,305,317,279,316,309,319,323,321,326,315,318,320,333,324,332,327,343,349,292,307,306,328,329,344,334,337,325,330,331,354,338,335,322,350,351,352,336,345,339,346,340,347,353,359,360,369,370,356,355,341,342,365,366,357,361,363,364,362,358,367,368,373,371,378,374,376,387,375,405,413,386,381,388,379,391,377,392,348,393,372,383,380,390,394,395,396,406,408,407,382,409,389,384,385,410,412,411,414,398,399,400,401,402,397,403,404,415,419,420,418,421,422,417,423,416,430,435,424,428,431,436,448,432,444,429,433,449,434,445,437,452,450,442,446,447,477,443,455,453,426,460,454,483,451,457,459,469,461,458,438,439,440,462,466,467,470,425,463,464,468,456,465,471,472,441,427,473,485,486,490,484,489,478,488,494,493,474,479,487,491,504,505,480,492,475,481,500,508,498,499,501,506,476,509,513,511,516,495,522,502,503,507,533,523,514,510,538,524,528,517,527,496,482,518,519,525,520,512,521,544,542,515,529,543,579,526,534,539,549,530,531,580,532,535,545,536,497,540,547,553,554,548,550,557,546,555,558,556,537,564,568,566,569,565,585,567,578,570,562,581,582,561,583,591,584,551,572,552,559,560,563,586,587,589,590,588,592,593,594,597,576,575,541,577,595,596,573,571,574,598]
 
 
 def rank_program(g, core, T, topo):

@@ -2,76 +2,87 @@ from concourse.mybir import AluOpType as ALU, ActivationFunctionType as AF
 
 C, K, V_, S_ = 1536, 512, 3, 3
 NST = V_ * S_
-NH = 2
-NHD = 2
-REV = True
+O = 16
+Z = O + C
+R0 = Z + O
+DW = R0 + C
 
 SCRATCH = {
     "F": ("sbuf", [128, C], "bfloat16"),
     "fg0": ("sbuf", [128, K], "bfloat16"), "fg1": ("sbuf", [128, K], "bfloat16"),
     "dg0": ("sbuf", [128, K], "bfloat16"), "dg1": ("sbuf", [128, K], "bfloat16"), "dg2": ("sbuf", [128, K], "bfloat16"),
-    "lE0": ("sbuf", [128, K], "bfloat16"), "lE1": ("sbuf", [128, K], "bfloat16"),
-    "one": ("sbuf", [128, 32], "float16"),
-    "wg": ("sbuf", [128, K], "bfloat16"), "ex": ("sbuf", [128, K], "bfloat16"), "top": ("sbuf", [128, K], "bfloat16"),
+    "lE2": ("sbuf", [128, K], "bfloat16"), "lE0": ("sbuf", [128, K], "bfloat16"), "lE1": ("sbuf", [128, K], "bfloat16"),
+    "wg": ("sbuf", [128, K], "bfloat16"), "ex": ("sbuf", [128, K], "bfloat16"), "dh": ("sbuf", [128, K], "float16"),
+    "H16": ("sbuf", [128, 128], "float16"),
     "Bs0": ("sbuf", [128, K], "bfloat16"), "Bs1": ("sbuf", [128, K], "bfloat16"),
     "IB": ("sbuf", [128, 128], "bfloat16"), "IH": ("sbuf", [128, 128], "bfloat16"), "NB": ("sbuf", [128, 128], "bfloat16"),
     "NC": ("sbuf", [128, 128], "bfloat16"),
-    "X": ("sbuf", [128, C], "int32"), "DT": ("sbuf", [128, 2 * C + 16], "bfloat16"),
-    "U": ("sbuf", [128, C + 16], "bfloat16"), "W": ("sbuf", [128, 3 * K], "bfloat16"),
+    "X": ("sbuf", [128, Z], "int32"), "DT": ("sbuf", [128, DW], "bfloat16"),
+    "U": ("sbuf", [128, DW], "bfloat16"), "W": ("sbuf", [128, 3 * K], "bfloat16"),
     "Bi": ("sbuf", [128, K], "bfloat16"), "mi": ("sbuf", [128, 32], "int32"),
     "Bf": ("sbuf", [128, K], "float32"),
-    "SU0": ("sbuf", [128, 2 * K], "bfloat16"), "SU1": ("sbuf", [128, 2 * K], "bfloat16"),
+    "st0": ("sbuf", [128, K], "bfloat16"), "st1": ("sbuf", [128, K], "bfloat16"),
     "lw0": ("sbuf", [128, K], "bfloat16"), "lw1": ("sbuf", [128, K], "bfloat16"),
     "mk0": ("sbuf", [128, K], "bfloat16"), "mk1": ("sbuf", [128, K], "bfloat16"),
     "xs0": ("sbuf", [128, K], "float16"), "xs1": ("sbuf", [128, K], "float16"),
-    "sm": ("sbuf", [128, 32 * 170], "float32"), "sb": ("sbuf", [128, 32 * 90], "bfloat16"),
-    "sh": ("sbuf", [128, 32 * 130], "float16"), "su": ("sbuf", [128, 32 * 40], "uint16"),
+    "ug0": ("sbuf", [128, 2 * K], "bfloat16"), "ug1": ("sbuf", [128, 2 * K], "bfloat16"),
+    "sm": ("sbuf", [128, 32 * 90], "float32"), "sb": ("sbuf", [128, 32 * 90], "bfloat16"),
+    "sh": ("sbuf", [128, 32 * 200], "float16"), "su": ("sbuf", [128, 32 * 40], "uint16"),
     "si": ("sbuf", [128, 32 * 8], "int32"),
     "lB1": ("sbuf", [128, K], "bfloat16"), "lB2": ("sbuf", [128, K], "bfloat16"),
-    "lS1": ("sbuf", [128, 32 * 6], "float32"), "lS2": ("sbuf", [128, 32 * 9], "float32"),
-    "lm1": ("sbuf", [128, 32], "uint16"), "lm2": ("sbuf", [128, 32], "uint16"),
-    "lI1": ("sbuf", [128, 96], "uint16"), "lI2": ("sbuf", [128, 96], "uint16"),
-    "lD1": ("sbuf", [128, K], "bfloat16"), "lD2": ("sbuf", [128, K], "bfloat16"), "ug": ("sbuf", [128, K], "bfloat16"),
+    "lD1": ("sbuf", [128, K], "bfloat16"), "lD2": ("sbuf", [128, K], "bfloat16"),
+    "lW1": ("sbuf", [128, 32], "uint16"), "lW2": ("sbuf", [128, 32], "uint16"),
+    "lI1": ("sbuf", [128, 192], "uint16"), "lI2": ("sbuf", [128, 192], "uint16"),
+    "lL1": ("sbuf", [128, 32 * 2], "float16"), "lL2": ("sbuf", [128, 32 * 5], "float16"),
     "xa": ("sbuf", [128, 96], "int32"), "xf": ("sbuf", [128, 96], "float32"), "xt": ("sbuf", [128, 96], "float32"),
-    "xu": ("sbuf", [128, 96], "uint16"), "xc": ("sbuf", [128, 96], "int32"), "xy": ("sbuf", [128, 96], "float32"),
+    "xu": ("sbuf", [128, 96], "uint16"), "xp": ("sbuf", [128, 96], "float32"), "xy": ("sbuf", [128, 96], "float32"),
+    "xd": ("sbuf", [128, 96], "float32"), "tj": ("sbuf", [128, 96], "float32"), "tm": ("sbuf", [128, 96], "float32"),
     "xh": ("sbuf", [128, 96], "bfloat16"), "xl": ("sbuf", [128, 96], "bfloat16"),
-    "pi": ("sbuf", [128, 8], "int32"), "pc": ("sbuf", [128, 16], "float32"),
+    "pi": ("sbuf", [128, 16], "int32"), "pc": ("sbuf", [128, 16], "float32"),
     "xi": ("sbuf", [128, 144], "float32"), "dd": ("sbuf", [128, 144], "float32"), "rel": ("sbuf", [128, 128], "float32"),
     "EA": ("sbuf", [128, 144], "float16"), "EB": ("sbuf", [128, 144], "bfloat16"),
+    "E8": ("sbuf", [128, 144], "float16"), "EA8": ("sbuf", [128, 144], "float16"), "EB8": ("sbuf", [128, 144], "bfloat16"),
+    "par": ("sbuf", [128, 64], "float32"), "pw": ("sbuf", [128, 64], "float16"), "farA": ("sbuf", [128, 64], "float16"),
+    "farL": ("sbuf", [128, 64], "float16"), "farB": ("sbuf", [128, 64], "bfloat16"),
     "cl": ("sbuf", [128, 128], "float32"), "SG": ("sbuf", [128, 128], "float32"), "I32": ("sbuf", [128, 128], "float32"),
     "g0": ("sbuf", [128, 128], "float32"), "T2b": ("sbuf", [128, 128], "float32"), "T1b": ("sbuf", [128, 128], "float32"),
     "T1": ("sbuf", [128, 128], "bfloat16"), "T2": ("sbuf", [128, 128], "bfloat16"),
-    "I16": ("sbuf", [128, 128], "float16"), "NI": ("sbuf", [128, 128], "bfloat16"),
+    "I16": ("sbuf", [128, 128], "float16"), "N16": ("sbuf", [128, 128], "float16"), "K16": ("sbuf", [128, 128], "float16"),
+    "W16": ("sbuf", [128, 128], "float16"),
+    "cz": ("sbuf", [128, 32], "float16"), "co": ("sbuf", [128, 32], "float16"), "anz": ("sbuf", [128, 64], "float32"),
     "PLC": ("sbuf", [128, 288], "float32"), "ri": ("sbuf", [128, 32], "float32"), "rep": ("sbuf", [128, 32], "uint16"),
-    "rf": ("sbuf", [128, 32], "float32"), "ki": ("sbuf", [128, 32], "float32"), "kk": ("sbuf", [128, 32], "float32"),
+    "ki": ("sbuf", [128, 32], "float32"), "kk": ("sbuf", [128, 32], "float16"), "kz": ("sbuf", [128, 32], "float32"),
     "yo": ("sbuf", [128, 288], "float32"),
     "z0": ("psum", [128, 512], "float32"), "z1": ("psum", [128, 512], "float32"),
-    "BA": ("psum", [128, 512], "float32"), "BB": ("psum", [128, 512], "float32"),
-    "PB": ("psum", [128, 512], "float32"), "PA": ("psum", [128, 512], "float32"),
+    "B0": ("psum", [128, 512], "float32"), "B1": ("psum", [128, 512], "float32"),
+    "B2": ("psum", [128, 512], "float32"), "PB": ("psum", [128, 512], "float32"),
     "PL": ("psum", [128, 512], "float32"), "PT": ("psum", [128, 512], "float32"),
 }
-BFA = False
-MERGE = True
-FCUT = CUT = XCUT = (0, 160, 352, 512)
-COPY = (4, 7)
-WCUT = 288
-XA, XX = 500, 1150
-TQ = ("PL", 320, 352)
-PEO = ()
-PEM = ()
-NHG = 1
-UMODE = ["none", "next", "sep", "sep", "sep", "sep", "sep", "sep", "sep"]
-PSUM = ("z0", "z1", "BA", "BB", "PB", "PA", "PL", "PT")
-NDMA = 40
-SEMAPHORES = ["eV", "eA", "eP", "eG"] + ["d%d" % i for i in range(NDMA)] + ["r%d" % i for i in range(12)] + ["l%d" % i for i in range(12)]
+PSUM = ("z0", "z1", "B0", "B1", "B2", "PB", "PL", "PT")
+NDMA, NREM = 32, 14
+SEMAPHORES = ["eV", "eA", "eP", "eG"] + ["d%d" % i for i in range(NDMA)] + ["r%d" % i for i in range(NREM)] + ["l%d" % i for i in range(NREM)]
 
-CY, PCY = 0.83e-3, 0.6e-3
-HOP, SAME = 0.12, 0.07
+OPT = {
+    "fcut": (0, 128, 256, 512), "feng": "AAA",
+    "cut": (0, 256, 512),
+    "xcut": (0, 256, 512),
+    "dcut": (0, 256, 512), "deng": "AAA", "leng": "AAA", "vcut": (0, 320, 512), "veng": "AV",
+    "wcut": (0, 256, 512), "weng": "VVV",
+    "yeng": "AAA", "vclamp": (), "gate": "F", "wown": False, "peo": (8, 9), "pem": (), "sp": ("B2", 32), "uearly": True,
+    "xsplit": True, "cq": ("B2", 0, 32), "sendB": 4, "pD": "ab", "pI": "ab", "half": 1.5, "bcut": (0, 256, 512), "uq": ("z1", 416, 512),
+    "zat": (("z0", 0), ("z1", 0), ("z0", 256), ("z1", 208)), "a16": "", "feng0": "VVV", "rfirst": 4.0,
+    "copy": (1, 4, 7),
+    "split": (4,),
+    "ugroups": ((1, 2), (3,), (4, 5), (6,), (7,), (8,)), "ueng": "AAAAAAAAV",
+    "cy": 0.83e-3, "pcy": 0.4e-3, "hop": 0.14, "same": 0.2, "gat": 1.5, "afix": 0.08,
+    "dfix": 1.0, "drate": 280.0, "rfix": 1.0, "rrate": 100.0, "rissue": 1.2, "sweeps": 4000, "noise": 1.2, "width": 2.0, "allow": 0.05,
+}
 
 
-def plan(T, g, dst_addr, mask, neng):
+def plan(T, g, dst_addr, engines):
     ops = []
     used = {"sm": 0, "sb": 0, "sh": 0, "su": 0, "si": 0}
+    CY, PCY, GAT = OPT["cy"], OPT["pcy"], OPT["gat"]
 
     def new(buf, blocks=1):
         a = used[buf]; used[buf] += 32 * blocks
@@ -86,8 +97,11 @@ def plan(T, g, dst_addr, mask, neng):
     def sub(r, a, b):
         return (r[0], r[1] + a, r[1] + b)
 
-    def add(eng, fn, rd, wr, cost, kind="c", lat=0.0):
-        ops.append({"e": eng, "fn": fn, "rd": rd, "wr": wr, "cost": cost, "kind": kind, "lat": lat})
+    def blk(r, a, n=1):
+        return sub(r, 32 * a, 32 * (a + n))
+
+    def add(eng, fn, rd, wr, cost, kind="c", kb=0.0):
+        ops.append({"e": eng, "fn": fn, "rd": rd, "wr": wr, "cost": cost, "kind": kind, "kb": kb})
 
     def two(r):
         return SCRATCH[r[0]][2] in ("bfloat16", "float16", "uint16")
@@ -107,36 +121,71 @@ def plan(T, g, dst_addr, mask, neng):
         add("V", lambda: g.vector.tensor_tensor(ap(o), ap(a), ap(b), op), [a, b], [o], c)
 
     def cp(o, i):
-        add("V", lambda: g.vector.tensor_copy(ap(o), ap(i)), [i], [o], max(64, n_of(o)) * CY)
+        add("V", lambda: g.vector.tensor_copy(ap(o), ap(i)), [i], [o], max(64, n_of(o) * (0.5 if two(o) and two(i) else 1)) * CY)
 
-    def gt(o, win, off, b, op, oap=None):
-        oa = ap(o) if oap is None else oap
-        add("V", lambda: g.vector.tensor_tensor(oa, ap(win).indirect(ap(off)), ap(b), op), [win, off, b], [o],
-            0.05 + 1.5 * n_of(o) * CY)
+    def fill(o, v):
+        add("V", lambda: g.vector.memset(ap(o), v), [], [o], max(64, n_of(o) * (0.5 if two(o) else 1)) * CY)
+
+    def gt(o, win, off, b, op):
+        add("V", lambda: g.vector.tensor_tensor(ap(o), ap(win).indirect(ap(off)), ap(b), op), [win, off, b], [o],
+            0.05 + GAT * n_of(o) * CY)
 
     def act(o, i, func=AF.Identity, bias=0.0, scale=1.0, cols=()):
         add("A", lambda: g.scalar.activation(ap(o), ap(i), func, bias=bias, scale=scale), [i] + list(cols), [o],
-            max(64, n_of(o)) * CY + 0.03)
+            max(64, n_of(o)) * CY + OPT["afix"])
 
-    def agather(o, win, off, bias=0.0):
-        add("A", lambda: g.scalar.activation(ap(o), ap(win).indirect(ap(off)), AF.Identity, bias=bias), [win, off], [o],
-            0.065 + 1.5 * n_of(o) * CY)
+    def gather(eng, o, win, off, bias=0.0, scale=1.0):
+        if eng == "A":
+            add("A", lambda: g.scalar.activation(ap(o), ap(win).indirect(ap(off)), AF.Identity, bias=bias, scale=scale),
+                [win, off], [o], 0.065 + GAT * n_of(o) * CY)
+        else:
+            add("V", lambda: g.vector.tensor_scalar(ap(o), ap(win).indirect(ap(off)), scale, bias, ALU.mult, ALU.add),
+                [win, off], [o], 0.05 + GAT * n_of(o) * CY)
 
-    def mm(o, items, rd, start=True, stop=True):
+    def pieces(cut, eng):
+        return [(cut[i], cut[i + 1], eng[i]) for i in range(len(cut) - 1)]
+
+    def mm(items, start=True, stop=True):
         def fn():
-            for i, (l, r, _) in enumerate(items):
-                ins = g.tensor.matmul(ap(o), l, r, start and i == 0, stop and i == len(items) - 1)
+            for i, (o, l, r) in enumerate(items):
+                ins = g.tensor.matmul(ap(o), T[l][:, :], ap(r), start and i == 0, stop and i == len(items) - 1)
             return ins
-        add("P", fn, rd, [o], sum(x[2] for x in items) * PCY, kind="c" if start else "acc")
+        add("P", fn, [whole(l) for _, l, _ in items] + [r for _, _, r in items], [o for o, _, _ in items],
+            sum(max(64, n_of(r)) for _, _, r in items) * PCY)
+
+    def to_list(o, E, x, more=(), stop=True):
+        def fn():
+            for j in range(16):
+                ins = g.tensor.matmul(ap(o), T[E][:, 15 - j:143 - j], T[x[0]][:, x[1] + j:x[2]:16], j == 0, stop and j == 15 and not more)
+            for i, (p, l, r) in enumerate(more):
+                ins = g.tensor.matmul(ap(p), T[l][:, :], ap(r), False, i == len(more) - 1)
+            return ins
+        add("P", fn, [whole(E), x] + [whole(l) for _, l, _ in more] + [r for _, _, r in more], [o], 64 * (16 + len(more)) * PCY)
+
+    def least(o, at, E, x, far, M, y, cap):
+        def fn():
+            for j in range(8):
+                g.tensor.matmul(ap(at), T[E][:, 15 - j:143 - j], T[x[0]][:, x[1] + j:x[2]:8], j == 0, False)
+            g.tensor.matmul(ap(at), T[far[0]][:, :], T[far[1]][:, :], False, False)
+            for h in range(2):
+                ins = g.tensor.matmul(T[at[0]][:, at[1] + h:at[2]:2], T[M][:, :], ap(y), False, h == 1)
+            return ins
+        add("P", fn, [whole(E), x, whole(far[0]), whole(far[1]), whole(M), y], [at], 64 * 11 * PCY)
+        half = new("sm")
+        add("V", lambda: g.vector.tensor_tensor(ap(half), T[at[0]][:, at[1]:at[2]:2], ap(cap), ALU.min), [at, cap], [half], 64 * CY)
+        add("V", lambda: g.vector.tensor_tensor(ap(o), T[at[0]][:, at[1] + 1:at[2]:2], ap(half), ALU.min), [at, half], [o], 64 * CY)
 
     def dma(q, o, i, rd, wr, kb):
         eng = g.sync if q == "S" else (g.scalar if q == "A" else g)
-        add(q, lambda: eng.dma_start(o, i), rd, wr, 0.06, kind="dma", lat=1.8 + kb / 250.0)
+        add(q, lambda: eng.dma_start(o, i), rd, wr, 0.06, kind="dma", kb=kb)
 
-    def remote(land, src):
-        kb = n_of(src) * (2 if two(src) else 4) / 8.0
-        add("G", lambda rs, ls: g.remote_dma(ap(land), ap(src), rs, ls, dst_addr[1], dst_addr[0], mask), [src], [land], 0.5,
-            kind="rem", lat=2.0 + kb / 100.0)
+    def remote(land, src, part="ab"):
+        half = len(engines) // 2
+        use = (engines[:half] if "a" in part else []) + (engines[half:] if "b" in part else [])
+        mask = sum(1 << e for e in use)
+        add("G", lambda rs, ls: g.remote_dma(ap(land), ap(src), rs, ls, dst_addr[1], dst_addr[0], mask), [src], [land],
+            OPT["rissue"], kind="rem", kb=(n_of(src) * (2 if two(src) else 4) / 8.0 + 20) * (1.0 if part == "ab" else OPT["half"]))
+        ops[-1]["part"], ops[-1]["n"] = part, len(use)
 
     def iota(o, pattern, base, cm):
         if SCRATCH[o[0]][2] == "int32":
@@ -147,22 +196,21 @@ def plan(T, g, dst_addr, mask, neng):
     def col(j):
         return ("pc", j, j + 1)
 
-    dma("S", T.mi[:, :], T.m0[:, :], [], [whole("mi")], 16)
-    dma("S", T.F[:, :], T.fm[:, :], [], [whole("F")], 384)
+    FW, XW, DTW = ("DT", 0, Z), whole("X"), whole("DT")
+    dma("S", T.mi[:, :], T.m0[:, :], [], [whole("mi")], 30)
+    dma("S", T.DT[:, O:Z], T.fm[:, :], [], [("DT", O, Z)], 384)
     dma("A", T.Bi[:, :], T.b0[:, :], [], [whole("Bi")], 128)
     for gg in range(2):
-        dma("S", T.xa[:, 48 * gg:48 * gg + 48], T.nx[16 * gg::32, :], [], [("xa", 48 * gg, 48 * gg + 48)], XA)
-    dma("S", T.X[:, :], T.nx[:, :], [], [whole("X")], XX)
-    for i, o in enumerate(ops):
-        o["first"] = 100.0 - i
+        dma("S", T.xa[:, 48 * gg:48 * gg + 48], T.nx[16 * gg::32, :], [], [("xa", 48 * gg, 48 * gg + 48)], 50)
+    dma("S", T.X[:, O:Z], T.nx[:, :], [], [("X", O, Z)], 768)
     iota(("pi", 0, 1), [[0, 1]], 0, 1)
     iota(whole("xi"), [[1, 144]], 0, 0)
     iota(whole("rel"), [[1, 128]], 0, -1)
     ts(("pi", 4, 5), ("pi", 0, 1), 112, ALU.bitwise_and)
     cp(col(0), ("pi", 4, 5))
     tt(col(1), ("pi", 0, 1), ("pi", 4, 5), ALU.subtract)
-    ts(col(2), col(1), 1.0, ALU.min, 3.0 * 4096, ALU.mult)
-    ts(col(3), col(2), -4096.0, ALU.add)
+    ts(col(2), col(1), 1.0, ALU.min, -3.0 * 4096, ALU.mult)
+    ts(col(3), col(2), 4096.0, ALU.add)
     ts(col(4), col(1), 15.0, ALU.is_equal, 2048.0, ALU.mult)
     ts(whole("dd"), whole("xi"), ap(col(0)), ALU.subtract, cols=[col(0)])
     ts(whole("EB"), whole("dd"), 15.0, ALU.is_equal, ap(col(3)), ALU.mult, cols=[col(3)])
@@ -176,354 +224,394 @@ def plan(T, g, dst_addr, mask, neng):
     act(whole("T1b"), whole("T2b"), bias=-4.0, scale=512.0)
     tt(whole("T1"), whole("T1b"), whole("SG"), ALU.mult)
     cp(whole("I16"), whole("I32"))
-    act(whole("NI"), whole("I32"), scale=-4096.0)
+    for name, v in (("N16", -1.0), ("K16", -4096.0), ("W16", 1024.0), ("H16", 0.5)):
+        ts(whole(name), whole("I16"), v, ALU.mult)
+    for name, v in (("IB", 1.0), ("IH", 0.5), ("NB", -1.0), ("NC", -0.5)):
+        act(whole(name), whole("I32"), scale=v)
     iota(whole("PLC"), [[1, 9], [0, 32]], 1, 0)
     iota(("ri", 0, 18), [[0, 9], [16, 2]], 0, 1)
     ts(("rep", 0, 18), ("ri", 0, 18), ap(col(0)), ALU.subtract, cols=[col(0)])
     iota(whole("ki"), [[16, 32]], 0, 1)
     ts(whole("kk"), whole("ki"), ap(col(0)), ALU.subtract, cols=[col(0)])
-    act(whole("IB"), whole("I32"))
-    act(whole("IH"), whole("I32"), scale=0.5)
-    act(whole("NB"), whole("I32"), scale=-1.0)
-    act(whole("NC"), whole("I32"), scale=-0.5)
-    add("V", lambda: g.vector.memset(T.top[:, :], 255.0), [], [whole("top")], 256 * CY)
-    add("V", lambda: g.vector.memset(T.DT[:, C:C + 1] if REV else T.DT[:, 0:1], 0.0), [], [("DT", C, C + 1) if REV else ("DT", 0, 1)], 64 * CY)
-    add("V", lambda: g.vector.memset(T.DT[:, 2 * C + 1:2 * C + 2], 0.0), [], [("DT", 2 * C + 1, 2 * C + 2)], 64 * CY)
-    NF = ("DT", C + 1, 2 * C + 1)
-    ts(NF, whole("F"), -1.0, ALU.mult)
-    ts(whole("xy"), whole("xa"), 1.0, ALU.add, 1.0 / 8192, ALU.mult)
-    for blk in range(3):
+    ts(whole("kz"), whole("kk"), float(K), ALU.add)
+    fill(whole("cz"), float(Z)); fill(whole("co"), float(O)); fill(("anz", 32, 64), 0.0)
+    fill(("DT", 0, O), 0.0); fill(("DT", Z, R0), 0.0); fill(("X", 0, O), 0)
+    fill(("W", K, 2 * K), 0.0); ops[-1]["early"] = True
+    iota(whole("tj"), [[0, 2], [1, 48]], 0, 0)
+    remote(whole("lB1"), whole("Bi"))
+    first = len(ops) - 1
+    ops[first]["rd"].append(FW if OPT["gate"] == "F" else XW); ops[first]["cost"] = OPT["rfirst"]
+    ops[first]["after"] = [i for i in range(first) if ops[i]["e"] == "G"]
+    for a in range(0, DW, K):
+        b = min(a + K, DW)
+        dma("S", T.U[:, a:b], T.W[:, K:K + b - a], [XW, ("W", K, 2 * K)], [("U", a, b)], (b - a) / 4 + 10)
+    ts(("pi", 8, 9), ("pi", 0, 1), 31, ALU.bitwise_and)
+    ts(col(5), ("pi", 8, 9), 48.0, ALU.mult)
+    ts(whole("tm"), whole("tj"), ap(col(5)), ALU.add, cols=[col(5)])
+    ts(whole("xp"), whole("xa"), float(O), ALU.add)
+    for b in range(3):
         for gg in range(2):
-            act(("xf", 32 * blk + 16 * gg, 32 * blk + 16 * gg + 16), ("xy", 48 * gg + 16 * blk, 48 * gg + 16 * blk + 16), scale=8192.0)
+            act(("xf", 32 * b + 16 * gg, 32 * b + 16 * gg + 16), ("xp", 48 * gg + 16 * b, 48 * gg + 16 * b + 16))
     add("V", lambda: g.vector.transpose(T.xt[:, :], T.xf[:, :]), [whole("xf")], [whole("xt")], 96 * CY)
-    for blk in range(3):
-        add("V", lambda b=blk: g.vector.tensor_copy(T.xu[:, b:96:3], T.xt[:, 32 * b:32 * b + 32]), [whole("xt")], [("xu", 32 * blk, 32 * blk + 32)], 64 * CY)
+    for b in range(3):
+        add("V", lambda b=b: g.vector.tensor_copy(T.xu[:, b:96:3], T.xt[:, 32 * b:32 * b + 32]), [whole("xt")], [blk(whole("xu"), b)], 64 * CY)
     for i in range(3):
-        hi = C - 1 - 512 * i
-        gt(("DT", hi - 511, hi + 1), ("DT", C, 2 * C + 1), ("xu", 32 * i, 32 * i + 32), ("F", 512 * i, 512 * i + 512), ALU.add,
-           oap=T.DT[:, hi:hi - 512:-1] if i < 2 else T.DT[:, hi::-1])
+        (cp if OPT["feng0"][i] == "V" else act)(("F", K * i, K * i + K), ("DT", O + K * i, O + K * i + K))
+        gt(("DT", R0 + K * i, R0 + K * i + K), FW, blk(whole("xu"), i), ("F", K * i, K * i + K), ALU.subtract)
         ops[-1]["rd"].append(whole("xu"))
-    add("V", lambda: g.vector.memset(T.U[:, :], 0.0), [], [whole("U")], 776 * CY)
+    tt(whole("xd"), whole("tm"), whole("xa"), ALU.subtract)
+    act(whole("xy"), whole("xd"), scale=1.0 / 8192)
     act(whole("xh"), whole("xy"))
     tt(whole("xl"), whole("xy"), whole("xh"), ALU.subtract)
+    for o in ops[-4:]:
+        o["early"] = OPT["uearly"]
     for gg in range(2):
-        dma("S", T.U[16 * gg + 1::32, 1:C + 1], T.xh[:, 48 * gg:48 * gg + 48], [whole("xh"), ("U", 0, 1)], [("U", 1 + gg, 2 + gg)], 300)
-        dma("S", T.U[16 * gg + 2::32, 1:C + 1], T.xl[:, 48 * gg:48 * gg + 48], [whole("xl"), ("U", 0, 1)], [("U", 3 + gg, 4 + gg)], 300)
-    add("V", lambda: g.vector.memset(T.W[:, K:2 * K], 0.0), [], [("W", K, 2 * K)], 256 * CY)
-    DTW = ("DT", 0, 2 * C + 2)
-    UW = ("U", 0, C + 1)
+        dma("S", T.U[16 * gg + 1::32, R0:DW], T.xh[:, 48 * gg:48 * gg + 48], [whole("xh"), ("U", R0 + 4, DW)], [("U", R0 + gg, R0 + gg + 1)], 40)
+        dma("S", T.U[16 * gg + 2::32, R0:DW], T.xl[:, 48 * gg:48 * gg + 48], [whole("xl"), ("U", R0 + 4, DW)], [("U", R0 + 2 + gg, R0 + 3 + gg)], 40)
+    dma("S", T.W[:, 0:K], T.wl[:, 0:K], [XW], [("W", 0, K)], 128)
+    dma("S", T.W[:, 2 * K:3 * K], T.wl[:, K:2 * K], [XW], [("W", 2 * K, 3 * K)], 128)
 
-    mu = new("su"); cp(mu, whole("mi"))
-    m = new("sh"); ts(m, whole("mi"), 1.0, ALU.add)
-    add("V", lambda: g.vector.memset(T.one[:, :], 1.0), [], [whole("one")], 64 * CY)
-    mm(whole("BA"), [(T.IB[:, :], T.Bi[:, :], K)], [whole("IB"), whole("Bi")])
-    mm(whole("BB"), [(T.IH[:, :], T.Bi[:, :], K)], [whole("IH"), whole("Bi")])
-    parts = []
-    t1 = c1 = n1 = amp = OCp = th = wprev = pend = None
+    mu = new("su"); ts(mu, whole("mi"), float(O), ALU.add)
+    m = new("sh"); ts(m, whole("mi"), float(O), ALU.add)
+    CUT = [(i, OPT["bcut"][i], OPT["bcut"][i + 1]) for i in range(len(OPT["bcut"]) - 1)]
+    FINE = [(max(i for i, c, _ in CUT if c <= a), a, b) for a, b, _ in pieces(OPT["cut"], "VVVVVV")]
 
-    def write(s, o0, q, place, uq, stop):
-        bu = new("sm"); tt(bu, uq, o0, ALU.mult)
-        M2 = new("sh", s)
-        if s in PEM:
-            dv = new("sh"); tt(dv, q, bu, ALU.add)
-            spread(dv, s)
-            tt(M2, ("PT", 32, 32 + 32 * s), place, ALU.mult)
+    def BA(i, a, b):
+        return ("B%d" % i, a - CUT[i][1], b - CUT[i][1])
+
+    def BB(i, a, b):
+        return ("B%d" % i, 256 + a - CUT[i][1], 256 + b - CUT[i][1])
+
+    def stocks(terms, start, stop, half=True, only=None):
+        for p in CUT:
+            if only is None or p[0] == only:
+                mm([(BA(*p), x, sub(y, p[1], p[2])) for x, _, y in terms]
+                   + [(BB(*p), x, sub(y, p[1], p[2])) for _, x, y in terms if half], start, stop)
+
+    terms = [("IB", "IH", whole("Bi"))]
+    stocks(terms, True, True)
+    parts, idxs, ams, OCs = [], {}, {}, {}
+    tl = cn = clip = None
+    tz = whole("cz")
+    TQ, TN, TW, CN, UQ = ("PT", 0, 128), ("PT", 128, 160), ("PT", 160, 192), ("PT", 192, 256), OPT["uq"]
+
+    def logsum(width, start=True, stop=True, now=None):
+        now = sorted(parts if now is None else now, key=lambda x: -n_of(x))
+        mm([(("PL", 0, min(n_of(x), 32 * width)), "I16", sub(x, 0, min(n_of(x), 32 * width))) for x in now], start, stop)
+
+    def repeat(o, x, y, op, pe):
+        k = n_of(o) // 32
+        if pe:
+            at = (OPT["sp"][0], OPT["sp"][1], OPT["sp"][1] + 32 * k)
+            mm([(blk(at, i), "IB" if x[0] == "sb" else "I16", x) for i in range(k)])
+            tt(o, at, y, op)
         else:
-            dv = new("sm"); tt(dv, q, bu, ALU.add)
-            gt(M2, dv, ("rep", 0, 2 * s), place, ALU.mult)
-        parts.insert(0, M2)
-        if s < NST - 2:
-            logsum()
+            gt(o, x, ("rep", 0, 2 * k), y, op)
 
-    def spread(x, k):
-        def fn():
-            for i in range(k):
-                ins = g.tensor.matmul(T.PT[:, 32 + 32 * i:64 + 32 * i], T.I16[:, :], ap(x), True, True)
-            return ins
-        add("P", fn, [whole("I16"), x], [("PT", 32, 32 + 32 * k)], 64 * k * PCY)
+    def place(s, value):
+        M = new("sh", s); repeat(M, value, OCs[s], ALU.mult, value[0] == "sh")
+        parts.append(M)
 
-    def logsum(stop=True):
-        now = list(parts)
-
-        def fn():
-            for i, x in enumerate(now):
-                ins = g.tensor.matmul(T.PL[:, 0:n_of(x)], T.I16[:, :], ap(x), i == 0, stop and i == len(now) - 1)
-            return ins
-        add("P", fn, [whole("I16")] + now, [("PL", 0, n_of(now[0]))], sum(max(64, n_of(x)) for x in now) * PCY)
+    def partners(n, group):
+        ug = ("ug%d" % (n % 2), 0, K * len(group))
+        for i, s in enumerate(group):
+            gather(OPT["ueng"][s], sub(ug, K * i, K * i + K), whole("U"), idxs[s])
+        uq = blk(UQ, 0, len(group))
+        to_list(uq, "EB", ug, [(blk(uq, i), "I16", ams[s - 1]) for i, s in enumerate(group) if s > 1 and s not in OPT["split"]])
+        for i, s in enumerate(group):
+            if s == 1:
+                dv = new("sh"); cp(dv, blk(uq, i)); parts.append(dv)
+            else:
+                dv = new("sh" if s in OPT["pem"] else "sm"); act(dv, blk(uq, i)); place(s, dv)
 
     for s in range(NST):
         last = s == NST - 1
         vend = s % S_ == S_ - 1 and not last
-        SU, lw, mk, xs = whole("SU%d" % (s % 2)), whole("lw%d" % (s % 2)), whole("mk%d" % (s % 2)), whole("xs%d" % (s % 2))
-        h = K // NH; hl = h // 16
-        m1 = m
-        if last:
-            m = new("sm"); ts(m, m1, -1.0, ALU.add)
-        fg = whole("fg%d" % (s % 2))
-        for i in range(len(FCUT) - 1):
-            a, b = FCUT[i], FCUT[i + 1]
-            agather(sub(fg, a, b), whole("F"), sub(mu, a // 16, b // 16))
-        for i in range(len(CUT) - 1):
-            a, b = CUT[i], CUT[i + 1]
-            tt(sub(SU, a, b), sub(fg, a, b), ("BA", a, b), ALU.is_gt)
-            tt(sub(lw, a, b), sub(fg, a, b), ("BB", a, b), ALU.is_gt)
-        shift = 0.0
-        if s == 0:
-            terms = [("IB", "IH", whole("Bi"))]
-        elif s % S_ == 0:
-            act(whole("ex"), whole("BA"), AF.Relu, bias=255.0, scale=-1.0)
-            terms = [("NB", "NC", whole("ex")), ("IB", "IH", whole("top"))]
-        elif vend and s > S_:
-            Bs, shift = whole("Bs%d" % (s % 2)), 128.0
-            act(Bs, whole("BA"), bias=-128.0)
-        elif s in COPY:
-            shift = 128.0
-            act(whole("Bs%d" % (s % 2)), whole("BA"), bias=-128.0)
-            terms = [("IB", "IH", whole("Bs%d" % (s % 2)))]
-        for i, (a, b, x) in enumerate(terms):
-            if not vend:
-                mm(whole("BA"), [(T[a][:, :], ap(x), K)], [whole(a), x], start=(i == 0), stop=False)
-            if not (last or vend):
-                mm(whole("BB"), [(T[b][:, :], ap(x), K)], [whole(b), x], start=(i == 0), stop=False)
-        if s == 0:
-            dma("S", T.W[:, 0:K], T.wl[:, K:2 * K], [whole("X")], [("W", 0, K)], 256)
-            dma("S", T.W[:, 2 * K:3 * K], T.wl[:, 0:K], [whole("X")], [("W", 2 * K, 3 * K)], 256)
-        if s == 0:
-            remote(whole("lB1"), whole("Bi"))
-            ops[-1]["rd"].append(whole("X"))
-        if vend and s > S_:
-            remote(whole("lB%d" % (s // S_ + 1)), Bs)
-        nb = 64 if UMODE[s] == "now" or pend is not None else 32
-        if UMODE[s] == "now":
-            agather(sub(SU, K, 2 * K), UW, th)
-        if UMODE[s] == "next":
-            agather(("SU%d" % ((s + 1) % 2), K, 2 * K), UW, th)
-        mm(("PB", 0, nb), [(T.EB[:, 15 - j:143 - j], T[SU[0]][:, j:16 * nb:16], 64) for j in range(16)],
-           [whole("EB"), sub(SU, 0, 16 * nb)], stop=False)
-        mm(("PB", 0, 32), [(T.I16[:, :], ap(m1), 64)], [whole("I16"), m1], start=False)
-        for i in range(len(CUT) - 1):
-            a, b = CUT[i], CUT[i + 1]
-            z = (("z0", "z1", "PT")[i % 3], 0, b - a)
-            mm(z, [(T.T1[:, :], ap(sub(SU, a, b)), max(64, b - a)), (T.T2[:, :], ap(sub(lw, a, b)), max(64, b - a))],
-               [whole("T1"), whole("T2"), sub(SU, a, b), sub(lw, a, b)])
-            act(sub(mk, a, b), z, AF.Relu, bias=ap(col(4)), scale=2048.0, cols=[col(4)])
-        for i in range(len(XCUT) - 1):
-            a, b = XCUT[i], XCUT[i + 1]
-            gt(sub(xs, a, b), whole("X"), sub(mu, a // 16, b // 16), sub(mk, a, b), ALU.min)
-        Cq, Uq = ("PB", 0, 32), ("PB", 32, 64)
-        if vend:
-            msg = new("sm", 4 + s)
-            t1n, c1n, n1n, am = sub(msg, 0, 32), sub(msg, 32, 64), sub(msg, 64, 96), sub(msg, 96, 128)
-        else:
-            t1n, c1n, n1n, am = new("sm"), new("sh" if s in PEO else "sm"), new("sm"), new("sm" if last or s == 0 else "sh")
-        idx = new("su")
-        if s == 0:
-            ts(idx, Cq, C + 1.0, ALU.min)
-        else:
-            r = new("sm"); tt(r, Cq, t1, ALU.max)
-            ts(idx, r, float(C), ALU.add, 2 * C + 1.0, ALU.min)
-        ok = new("sm"); tt(ok, Cq, m1, ALU.is_equal)
-        tt(am, ok, m1, ALU.mult)
-        items = [(T.EA[:, 15 - j:143 - j], T[xs[0]][:, j:K:16], 64) for j in range(16)]
-        mn = new("sm" if last else "sh"); mun = new("su")
-        if s == 0:
-            c1n = ok
-            ts(n1n, ok, 1.0, ALU.add)
-            act(t1n, am, scale=-1.0)
-            OC = ok
-            thn = new("su"); cp(thn, am)
-            mm(("PA", 0, 32), items, [whole("EA"), xs])
-            cp(mun, ("PA", 0, 32))
-            ts(mn, ("PA", 0, 32), 1.0, ALU.add)
-        else:
-            o0 = new("sm"); ts(o0, Cq, 0.0, ALU.is_lt)
-            if not last:
-                rs = new("sm"); ts(rs, r, 2048.0, ALU.is_ge)
-            if pend is not None:
-                write(pend[0], pend[1], pend[2], pend[3], Uq, False)
-                pend = None
-            bt = new("sm"); ts(bt, r, 0.0, ALU.min)
-            bf = new("sb")
-            if BFA:
-                act(bf, bt, AF.Sign, scale=-1.0)
-            else:
-                ts(bf, r, 0.0, ALU.is_lt)
-            w = new("sm"); tt(w, bf, m, ALU.mult)
-            mm(("PA", 0, 32), [(T.NI[:, :], ap(bf), 64)] + ([] if last else [(T.I16[:, :], T.one[:, :], 64)]),
-               [whole("NI"), whole("I16"), whole("one"), bf], stop=False)
-            mm(("PA", 0, 32), items, [whole("EA"), xs], start=False)
-            tt(mn, ("PA", 0, 32), w, ALU.max)
-            if not (last or vend):
-                ts(mun, mn, -1.0, ALU.add)
-            an = new("sm"); tt(an, ok, n1, ALU.mult)
-            y = new("sm"); tt(y, c1, o0, ALU.subtract)
-            tt(c1n, y, an, ALU.max)
-            if not last:
-                tt(n1n, n1, ok, ALU.add)
-            q = new("sm"); tt(q, amp, bt, ALU.add)
-            nw = s - 1 if vend else s + 1
-            OC = new("sb", nw)
-            if s in PEO:
-                spread(c1n, nw)
-                tt(OC, ("PT", 32, 32 + 32 * nw), ("PLC", 0, 32 * nw), ALU.is_equal)
-            else:
-                gt(OC, n1 if last else c1n, ("rep", 0, 2 * nw), ("PLC", 0, 32 * nw), ALU.is_equal)
-            if not last:
-                ra = new("sh"); tt(ra, rs, amp, ALU.mult)
-                if s == 1:
-                    tp = new("sm"); tt(tp, ra, am, ALU.add)
-                    thn = new("su"); cp(thn, tp)
-                    act(t1n, tp, scale=-1.0)
+        st, lw, mk, xs, fg = (whole(x + str(s % 2)) for x in ("st", "lw", "mk", "xs", "fg"))
+        if s >= 2:
+            OCs[s] = new("sb", s); repeat(OCs[s], blk(cn, 0), ("PLC", 0, 32 * s), ALU.is_equal, s in OPT["peo"])
+            if s in OPT["split"]:
+                place(s, ams[s - 1])
+        if s >= 1:
+            below = []
+            if 2 <= s < NST - 1:
+                M4 = new("sh", s - 1)
+                if s == 2:
+                    tt(M4, ams[0], blk(OCs[s], 1), ALU.mult)
                 else:
-                    M4 = new("sh", s - 1); tt(M4, ("PL", 0, 32 * s - 32), sub(OC, 0, 32 * s - 32), ALU.mult)
-                    mm(TQ, [(T.I32[:, :], ap(am), 256) if vend else (T.I16[:, :], ap(am), 64), (T.I16[:, :], ap(ra), 64)]
-                       + [(T.I16[:, :], ap(sub(M4, 32 * i, 32 * i + 32)), 64) for i in range(s - 1)],
-                       [whole("I32"), whole("I16"), am, ra, M4])
-                    if vend:
-                        imsg = new("su", 3)
-                        ti = new("si"); ts(ti, TQ, 1024.0, ALU.mult, 512.0, ALU.max)
-                        cp(sub(imsg, 32, 64), TQ)
-                    else:
-                        thn = new("su"); cp(thn, TQ)
-                    act(t1n, TQ, scale=-1.0)
-            if UMODE[s] == "next":
-                pend = (s, o0, q, OCp)
+                    tt(M4, ("PL", 0, 32 * s - 32), blk(OCs[s], 1, s - 1), ALU.mult)
+                below = [(blk(TQ, 0), "I16", blk(M4, i)) for i in range(s - 1)]
+            if not last:
+                mm([(blk(TQ, 0), "N16", tl)] + below)
+                mm([(blk(TQ, 1), "I16", m), (blk(TQ, 1), "N16", tl)])
+                if not vend:
+                    mm([(blk(TQ, 2), "I16", m), (blk(TQ, 3), "I16", m)])
             else:
-                if UMODE[s] == "sep":
-                    ug = whole("ug")
-                    agather(ug, UW, th)
-                    Uq = ("PL", 352, 384) if last else ("PB", 64, 96)
-                    mm(Uq, [(T.EB[:, 15 - j:143 - j], T.ug[:, j:K:16], 64) for j in range(16)], [whole("EB"), ug])
-                write(s, o0, q, OCp, Uq, vend)
+                mm([(blk(TQ, 2), "I16", m), (blk(TQ, 2), "N16", whole("co")), (blk(TQ, 3), "I16", m)])
+                ON = new("sb", 9); repeat(ON, blk(cn, 1), whole("PLC"), ALU.is_equal, 9 in OPT["peo"])
+        for a, b, e in pieces(OPT["fcut"], OPT["feng"]):
+            gather(e, sub(fg, a, b), FW, sub(mu, a // 16, b // 16))
+        for i, a, b in FINE:
+            tt(sub(st, a, b), sub(fg, a, b), BA(i, a, b), ALU.is_gt)
+            tt(sub(lw, a, b), sub(fg, a, b), BB(i, a, b), ALU.is_gt)
+        shift = 0.0
+        if s in OPT["vclamp"]:
+            for i, a, b in CUT:
+                ts(("ex", a, b), BA(i, a, b), 255.0, ALU.min)
+            terms = [("IB", "IH", whole("ex"))]
+        elif s % S_ == 0 and s:
+            for i, a, b in CUT:
+                act(("ex", a, b), BA(i, a, b), AF.Relu, bias=255.0, scale=-1.0)
+            terms, shift = [("NB", "NC", whole("ex"))], 255.0
+        elif s == OPT["sendB"] or s in OPT["copy"]:
+            Bs, shift = whole("Bs%d" % (s % 2)), 128.0 if s > 1 else 0.0
+            for i, a, b in CUT:
+                act(sub(Bs, a, b), BA(i, a, b), bias=-shift)
+            terms = [("IB", "IH", Bs)]
+            if s == OPT["sendB"]:
+                remote(whole("lB2"), Bs)
+        if not vend:
+            stocks(terms, True, False, not last)
+        Cq = OPT["cq"]
+        idx = idxs[s] = new("su")
+        FL = new("sh", 2); bf, ok = blk(FL, 0), blk(FL, 1)
+        to_list(Cq, "EB", st, [(Cq, "I16", m)])
+        tt(idx, Cq, tz, ALU.min)
+        tt(ok, Cq, m, ALU.is_equal)
+        if s:
+            ts(bf, idx, float(Z), ALU.is_gt)
+        for i, (_, a, b) in enumerate(FINE):
+            z = (OPT["zat"][i][0], OPT["zat"][i][1], OPT["zat"][i][1] + b - a)
+            mm([(z, "T1", sub(st, a, b)), (z, "T2", sub(lw, a, b))])
+            act(sub(mk, a, b), z, AF.Relu, bias=ap(col(4)), scale=2048.0, cols=[col(4)])
+        for a, b, _ in pieces(OPT["xcut"], "VVVVVV"):
+            gt(sub(xs, a, b), XW, sub(mu, a // 16, b // 16), sub(mk, a, b), ALU.min)
+        PA = ("PB", 64, 96)
+        msg = new("su", 6) if vend else None
+        mn = new("sm" if last else "sh"); mun = blk(msg, 0) if vend else new("su")
+        if s == 0:
+            to_list(PA, "EA", xs)
+            ts(mun, PA, float(O), ALU.add)
+            ts(mn, PA, float(O), ALU.add)
+            tln = ams[0] = new("sh"); tt(tln, ok, m, ALU.mult)
+            tzn = new("sm"); ts(tzn, tln, float(Z), ALU.add)
+            parts.append(tln)
+            cnn = new("sb", 2); cp(blk(cnn, 0), ok); ts(blk(cnn, 1), ok, 1.0, ALU.add)
+        else:
             if vend:
-                act(sub(msg, 128, 128 + 32 * s), ("PL", 0, 32 * s))
-        dg = whole("dg%d" % (s % 3))
-        terms.append(("IB", "IH", dg))
-        hg = K // NHG
-        for i in range(NHG):
-            part = sub(dg, i * hg, i * hg + hg)
-            agather(part, DTW if s else ("DT", C, 2 * C + 2), sub(idx, i * hg // 16, (i + 1) * hg // 16), bias=shift)
-            if not vend:
-                mm(("BA", i * hg, i * hg + hg), [(T.IB[:, :], ap(part), hg)], [whole("IB"), part], start=False, stop=(i == NHG - 1))
+                w = new("sh"); tt(w, bf, m, ALU.mult); tt(blk(msg, 2), ok, m, ALU.mult)
+            else:
+                wa = new("sm" if last or s + 1 in OPT["split"] else "sh", 2); w, ams[s] = blk(wa, 0), blk(wa, 1)
+                tt(wa, blk(TQ, 2, 2), FL, ALU.mult)
+            more = [(PA, "K16", bf)] + ([] if last else [(PA, "I16", whole("co"))])
+            if OPT["xsplit"]:
+                to_list(PA, "EA", xs, stop=False)
+                mm(more, start=False)
+            else:
+                to_list(PA, "EA", xs, more)
+            tt(mn if last else mun, PA, w, ALU.max)
             if not (last or vend):
-                mm(("BB", i * hg, i * hg + hg), [(T.IH[:, :], ap(part), hg)], [whole("IH"), part], start=False, stop=(i == NHG - 1))
+                (act if "m" in OPT["a16"] else cp)(mn, mun)
+            tt(("anz", 0, 32), ok, blk(cn, 1), ALU.mult)
+            if last:
+                mm([(blk(CN, 0), "IB", blk(cn, 0)), (blk(CN, 0), "N16", bf)])
+                cnn = new("sm"); tt(cnn, blk(CN, 0), ("anz", 0, 32), ALU.max)
+            else:
+                mm([(CN, "IB", cn), (blk(CN, 0), "N16", bf), (blk(CN, 1), "I16", ok)])
+                cnn = blk(msg, 3, 2) if vend else new("sb", 2)
+                tt(cnn, CN, whole("anz"), ALU.max)
+                pr = new("sh", 2); tt(pr, blk(TQ, 0, 2), FL, ALU.mult)
+                three = [tl, blk(pr, 0), blk(pr, 1)]
+                if vend:
+                    mm([(TW, "W16", x) for x in three] + [(TW, "I16", whole("kk"))])
+                mm([(TN, "I16", x) for x in three])
+                tln = blk(msg, 1) if vend else new("sh")
+                (act if "t" in OPT["a16"] else cp)(tln, TN)
+                if not vend:
+                    tzn = new("sm"); act(tzn, TN, bias=float(Z))
+        dg = whole("dh" if shift == 255.0 else "dg%d" % (s % 3))
+        terms = terms + [("I16", "H16", dg) if shift == 255.0 else ("IB", "IH", dg)]
+        for a, b, e in pieces(OPT["vcut"], OPT["veng"]) if vend else pieces(OPT["dcut"], OPT["leng" if last else "deng"]):
+            gather(e, sub(dg, a, b), DTW if s else ("DT", 0, R0), sub(idx, a // 16, b // 16), bias=shift, scale=-1.0)
+        if not vend:
+            stocks(terms[-1:], False, True, not last)
         if s < S_ - 1:
             remote(whole("lE%d" % s), dg)
-        if last:
-            hd = K // NHD
-            for i in range(NHD):
-                part = ("Bf", i * hd, i * hd + hd)
-                act(part, ("BA", i * hd, i * hd + hd))
-                dma("S", T.yb[:, i * hd:i * hd + hd], ap(part), [part], [], 256 // NHD)
-            M5 = new("sh", 9); gt(M5, am, ("rep", 0, 18), OC, ALU.mult)
-            newest = parts.pop(0)
-            parts.insert(0, M5)
-            logsum(stop=False)
-            mm(("PL", 0, n_of(newest)), [(T.I16[:, :], ap(newest), n_of(newest))], [whole("I16"), newest], start=False)
-            act(whole("yo"), ("PL", 0, 288), bias=-1.0)
-            yc = new("sm"); act(yc, c1n, bias=-1.0)
-            dma("S", T.yc[:, :], ap(yc), [yc], [], 16)
-            dma("A", T.yl[:, :], T.yo[:, :], [whole("yo")], [], 144)
-            dma("S", T.ym[:, :], ap(mn), [mn], [], 16)
-            break
+        if s == OPT["sendB"] and not vend:
+            remote(whole("lE2"), dg)
         if vend:
             v = s // S_ + 1
-            lB, lD, lS, lI, lm = (whole(x + str(v)) for x in ("lB", "lD", "lS", "lI", "lm"))
-            pa = new("si"); ts(pa, ti, 3 * K, ALU.bitwise_and)
-            x4 = new("sm"); tt(x4, whole("kk"), pa, ALU.add)
-            if wprev is not None:
-                eq = new("sm"); tt(eq, pa, wprev[0], ALU.is_equal)
-                e = new("sm"); tt(e, eq, wprev[1], ALU.mult)
-                x2, x4 = x4, new("sm"); tt(x4, x2, e, ALU.add)
+            lB, lD, lW, lI, lL = (whole(x + str(v)) for x in ("lB", "lD", "lW", "lI", "lL"))
+            ti = new("si"); tt(ti, TW, whole("kz"), ALU.max)
+            x = new("si"); ts(x, ti, 4 * K - 1, ALU.bitwise_and)
+            if clip is None:
+                e0, e1, lo, hi = new("sm"), new("sm"), new("sm"), new("sm")
+                ts(e0, x, float(K), ALU.is_lt, float(K), ALU.mult); tt(lo, e0, whole("kk"), ALU.add)
+                ts(e1, x, 2.0 * K, ALU.is_lt, float(K), ALU.mult); tt(hi, e1, whole("kz"), ALU.add)
+                clip = (lo, hi)
             else:
-                gap = new("sm"); ts(gap, pa, -1.0, ALU.mult, float(K), ALU.add)
-                wprev = (pa, gap)
-            cp(sub(imsg, 0, 32), x4)
-            ts(sub(imsg, 64, 96), mn, -1.0, ALU.add)
-            remote(lD, dg)
-            if MERGE:
-                remote(lI, imsg)
-                mun = sub(lI, 64, 96)
+                x1, x2 = new("sm"), new("sm")
+                tt(x1, x, clip[0], ALU.max); tt(x2, x1, clip[1], ALU.min)
+                x = x2
+            if OPT["wown"]:
+                wx = new("su"); cp(wx, x)
+                remote(lW, wx)
+                msg, lI = blk(msg, 0, 5), blk(lI, 0, 5)
             else:
-                remote(sub(lI, 0, 64), sub(imsg, 0, 64)); remote(lm, sub(imsg, 64, 96))
-                mun = lm
-            remote(lS, msg)
-            t1n, c1n, n1n, am = sub(lS, 0, 32), sub(lS, 32, 64), sub(lS, 64, 96), sub(lS, 96, 128)
-            thn = sub(lI, 32, 64)
-            mn = new("sh"); ts(mn, mun, 1.0, ALU.add)
-            wg = whole("wg")
-            o = sub(wg, 0, WCUT)
-            add("V", lambda a=sub(lI, 0, WCUT // 16): g.vector.tensor_copy(T.wg[:, 0:WCUT], T.W[:, :].indirect(ap(a))),
-                [whole("W"), sub(lI, 0, 32)], [o], 0.05 + 1.5 * n_of(o) * CY)
-            agather(sub(wg, WCUT, K), whole("W"), sub(lI, WCUT // 16, 32))
-            come = [lB] + ([whole("lE0"), whole("lE1")] if v == 1 else []) + [lD, wg]
+                if v == 2:
+                    ops.pop(); tt(blk(msg, 5), x1, clip[1], ALU.min)
+                else:
+                    cp(blk(msg, 5), x)
+                lW = blk(lI, 5)
+            remote(lD, dg, OPT["pD"])
+            remote(lI, msg, OPT["pI"])
+        for n, group in enumerate(OPT["ugroups"]):
+            if group[-1] == s:
+                if last:
+                    M5 = new("sh", 9); repeat(M5, ams[s], ON, ALU.mult, False)
+                    parts.append(M5)
+                    logsum(9, stop=False)
+                    del parts[:]
+                partners(n, group)
+        if last:
+            for i, a, b in CUT:
+                part = ("Bf", a, b)
+                act(part, BA(i, a, b)) if OPT["yeng"][i] == "A" else cp(part, BA(i, a, b))
+                dma("S", T.yb[:, a:b], ap(part), [part], [], (b - a) / 2)
+            logsum(9, start=False)
+            ts(whole("yo"), ("PL", 0, 288), -float(O), ALU.add, -1.0, ALU.max)
+            yc = new("sm"); act(yc, cnn, bias=-1.0)
+            dma("S", T.yc[:, :], ap(yc), [yc], [], 30)
+            dma("A", T.yl[:, :], T.yo[:, :], [whole("yo")], [], 144)
+            dma("S", T.ym[:, :], ap(mn), [mn], [], 30)
+            break
+        if vend:
+            logsum(s)
+            lg = new("sh", s); cp(lg, ("PL", 0, 32 * s))
+            remote(lL, lg)
+            parts[:] = [lL]
+            mun = blk(lI, 0)
+            ta = new("sh", 3); cp(ta, blk(lI, 0, 3)); mn, tln, ams[s] = blk(ta, 0), blk(ta, 1), blk(ta, 2)
+            tzn = new("sm"); ts(tzn, blk(lI, 1), float(Z), ALU.add)
+            cnn = new("sb", 2); cp(cnn, blk(lI, 3, 2))
+            for a, b, e in pieces(OPT["wcut"], OPT["weng"]):
+                gather(e, ("wg", a, b), whole("W"), sub(lW, a // 16, b // 16))
+            come = [lB] + ([whole("lE0"), whole("lE1")] if v == 1 else [whole("lE2")] * (OPT["sendB"] < s)) + ([whole("wg"), lD] if OPT["wown"] else [lD, whole("wg")])
             for i, x in enumerate(come):
-                mm(whole("BA"), [(T.IB[:, :], ap(x), K)], [whole("IB"), x], start=(i == 0), stop=(x == wg))
-                mm(whole("BB"), [(T.IH[:, :], ap(x), K)], [whole("IH"), x], start=(i == 0), stop=(x == wg))
-            OC = new("sb", s + 1); gt(OC, c1n, ("rep", 0, 2 * s + 2), ("PLC", 0, 32 * s + 32), ALU.is_equal)
-            Ll = sub(lS, 128, 128 + 32 * s)
-            Lh = new("sh", s); cp(Lh, Ll)
-            parts[:] = [Lh]
-            logsum()
-        m, mu, t1, c1, n1, amp, OCp, th = mn, mun, t1n, c1n, n1n, am, OC, thn
+                stocks([("IB", "IH", x)], i == 0, x == come[-1])
+        if 2 <= s < NST - 2:
+            if s + 1 in OPT["split"] or True:
+                logsum(s)
+        m, mu, tl, tz, cn = mn, mun, tln, tzn, cnn
     return ops
 
 
 def depend(ops):
     def meet(a, b):
-        return a[0] == b[0] and (a[0] in PSUM or (a[1] < b[2] and b[1] < a[2]))
+        return a[0] == b[0] and a[1] < b[2] and b[1] < a[2]
     deps = []
     for i, o in enumerate(ops):
         d = {}
         for j in range(i):
             p = ops[j]
-            raw = any(meet(a, b) for a in o["rd"] + o["wr"] for b in p["wr"])
-            war = any(meet(a, b) for a in o["wr"] for b in p["rd"])
-            rar = o["e"] != p["e"] and any(a[0] == b[0] and a[0] in PSUM for a in o["rd"] for b in p["rd"])
-            if raw or rar:
+            if any(meet(a, b) for a in o["rd"] + o["wr"] for b in p["wr"]):
                 d[j] = "done"
-            elif war:
+            elif any(meet(a, b) for a in o["wr"] for b in p["rd"]):
                 d[j] = "left" if p["kind"] == "rem" else "done"
+        for j in o.get("after", ()):
+            d.setdefault(j, "issued")
         deps.append(d)
     return deps
 
 
-def order(ops, deps, bump=None):
+def banks(o):
+    return {r[0] for r in o["rd"] + o["wr"] if r[0] in PSUM}
+
+
+def timing(ops, deps):
+    HOP, SAME = OPT["hop"], OPT["same"]
+    span, uses, lag = [], [], []
+    for i, o in enumerate(ops):
+        c, u = o["cost"], [(o["e"], 0.0, o["cost"], 0.0)] + [(k, 0.0, o["cost"], HOP) for k in banks(o)]
+        if o["kind"] != "c":
+            fix, rate = (OPT["dfix"], OPT["drate"]) if o["kind"] == "dma" else (OPT["rfix"], OPT["rrate"])
+            u += [(k, c + fix, o["kb"] / rate, 0.0) for k in o.get("part", ["dma"])]; c += fix + o["kb"] / rate
+        span.append(c); uses.append(u)
+        lag.append({j: HOP if ops[j]["e"] != o["e"] or ops[j]["kind"] != "c" else (0.0 if o["e"] == "P" else SAME) for j in deps[i]})
+        for j, how in deps[i].items():
+            if how == "issued":
+                lag[i][j] = ops[j]["cost"] - span[j]
+    return span, uses, lag
+
+
+def sweep(ops, span, uses, before, key):
     n = len(ops)
-    succ = [[] for _ in ops]
-    for i, d in enumerate(deps):
-        for j in d:
-            succ[j].append(i)
+    after = [[] for _ in ops]
+    for i in range(n):
+        for j in before[i]:
+            after[j].append(i)
+    left = [len(d) for d in before]; start = [0.0] * n; taken = {}
+    cand = [(key[i], i) for i in range(n) if left[i] == 0]
+    while cand:
+        c = min(cand); cand.remove(c); i = c[1]; e = ops[i]["e"]
+        t = max([start[j] + span[j] + d for j, d in before[i].items()] + [0.0])
+        busy = []
+        for k, off, ln, pad in uses[i]:
+            for a, b, f in reversed(taken.get(k, ())):
+                if a < t + off - 4.5:
+                    break
+                if b + pad - off > t and not (pad and f == e):
+                    busy.append((a - pad - off - ln, b + pad - off))
+        for a, b in sorted(busy):
+            if a < t - 1e-9 and t < b:
+                t = b
+        start[i] = t
+        for k, off, ln, pad in uses[i]:
+            row = taken.setdefault(k, []); q = len(row)
+            while q and row[q - 1][0] > t + off:
+                q -= 1
+            row.insert(q, (t + off, t + off + ln, e))
+        for k in after[i]:
+            left[k] -= 1
+            if left[k] == 0:
+                cand.append((key[k], k))
+    return start, max(start[i] + span[i] for i in range(n))
+
+
+def schedule(ops, deps):
+    n = len(ops)
+    span, uses, lag = timing(ops, deps)
+    back = [{} for _ in ops]
+    for i in range(n):
+        for j, d in lag[i].items():
+            back[j][i] = d
+    mirror = [[(k, span[i] - off - ln, ln, pad) for k, off, ln, pad in uses[i]] for i in range(n)]
+    loads = [i for i in range(n) if ops[i]["kind"] == "dma" and not deps[i]]
+    early = [i for i in range(n) if ops[i].get("early") or (ops[i]["kind"] == "dma" and ops[i]["wr"])]
     tail = [0.0] * n
     for i in range(n - 1, -1, -1):
-        tail[i] = ops[i]["cost"] + ops[i]["lat"] + max([HOP + tail[k] for k in succ[i]] + [0.0])
-    tail = [tail[i] + ops[i].get("first", 0.0) + (bump[i] if bump is not None else 0.0) for i in range(n)]
-    free = {e: 0.0 for e in "VAPGS"}
-    end = [None] * n; left = [len(d) for d in deps]; ready = [0.0] * n
-    cand = [i for i in range(n) if left[i] == 0]; out = []
-    while cand:
-        t0 = min(max(ready[i], free[ops[i]["e"]]) for i in cand)
-        near = [i for i in cand if max(ready[i], free[ops[i]["e"]]) <= t0 + 1e-9]
-        e = ops[near[0]]["e"]
-        pool = [i for i in cand if ops[i]["e"] == e and max(ready[i], free[e]) <= t0 + SLACK]
-        i = max(pool, key=lambda k: tail[k])
-        st = max(ready[i], free[e]); free[e] = st + ops[i]["cost"]; end[i] = free[e] + ops[i]["lat"]
-        ops[i]["st"] = st
-        cand.remove(i); out.append(i)
-        for k in succ[i]:
-            same = ops[k]["e"] == e and ops[i]["kind"] in ("c", "acc")
-            hop = (0.0 if e == "P" else SAME) if same else HOP
-            ready[k] = max(ready[k], end[i] + hop); left[k] -= 1
-            if left[k] == 0:
-                cand.append(k)
-    return out, max(end)
+        tail[i] = span[i] + max([tail[k] + d for k, d in back[i].items()] + [0.0])
+    key, best, top, x = [-t for t in tail], None, None, 1
+    for it in range(OPT["sweeps"]):
+        for i in early:
+            key[i] = i - 1000.0
+        start, end = sweep(ops, span, uses, lag, key)
+        if top is None or end <= top[1]:
+            top = (start, end)
+        if best is None or end <= best[1] + OPT["allow"] * (1.0 - it / OPT["sweeps"]):
+            best = (start, end)
+        noise = []
+        x = (x * 1103515245 + 12345) % 2147483648
+        mid = best[1] * x / 2147483648.0
+        for i in range(n):
+            x = (x * 1103515245 + 12345) % 2147483648
+            noise.append(OPT["noise"] * (x / 2147483648.0 - 0.5) if abs(best[0][i] - mid) < OPT["width"] and x % 8192 < 2048 else 0.0)
+        late, _ = sweep(ops, span, mirror, back, [noise[i] - best[0][i] - span[i] for i in range(n)])
+        key = [-late[i] - span[i] for i in range(n)]
+    return sorted(range(n), key=lambda i: (i not in loads, top[0][i], i)), top[1]
 
 
-SLACK = 0.08
-LOADS = [0, 1, 2, 3, 4, 5]
-
-
-ORDER = [31,8,55,0,2,1,3,4,5,6,21,29,20,9,10,36,33,34,66,7,81,28,32,26,22,24,35,11,15,37,12,17,18,14,63,19,65,13,39,62,69,70,23,38,25,40,41,64,73,16,75,68,71,43,42,47,56,46,44,67,72,60,79,80,57,58,59,30,74,45,27,48,76,82,83,84,85,86,87,88,89,50,49,51,93,94,102,53,105,95,97,91,90,92,96,98,52,78,104,99,100,107,54,77,103,111,112,106,109,110,108,113,114,101,124,125,129,122,123,128,126,127,130,61,119,120,121,131,138,115,116,132,133,134,154,135,136,145,139,150,151,140,141,137,142,143,147,152,148,144,146,149,117,118,158,155,161,156,162,169,160,165,166,173,159,163,167,168,164,153,170,175,174,177,178,184,171,172,180,182,189,185,179,213,194,186,195,176,225,191,187,227,196,183,197,181,199,200,192,201,202,188,190,193,203,198,214,204,215,218,217,206,207,208,216,209,205,210,211,212,226,228,157,230,229,219,232,220,223,224,222,231,233,239,243,238,241,234,244,256,240,245,252,247,242,254,246,258,221,235,236,237,257,261,255,253,263,260,270,249,251,248,250,259,262,264,268,265,267,282,276,271,277,269,272,278,273,274,280,275,281,287,288,289,290,266,283,293,297,294,301,295,284,302,312,296,299,300,310,298,303,308,285,313,291,304,314,286,311,305,317,279,316,309,319,323,321,326,315,318,320,333,324,332,327,343,349,292,307,306,328,329,344,334,337,325,330,331,354,338,335,322,350,351,352,336,345,339,346,340,347,353,359,360,369,370,356,355,341,342,365,366,357,361,363,364,362,358,367,368,373,371,378,374,376,387,375,405,413,386,381,388,379,391,377,392,348,393,372,383,380,390,394,395,396,406,408,407,382,409,389,384,385,410,412,411,414,398,399,400,401,402,397,403,404,415,419,420,418,421,422,417,423,416,430,435,424,428,431,436,448,432,444,429,433,449,434,445,437,452,450,442,446,447,477,443,455,453,426,460,454,483,451,457,459,469,461,458,438,439,440,462,466,467,470,425,463,464,468,456,465,471,472,441,427,473,485,486,490,484,489,478,488,494,493,474,479,487,491,504,505,480,492,475,481,500,508,498,499,501,506,476,509,513,511,516,495,522,502,503,507,533,523,514,510,538,524,528,517,527,496,482,518,519,525,520,512,521,544,542,515,529,543,579,526,534,539,549,530,531,580,532,535,545,536,497,540,547,553,554,548,550,557,546,555,558,556,537,564,568,566,569,565,585,567,578,570,562,581,582,561,583,591,584,551,572,552,559,560,563,586,587,589,590,588,592,593,594,597,576,575,541,577,595,596,573,571,574,598]
+MADE = {}
 
 
 def rank_program(g, core, T, topo):
@@ -531,12 +619,20 @@ def rank_program(g, core, T, topo):
     if rank is None:
         return
     dst = T.cores[(rank + 1) % len(T.cores)]
-    mask = topo.mask(core, dst); neng = len(topo.engines(core, dst))
-    ops = plan(T, g, topo.addr(dst, core), mask, neng)
-    deps = depend(ops)
-    seq = LOADS + [i for i in ORDER if i not in LOADS]
-    for k, i in enumerate(seq):
-        ops[i]["st"] = k
+    ops = plan(T, g, topo.addr(dst, core), topo.engines(core, dst))
+    if not MADE:
+        deps = depend(ops)
+        seq, MADE["time"] = schedule(ops, deps)
+        latest = {}
+        for i in seq:
+            for k in banks(ops[i]):
+                for e, j in latest.setdefault(k, {}).items():
+                    if e != ops[i]["e"]:
+                        deps[i][j] = "done"
+                latest[k][ops[i]["e"]] = i
+        MADE["deps"], MADE["seq"] = deps, seq
+    deps, seq = MADE["deps"], MADE["seq"]
+    pos = {i: k for k, i in enumerate(seq)}
     queue = {"V": g.vector, "A": g.scalar, "P": g.tensor, "G": g, "S": g.sync}
     count = {e: 0 for e in "VAPG"}
     know = {e: {} for e in "VAPGS"}
@@ -545,13 +641,12 @@ def rank_program(g, core, T, topo):
         o = ops[i]; e = o["e"]; kn = know[e]
         need = {}
         for j, how in deps[i].items():
-            p = ops[j]
-            if e == "P" and p["e"] == "P":
+            if how == "issued" or (e == "P" and ops[j]["e"] == "P"):
                 continue
             sem, val = token[(j, how)]
             if kn.get(sem, 0) < val and need.get(sem, (0, 0))[0] < val:
                 need[sem] = (val, j)
-        for sem, (val, j) in sorted(need.items(), key=lambda x: -ops[x[1][1]]["st"]):
+        for sem, (val, j) in sorted(need.items(), key=lambda x: -pos[x[1][1]]):
             if kn.get(sem, 0) >= val:
                 continue
             queue[e].wait_ge(T.sem[sem], val)
@@ -566,11 +661,10 @@ def rank_program(g, core, T, topo):
             o["fn"]().then_inc(T.sem[sem], 16); token[(i, "done")] = (sem, 16); total[sem] = 16
         elif o["kind"] == "rem":
             rs, ls = "r%d" % nr, "l%d" % nr; nr += 1
-            o["fn"](T.sem[rs], T.sem[ls])
+            o["fn"](T.sem[rs], T.sem[ls]); neng = o["n"]
             token[(i, "done")] = (rs, neng); token[(i, "left")] = (ls, neng); total[rs] = neng; total[ls] = neng
         else:
             count[e] += 1
             o["fn"]().then_inc(T.sem["e" + e], 1); token[(i, "done")] = ("e" + e, count[e]); total["e" + e] = count[e]
     for sem, val in total.items():
-        if know["G"].get(sem, 0) < val or True:
-            g.wait_ge(T.sem[sem], val)
+        g.wait_ge(T.sem[sem], val)

@@ -11,24 +11,24 @@ SCRATCH = {
     "F": ("sbuf", [128, C], "bfloat16"),
     "fg0": ("sbuf", [128, K], "bfloat16"), "fg1": ("sbuf", [128, K], "bfloat16"),
     "dg0": ("sbuf", [128, K], "bfloat16"), "dg1": ("sbuf", [128, K], "bfloat16"), "dg2": ("sbuf", [128, K], "bfloat16"),
-    "lE2": ("sbuf", [128, K], "bfloat16"), "lE0": ("sbuf", [128, K], "bfloat16"), "lE1": ("sbuf", [128, K], "bfloat16"),
+    "lH": ("sbuf", [128, K], "float16"), "lE2": ("sbuf", [128, K], "bfloat16"), "lE0": ("sbuf", [128, K], "bfloat16"), "lE1": ("sbuf", [128, K], "bfloat16"),
     "wg": ("sbuf", [128, K], "bfloat16"), "ex": ("sbuf", [128, K], "bfloat16"), "dh": ("sbuf", [128, K], "float16"),
     "H16": ("sbuf", [128, 128], "float16"),
     "Bs0": ("sbuf", [128, K], "bfloat16"), "Bs1": ("sbuf", [128, K], "bfloat16"),
     "IB": ("sbuf", [128, 128], "bfloat16"), "IH": ("sbuf", [128, 128], "bfloat16"), "NB": ("sbuf", [128, 128], "bfloat16"),
-    "NC": ("sbuf", [128, 128], "bfloat16"),
+    "NC": ("sbuf", [128, 128], "bfloat16"), "IP": ("sbuf", [128, 128], "bfloat16"),
     "X": ("sbuf", [128, Z], "int32"), "DT": ("sbuf", [128, DW], "bfloat16"),
     "U": ("sbuf", [128, DW], "bfloat16"), "W": ("sbuf", [128, 3 * K], "bfloat16"),
     "Bi": ("sbuf", [128, K], "bfloat16"), "mi": ("sbuf", [128, 32], "int32"),
     "Bf": ("sbuf", [128, K], "float32"),
-    "st0": ("sbuf", [128, K], "bfloat16"), "st1": ("sbuf", [128, K], "bfloat16"),
+    "st0": ("sbuf", [128, 2 * K], "bfloat16"), "st1": ("sbuf", [128, 2 * K], "bfloat16"),
     "lw0": ("sbuf", [128, K], "bfloat16"), "lw1": ("sbuf", [128, K], "bfloat16"),
     "mk0": ("sbuf", [128, K], "bfloat16"), "mk1": ("sbuf", [128, K], "bfloat16"),
     "xs0": ("sbuf", [128, K], "float16"), "xs1": ("sbuf", [128, K], "float16"),
     "ug0": ("sbuf", [128, 2 * K], "bfloat16"), "ug1": ("sbuf", [128, 2 * K], "bfloat16"),
     "sm": ("sbuf", [128, 32 * 90], "float32"), "sb": ("sbuf", [128, 32 * 90], "bfloat16"),
     "sh": ("sbuf", [128, 32 * 200], "float16"), "su": ("sbuf", [128, 32 * 40], "uint16"),
-    "si": ("sbuf", [128, 32 * 8], "int32"),
+    "si": ("sbuf", [128, 32 * 12], "int32"),
     "lB1": ("sbuf", [128, K], "bfloat16"), "lB2": ("sbuf", [128, K], "bfloat16"),
     "lD1": ("sbuf", [128, K], "bfloat16"), "lD2": ("sbuf", [128, K], "bfloat16"),
     "lW1": ("sbuf", [128, 32], "uint16"), "lW2": ("sbuf", [128, 32], "uint16"),
@@ -47,6 +47,8 @@ SCRATCH = {
     "cl": ("sbuf", [128, 128], "float32"), "SG": ("sbuf", [128, 128], "float32"), "I32": ("sbuf", [128, 128], "float32"),
     "g0": ("sbuf", [128, 128], "float32"), "T2b": ("sbuf", [128, 128], "float32"), "T1b": ("sbuf", [128, 128], "float32"),
     "T1": ("sbuf", [128, 128], "bfloat16"), "T2": ("sbuf", [128, 128], "bfloat16"),
+    "T0": ("sbuf", [128, 128], "bfloat16"), "T3": ("sbuf", [128, 128], "bfloat16"), "T4": ("sbuf", [128, 128], "bfloat16"),
+    "ones": ("sbuf", [128, 256], "bfloat16"), "xg": ("sbuf", [128, K], "float16"), "xw": ("sbuf", [128, K], "uint16"),
     "I16": ("sbuf", [128, 128], "float16"), "N16": ("sbuf", [128, 128], "float16"), "K16": ("sbuf", [128, 128], "float16"),
     "W16": ("sbuf", [128, 128], "float16"),
     "cz": ("sbuf", [128, 32], "float16"), "co": ("sbuf", [128, 32], "float16"), "anz": ("sbuf", [128, 64], "float32"),
@@ -59,23 +61,23 @@ SCRATCH = {
     "PL": ("psum", [128, 512], "float32"), "PT": ("psum", [128, 512], "float32"),
 }
 PSUM = ("z0", "z1", "B0", "B1", "B2", "PB", "PL", "PT")
-NDMA, NREM = 32, 14
+NDMA, NREM = 36, 14
 SEMAPHORES = ["eV", "eA", "eP", "eG"] + ["d%d" % i for i in range(NDMA)] + ["r%d" % i for i in range(NREM)] + ["l%d" % i for i in range(NREM)]
 
 OPT = {
     "fcut": (0, 128, 256, 512), "feng": "AAA",
     "cut": (0, 256, 512),
     "xcut": (0, 256, 512),
-    "dcut": (0, 256, 512), "deng": "AAA", "leng": "AAA", "vcut": (0, 320, 512), "veng": "AV",
-    "wcut": (0, 256, 512), "weng": "VVV",
-    "yeng": "AAA", "vclamp": (), "gate": "F", "wown": False, "peo": (8, 9), "pem": (), "sp": ("B2", 32), "uearly": True,
-    "xsplit": True, "cq": ("B2", 0, 32), "sendB": 4, "pD": "ab", "pI": "ab", "half": 1.5, "bcut": (0, 256, 512), "uq": ("z1", 416, 512),
-    "zat": (("z0", 0), ("z1", 0), ("z0", 256), ("z1", 208)), "a16": "", "feng0": "VVV", "rfirst": 4.0,
+    "dcut": (0, 256, 512), "deng": "VA", "leng": "AA", "vcut": (0, 320, 512), "veng": "AV",
+    "wcut": (0, 128, 256, 512), "weng": "VAV",
+    "ycut": (0, 256, 512), "yeng": "AAAA", "vclamp": (), "gate": "F", "wown": False, "ahead": (3, 6, 8), "xmode": "NNNN", "gcut": (0, 512), "geng": "AAA", "ccut": (0, 256, 512), "peo": (8, 9), "pem": (), "sp": ("B2", 64), "along": (7,), "dvV": True, "uearly": True,
+    "xsplit": True, "cq": ("B2", 0, 32), "sendB": 4, "pD": "ab", "pI": "ab", "half": 1.5, "bcut": (0, 256, 512), "uq": ("B2", 416, 512),
+    "zat": (("z0", 0), ("z1", 0), ("z0", 256), ("z1", 208)), "a16": "t", "feng0": "PPV", "rfirst": 4.0,
     "copy": (1, 4, 7),
     "split": (4,),
-    "ugroups": ((1, 2), (3,), (4, 5), (6,), (7,), (8,)), "ueng": "AAAAAAAAV",
-    "cy": 0.83e-3, "pcy": 0.4e-3, "hop": 0.14, "same": 0.2, "gat": 1.5, "afix": 0.08,
-    "dfix": 1.0, "drate": 280.0, "rfix": 1.0, "rrate": 100.0, "rissue": 1.2, "sweeps": 4000, "noise": 1.2, "width": 2.0, "allow": 0.05,
+    "ugroups": ((1, 2), (3,), (4, 5), (6,), (7,), (8,)), "ueng": "AAAAAAAAA",
+    "cy": 0.83e-3, "pcy": 0.46e-3, "hop": 0.14, "same": 0.2, "gat": 1.5, "afix": 0.08,
+    "loads": "Fm0B1X", "mq": "A", "dfix": 0.95, "drate": 300.0, "rfix": 1.0, "rrate": 80.0, "rissue": 1.2, "seed": 1, "sweeps": 4000, "noise": 1.2, "width": 2.0, "allow": 0.05,
 }
 
 
@@ -197,12 +199,18 @@ def plan(T, g, dst_addr, engines):
         return ("pc", j, j + 1)
 
     FW, XW, DTW = ("DT", 0, Z), whole("X"), whole("DT")
-    dma("S", T.mi[:, :], T.m0[:, :], [], [whole("mi")], 30)
-    dma("S", T.DT[:, O:Z], T.fm[:, :], [], [("DT", O, Z)], 384)
-    dma("A", T.Bi[:, :], T.b0[:, :], [], [whole("Bi")], 128)
-    for gg in range(2):
-        dma("S", T.xa[:, 48 * gg:48 * gg + 48], T.nx[16 * gg::32, :], [], [("xa", 48 * gg, 48 * gg + 48)], 50)
-    dma("S", T.X[:, O:Z], T.nx[:, :], [], [("X", O, Z)], 768)
+    for c in OPT["loads"]:
+        if c == "m":
+            dma(OPT["mq"], T.mi[:, :], T.m0[:, :], [], [whole("mi")], 45)
+        if c == "F":
+            dma("S", T.DT[:, O:Z], T.fm[:, :], [], [("DT", O, Z)], 420)
+        if c == "B":
+            dma("A", T.Bi[:, :], T.b0[:, :], [], [whole("Bi")], 160)
+        if c in "01":
+            gg = int(c)
+            dma("S", T.xa[:, 48 * gg:48 * gg + 48], T.nx[16 * gg::32, :], [], [("xa", 48 * gg, 48 * gg + 48)], 55)
+        if c == "X":
+            dma("S", T.X[:, O:Z], T.nx[:, :], [], [("X", O, Z)], 810)
     iota(("pi", 0, 1), [[0, 1]], 0, 1)
     iota(whole("xi"), [[1, 144]], 0, 0)
     iota(whole("rel"), [[1, 128]], 0, -1)
@@ -223,11 +231,20 @@ def plan(T, g, dst_addr, engines):
     tt(whole("T2"), whole("T2b"), whole("SG"), ALU.mult)
     act(whole("T1b"), whole("T2b"), bias=-4.0, scale=512.0)
     tt(whole("T1"), whole("T1b"), whole("SG"), ALU.mult)
+    if "N" in OPT["xmode"]:
+        ts(whole("T0"), whole("I32"), ap(col(4)), ALU.mult, cols=[col(4)])
+        ts(whole("T3"), whole("T1"), 2048.0, ALU.mult); ts(whole("T4"), whole("T2"), 2048.0, ALU.mult)
+        fill(whole("ones"), 1.0)
     cp(whole("I16"), whole("I32"))
-    for name, v in (("N16", -1.0), ("K16", -4096.0), ("W16", 1024.0), ("H16", 0.5)):
+    for name, v in (("N16", -1.0), ("K16", -4096.0), ("W16", 1024.0)):
         ts(whole(name), whole("I16"), v, ALU.mult)
-    for name, v in (("IB", 1.0), ("IH", 0.5), ("NB", -1.0), ("NC", -0.5)):
+    ts(col(6), col(1), 15.0, ALU.not_equal, 0.5, ALU.mult)
+    ts(col(7), col(6), -1.0, ALU.mult)
+    ts(col(8), col(6), 3.0, ALU.mult, -1.0, ALU.add)
+    for name, v in (("IB", 1.0), ("NB", -1.0)):
         act(whole(name), whole("I32"), scale=v)
+    for name, j in (("IH", 6), ("NC", 7), ("IP", 8), ("H16", 8)):
+        act(whole(name), whole("I32"), scale=ap(col(j)), cols=[col(j)])
     iota(whole("PLC"), [[1, 9], [0, 32]], 1, 0)
     iota(("ri", 0, 18), [[0, 9], [16, 2]], 0, 1)
     ts(("rep", 0, 18), ("ri", 0, 18), ap(col(0)), ALU.subtract, cols=[col(0)])
@@ -244,7 +261,9 @@ def plan(T, g, dst_addr, engines):
     ops[first]["after"] = [i for i in range(first) if ops[i]["e"] == "G"]
     for a in range(0, DW, K):
         b = min(a + K, DW)
-        dma("S", T.U[:, a:b], T.W[:, K:K + b - a], [XW, ("W", K, 2 * K)], [("U", a, b)], (b - a) / 4 + 10)
+        dma("S", T.U[:, a:b], T.W[:, K:K + b - a], [XW, ("W", K, 2 * K)], [("U", a, b)], (b - a) / 4 + 25)
+    for i in range(2):
+        dma("S", T.W[:, 2 * i * K:2 * i * K + K], T.wl[:, i % 2 * K:i % 2 * K + K], [XW], [("W", 2 * i * K, 2 * i * K + K)], 150)
     ts(("pi", 8, 9), ("pi", 0, 1), 31, ALU.bitwise_and)
     ts(col(5), ("pi", 8, 9), 48.0, ALU.mult)
     ts(whole("tm"), whole("tj"), ap(col(5)), ALU.add, cols=[col(5)])
@@ -256,6 +275,13 @@ def plan(T, g, dst_addr, engines):
     for b in range(3):
         add("V", lambda b=b: g.vector.tensor_copy(T.xu[:, b:96:3], T.xt[:, 32 * b:32 * b + 32]), [whole("xt")], [blk(whole("xu"), b)], 64 * CY)
     for i in range(3):
+        if OPT["feng0"][i] == "P":
+            at = (("PL", "PT", "PB")[i], 0, K)
+            gather("A", ("F", K * i, K * i + K), FW, blk(whole("xu"), i))
+            ops[-1]["rd"].append(whole("xu"))
+            mm([(at, "IB", ("F", K * i, K * i + K)), (at, "NB", ("DT", O + K * i, O + K * i + K))])
+            act(("DT", R0 + K * i, R0 + K * i + K), at)
+            continue
         (cp if OPT["feng0"][i] == "V" else act)(("F", K * i, K * i + K), ("DT", O + K * i, O + K * i + K))
         gt(("DT", R0 + K * i, R0 + K * i + K), FW, blk(whole("xu"), i), ("F", K * i, K * i + K), ALU.subtract)
         ops[-1]["rd"].append(whole("xu"))
@@ -268,8 +294,6 @@ def plan(T, g, dst_addr, engines):
     for gg in range(2):
         dma("S", T.U[16 * gg + 1::32, R0:DW], T.xh[:, 48 * gg:48 * gg + 48], [whole("xh"), ("U", R0 + 4, DW)], [("U", R0 + gg, R0 + gg + 1)], 40)
         dma("S", T.U[16 * gg + 2::32, R0:DW], T.xl[:, 48 * gg:48 * gg + 48], [whole("xl"), ("U", R0 + 4, DW)], [("U", R0 + 2 + gg, R0 + 3 + gg)], 40)
-    dma("S", T.W[:, 0:K], T.wl[:, 0:K], [XW], [("W", 0, K)], 128)
-    dma("S", T.W[:, 2 * K:3 * K], T.wl[:, K:2 * K], [XW], [("W", 2 * K, 3 * K)], 128)
 
     mu = new("su"); ts(mu, whole("mi"), float(O), ALU.add)
     m = new("sh"); ts(m, whole("mi"), float(O), ALU.add)
@@ -290,14 +314,23 @@ def plan(T, g, dst_addr, engines):
 
     terms = [("IB", "IH", whole("Bi"))]
     stocks(terms, True, True)
-    parts, idxs, ams, OCs = [], {}, {}, {}
+    parts, idxs, ams, OCs, bfs, tzs = [], {}, {}, {}, {}, {}
     tl = cn = clip = None
     tz = whole("cz")
     TQ, TN, TW, CN, UQ = ("PT", 0, 128), ("PT", 128, 160), ("PT", 160, 192), ("PT", 192, 256), OPT["uq"]
 
+    wide = [0]
+
     def logsum(width, start=True, stop=True, now=None):
         now = sorted(parts if now is None else now, key=lambda x: -n_of(x))
-        mm([(("PL", 0, min(n_of(x), 32 * width)), "I16", sub(x, 0, min(n_of(x), 32 * width))) for x in now], start, stop)
+        items = []
+        if start:
+            wide[0] = min(n_of(now[0]), 32 * width)
+        for x in now:
+            n = min(n_of(x), 32 * width)
+            items += [(("PL", a, b), "I16", sub(x, a, b)) for a, b in ((0, min(n, wide[0])), (wide[0], n)) if a < b]
+            wide[0] = max(wide[0], n)
+        mm(items, start, stop)
 
     def repeat(o, x, y, op, pe):
         k = n_of(o) // 32
@@ -312,14 +345,32 @@ def plan(T, g, dst_addr, engines):
         M = new("sh", s); repeat(M, value, OCs[s], ALU.mult, value[0] == "sh")
         parts.append(M)
 
+    def below(s, tl):
+        more = []
+        if s >= 2:
+            M4 = new("sh", s - 1)
+            if s == 2:
+                tt(M4, ams[0], blk(OCs[s], 1), ALU.mult)
+            else:
+                tt(M4, ("PL", 0, 32 * s - 32), blk(OCs[s], 1, s - 1), ALU.mult)
+            more = [(blk(TQ, 0), "I16", blk(M4, i)) for i in range(s - 1)]
+        mm([(blk(TQ, 0), "N16", tl)] + more)
+
     def partners(n, group):
+        if group[0] in OPT["along"]:
+            gather(OPT["ueng"][group[0]], ("st%d" % ((group[0] + 1) % 2), K, 2 * K), whole("U"), idxs[group[0]])
+            return
         ug = ("ug%d" % (n % 2), 0, K * len(group))
         for i, s in enumerate(group):
-            gather(OPT["ueng"][s], sub(ug, K * i, K * i + K), whole("U"), idxs[s])
+            gather(OPT["ueng"][s], sub(ug, K * i, K * i + K), whole("U"), tzs[s] if s in OPT["ahead"] else idxs[s])
         uq = blk(UQ, 0, len(group))
-        to_list(uq, "EB", ug, [(blk(uq, i), "I16", ams[s - 1]) for i, s in enumerate(group) if s > 1 and s not in OPT["split"]])
+        to_list(uq, "EB", ug, [(blk(uq, i), "I16", ams[s - 1]) for i, s in enumerate(group)
+                               if s > 1 and s not in OPT["split"] + OPT["ahead"]])
         for i, s in enumerate(group):
-            if s == 1:
+            if s in OPT["ahead"]:
+                p, dv = new("sm"), new("sh" if s in OPT["pem"] else "sm")
+                tt(p, blk(uq, i), bfs[s], ALU.mult); tt(dv, p, ams[s - 1], ALU.add); place(s, dv)
+            elif s == 1:
                 dv = new("sh"); cp(dv, blk(uq, i)); parts.append(dv)
             else:
                 dv = new("sh" if s in OPT["pem"] else "sm"); act(dv, blk(uq, i)); place(s, dv)
@@ -327,22 +378,15 @@ def plan(T, g, dst_addr, engines):
     for s in range(NST):
         last = s == NST - 1
         vend = s % S_ == S_ - 1 and not last
-        st, lw, mk, xs, fg = (whole(x + str(s % 2)) for x in ("st", "lw", "mk", "xs", "fg"))
+        st, lw, mk, xs, fg = ((x + str(s % 2), 0, K) for x in ("st", "lw", "mk", "xs", "fg"))
         if s >= 2:
             OCs[s] = new("sb", s); repeat(OCs[s], blk(cn, 0), ("PLC", 0, 32 * s), ALU.is_equal, s in OPT["peo"])
             if s in OPT["split"]:
                 place(s, ams[s - 1])
         if s >= 1:
-            below = []
-            if 2 <= s < NST - 1:
-                M4 = new("sh", s - 1)
-                if s == 2:
-                    tt(M4, ams[0], blk(OCs[s], 1), ALU.mult)
-                else:
-                    tt(M4, ("PL", 0, 32 * s - 32), blk(OCs[s], 1, s - 1), ALU.mult)
-                below = [(blk(TQ, 0), "I16", blk(M4, i)) for i in range(s - 1)]
             if not last:
-                mm([(blk(TQ, 0), "N16", tl)] + below)
+                if s - 1 not in OPT["along"]:
+                    below(s, tl)
                 mm([(blk(TQ, 1), "I16", m), (blk(TQ, 1), "N16", tl)])
                 if not vend:
                     mm([(blk(TQ, 2), "I16", m), (blk(TQ, 3), "I16", m)])
@@ -363,29 +407,55 @@ def plan(T, g, dst_addr, engines):
             for i, a, b in CUT:
                 act(("ex", a, b), BA(i, a, b), AF.Relu, bias=255.0, scale=-1.0)
             terms, shift = [("NB", "NC", whole("ex"))], 255.0
-        elif s == OPT["sendB"] or s in OPT["copy"]:
+            if s == S_:
+                remote(whole("lB2"), whole("ex"))
+        elif s == 2 * S_ - 1:
+            shift = -128.0 if s - 1 in OPT["copy"] else 0.0
+        elif s in OPT["copy"]:
             Bs, shift = whole("Bs%d" % (s % 2)), 128.0 if s > 1 else 0.0
             for i, a, b in CUT:
                 act(sub(Bs, a, b), BA(i, a, b), bias=-shift)
             terms = [("IB", "IH", Bs)]
-            if s == OPT["sendB"]:
-                remote(whole("lB2"), Bs)
-        if not vend:
-            stocks(terms, True, False, not last)
+        ends = [(("B%d" % (i % 2), 256 * (i // 2), 256 * (i // 2) + b - a), a, b, e)
+                for i, (a, b, e) in enumerate(pieces(OPT["ycut"], OPT["yeng"]))]
+        if last:
+            for at, a, b, _ in ends[:2]:
+                mm([(at, x, sub(y, a, b)) for x, _, y in terms], True, False)
+        elif not vend:
+            stocks(terms, True, False)
         Cq = OPT["cq"]
         idx = idxs[s] = new("su")
         FL = new("sh", 2); bf, ok = blk(FL, 0), blk(FL, 1)
-        to_list(Cq, "EB", st, [(Cq, "I16", m)])
+        bfs[s], tzs[s] = bf, tz
+        if s - 1 in OPT["along"]:
+            to_list(sub(Cq, 0, 64), "EB", whole(st[0]), [(Cq, "I16", m), (sub(Cq, 32, 64), "I16", ams[s - 2])])
+        else:
+            to_list(Cq, "EB", st, [(Cq, "I16", m)])
         tt(idx, Cq, tz, ALU.min)
         tt(ok, Cq, m, ALU.is_equal)
+        if s - 1 in OPT["along"]:
+            dv = new("sm"); (cp if OPT["dvV"] else act)(dv, sub(Cq, 32, 64)); place(s - 1, dv)
+            if not last:
+                logsum(s - 1); below(s, tl)
         if s:
             ts(bf, idx, float(Z), ALU.is_gt)
         for i, (_, a, b) in enumerate(FINE):
             z = (OPT["zat"][i][0], OPT["zat"][i][1], OPT["zat"][i][1] + b - a)
-            mm([(z, "T1", sub(st, a, b)), (z, "T2", sub(lw, a, b))])
-            act(sub(mk, a, b), z, AF.Relu, bias=ap(col(4)), scale=2048.0, cols=[col(4)])
-        for a, b, _ in pieces(OPT["xcut"], "VVVVVV"):
-            gt(sub(xs, a, b), XW, sub(mu, a // 16, b // 16), sub(mk, a, b), ALU.min)
+            if OPT["xmode"][i] == "R" or s == 0:
+                mm([(z, "T1", sub(st, a, b)), (z, "T2", sub(lw, a, b))])
+                act(sub(mk, a, b), z, AF.Relu, bias=ap(col(4)), scale=2048.0, cols=[col(4)])
+                gt(sub(xs, a, b), XW, sub(mu, a // 16, b // 16), sub(mk, a, b), ALU.min)
+            else:
+                if i == 0:
+                    for c, d, e in pieces(OPT["gcut"], OPT["geng"]):
+                        gather(e, ("xg", c, d), XW, sub(mu, c // 16, d // 16), bias=0.0 if last else float(O))
+                if not lifted:
+                    mm([(z, "T0", ("ones", 0, b - a))], stop=False)
+                mm([(z, "T3", sub(st, a, b)), (z, "T4", sub(lw, a, b))], start=lifted)
+                tt(("xw", a, b), z, ("xg", a, b), ALU.min)
+                if b in OPT["ccut"]:
+                    c = OPT["ccut"][OPT["ccut"].index(b) - 1]
+                    cp(sub(xs, c, b), ("xw", c, b))
         PA = ("PB", 64, 96)
         msg = new("su", 6) if vend else None
         mn = new("sm" if last else "sh"); mun = blk(msg, 0) if vend else new("su")
@@ -401,9 +471,9 @@ def plan(T, g, dst_addr, engines):
             if vend:
                 w = new("sh"); tt(w, bf, m, ALU.mult); tt(blk(msg, 2), ok, m, ALU.mult)
             else:
-                wa = new("sm" if last or s + 1 in OPT["split"] else "sh", 2); w, ams[s] = blk(wa, 0), blk(wa, 1)
+                wa = new("sm" if (last and 9 not in OPT["pem"]) or s + 1 in OPT["split"] else "sh", 2); w, ams[s] = blk(wa, 0), blk(wa, 1)
                 tt(wa, blk(TQ, 2, 2), FL, ALU.mult)
-            more = [(PA, "K16", bf)] + ([] if last else [(PA, "I16", whole("co"))])
+            more = [(PA, "K16", bf)]
             if OPT["xsplit"]:
                 to_list(PA, "EA", xs, stop=False)
                 mm(more, start=False)
@@ -428,20 +498,26 @@ def plan(T, g, dst_addr, engines):
                 tln = blk(msg, 1) if vend else new("sh")
                 (act if "t" in OPT["a16"] else cp)(tln, TN)
                 if not vend:
-                    tzn = new("sm"); act(tzn, TN, bias=float(Z))
+                    tzn = new("su" if s + 1 in OPT["ahead"] else "sm"); act(tzn, TN, bias=float(Z))
         dg = whole("dh" if shift == 255.0 else "dg%d" % (s % 3))
-        terms = terms + [("I16", "H16", dg) if shift == 255.0 else ("IB", "IH", dg)]
-        for a, b, e in pieces(OPT["vcut"], OPT["veng"]) if vend else pieces(OPT["dcut"], OPT["leng" if last else "deng"]):
+        terms = terms + [("I16", "H16", dg) if shift == 255.0 else ("IB", "IP" if shift > 0 else "IH", dg)]
+        lifted = any(x in ("IP", "H16") for _, x, _ in terms)
+        for a, b, e in pieces(OPT["vcut"], OPT["veng"]) if vend else pieces(OPT["ycut" if last else "dcut"], OPT["leng" if last else "deng"]):
             gather(e, sub(dg, a, b), DTW if s else ("DT", 0, R0), sub(idx, a // 16, b // 16), bias=shift, scale=-1.0)
-        if not vend:
-            stocks(terms[-1:], False, True, not last)
+        if last:
+            for i, (at, a, b, _) in enumerate(ends):
+                mm([(at, x, sub(y, a, b)) for x, _, y in (terms[-1:] if i < 2 else terms)], i >= 2, True)
+                if i >= 2:
+                    ops[-1]["rd"].append(ends[i - 2][0])
+        elif not vend:
+            stocks(terms[-1:], False, True)
         if s < S_ - 1:
             remote(whole("lE%d" % s), dg)
-        if s == OPT["sendB"] and not vend:
-            remote(whole("lE2"), dg)
+        if S_ <= s < 2 * S_ - 1:
+            remote(whole("lH" if s == S_ else "lE2"), dg)
         if vend:
             v = s // S_ + 1
-            lB, lD, lW, lI, lL = (whole(x + str(v)) for x in ("lB", "lD", "lW", "lI", "lL"))
+            lB, lD, lI, lL = (whole(x + str(v)) for x in ("lB", "lD", "lI", "lL"))
             ti = new("si"); tt(ti, TW, whole("kz"), ALU.max)
             x = new("si"); ts(x, ti, 4 * K - 1, ALU.bitwise_and)
             if clip is None:
@@ -449,41 +525,32 @@ def plan(T, g, dst_addr, engines):
                 ts(e0, x, float(K), ALU.is_lt, float(K), ALU.mult); tt(lo, e0, whole("kk"), ALU.add)
                 ts(e1, x, 2.0 * K, ALU.is_lt, float(K), ALU.mult); tt(hi, e1, whole("kz"), ALU.add)
                 clip = (lo, hi)
+                cp(blk(msg, 5), x)
             else:
-                x1, x2 = new("sm"), new("sm")
-                tt(x1, x, clip[0], ALU.max); tt(x2, x1, clip[1], ALU.min)
-                x = x2
-            if OPT["wown"]:
-                wx = new("su"); cp(wx, x)
-                remote(lW, wx)
-                msg, lI = blk(msg, 0, 5), blk(lI, 0, 5)
-            else:
-                if v == 2:
-                    ops.pop(); tt(blk(msg, 5), x1, clip[1], ALU.min)
-                else:
-                    cp(blk(msg, 5), x)
-                lW = blk(lI, 5)
+                x1 = new("sm")
+                tt(x1, x, clip[0], ALU.max); tt(blk(msg, 5), x1, clip[1], ALU.min)
             remote(lD, dg, OPT["pD"])
             remote(lI, msg, OPT["pI"])
         for n, group in enumerate(OPT["ugroups"]):
             if group[-1] == s:
                 if last:
-                    M5 = new("sh", 9); repeat(M5, ams[s], ON, ALU.mult, False)
-                    parts.append(M5)
-                    logsum(9, stop=False)
+                    M5 = new("sh", 9); repeat(M5, ams[s], ON, ALU.mult, 9 in OPT["pem"])
+                    logsum(9, stop=False, now=parts[:-1])
+                    for x in (parts[-1], M5):
+                        logsum(9, start=False, stop=False, now=[x])
                     del parts[:]
                 partners(n, group)
         if last:
-            for i, a, b in CUT:
+            for at, a, b, e in ends:
                 part = ("Bf", a, b)
-                act(part, BA(i, a, b)) if OPT["yeng"][i] == "A" else cp(part, BA(i, a, b))
-                dma("S", T.yb[:, a:b], ap(part), [part], [], (b - a) / 2)
+                (act if e == "A" else cp)(part, at)
+                dma("S", T.yb[:, a:b], ap(part), [part], [], (b - a) / 2 + 32)
             logsum(9, start=False)
             ts(whole("yo"), ("PL", 0, 288), -float(O), ALU.add, -1.0, ALU.max)
             yc = new("sm"); act(yc, cnn, bias=-1.0)
-            dma("S", T.yc[:, :], ap(yc), [yc], [], 30)
-            dma("A", T.yl[:, :], T.yo[:, :], [whole("yo")], [], 144)
-            dma("S", T.ym[:, :], ap(mn), [mn], [], 30)
+            dma("S", T.yc[:, :], ap(yc), [yc], [], 48)
+            dma("A", T.yl[:, :], T.yo[:, :], [whole("yo")], [], 176)
+            dma("S", T.ym[:, :], ap(mn), [mn], [], 48)
             break
         if vend:
             logsum(s)
@@ -492,16 +559,16 @@ def plan(T, g, dst_addr, engines):
             parts[:] = [lL]
             mun = blk(lI, 0)
             ta = new("sh", 3); cp(ta, blk(lI, 0, 3)); mn, tln, ams[s] = blk(ta, 0), blk(ta, 1), blk(ta, 2)
-            tzn = new("sm"); ts(tzn, blk(lI, 1), float(Z), ALU.add)
+            tzn = new("su" if s + 1 in OPT["ahead"] else "sm"); ts(tzn, blk(lI, 1), float(Z), ALU.add)
             cnn = new("sb", 2); cp(cnn, blk(lI, 3, 2))
             for a, b, e in pieces(OPT["wcut"], OPT["weng"]):
-                gather(e, ("wg", a, b), whole("W"), sub(lW, a // 16, b // 16))
-            come = [lB] + ([whole("lE0"), whole("lE1")] if v == 1 else [whole("lE2")] * (OPT["sendB"] < s)) + ([whole("wg"), lD] if OPT["wown"] else [lD, whole("wg")])
+                gather(e, ("wg", a, b), whole("W"), sub(blk(lI, 5), a // 16, b // 16))
+            come = [lB] + ([whole("lE0"), whole("lE1")] if v == 1 else [whole("lH"), whole("lE2")]) + [lD, whole("wg")]
             for i, x in enumerate(come):
-                stocks([("IB", "IH", x)], i == 0, x == come[-1])
-        if 2 <= s < NST - 2:
-            if s + 1 in OPT["split"] or True:
-                logsum(s)
+                stocks([{"lB2": ("NB", "NC"), "lH": ("I16", "H16")}.get(x[0], ("IB", "IH")) + (x,)], i == 0, x == come[-1])
+            lifted = whole("lH") in come
+        if 2 <= s < NST - 2 and s not in OPT["along"]:
+            logsum(s)
         m, mu, tl, tz, cn = mn, mun, tln, tzn, cnn
     return ops
 
@@ -591,7 +658,7 @@ def schedule(ops, deps):
     tail = [0.0] * n
     for i in range(n - 1, -1, -1):
         tail[i] = span[i] + max([tail[k] + d for k, d in back[i].items()] + [0.0])
-    key, best, top, x = [-t for t in tail], None, None, 1
+    key, best, top, x = [-t for t in tail], None, None, OPT["seed"]
     for it in range(OPT["sweeps"]):
         for i in early:
             key[i] = i - 1000.0

from concourse.mybir import AluOpType as ALU, ActivationFunctionType as AF

C, K, V_, S_ = 1536, 512, 3, 3
NST = V_ * S_
O = 16
Z = O + C
R0 = Z + O
DW = R0 + C

SCRATCH = {
    "F": ("sbuf", [128, C], "bfloat16"),
    "fg0": ("sbuf", [128, K], "bfloat16"), "fg1": ("sbuf", [128, K], "bfloat16"),
    "dg0": ("sbuf", [128, K], "bfloat16"), "dg1": ("sbuf", [128, K], "bfloat16"), "dg2": ("sbuf", [128, K], "bfloat16"),
    "lH": ("sbuf", [128, K], "float16"), "lE2": ("sbuf", [128, K], "bfloat16"), "lE0": ("sbuf", [128, K], "bfloat16"), "lE1": ("sbuf", [128, K], "bfloat16"),
    "wg": ("sbuf", [128, K], "bfloat16"), "ex": ("sbuf", [128, K], "bfloat16"), "dh": ("sbuf", [128, K], "float16"),
    "H16": ("sbuf", [128, 128], "float16"),
    "Bs0": ("sbuf", [128, K], "bfloat16"), "Bs1": ("sbuf", [128, K], "bfloat16"),
    "IB": ("sbuf", [128, 128], "bfloat16"), "IH": ("sbuf", [128, 128], "bfloat16"), "NB": ("sbuf", [128, 128], "bfloat16"),
    "NC": ("sbuf", [128, 128], "bfloat16"), "IP": ("sbuf", [128, 128], "bfloat16"),
    "X": ("sbuf", [128, Z], "int32"), "DT": ("sbuf", [128, DW], "bfloat16"),
    "U": ("sbuf", [128, DW], "bfloat16"), "W": ("sbuf", [128, 3 * K], "bfloat16"),
    "Bi": ("sbuf", [128, K], "bfloat16"), "mi": ("sbuf", [128, 32], "int32"),
    "Bf": ("sbuf", [128, K], "float32"),
    "st0": ("sbuf", [128, 2 * K], "bfloat16"), "st1": ("sbuf", [128, 2 * K], "bfloat16"),
    "lw0": ("sbuf", [128, K], "bfloat16"), "lw1": ("sbuf", [128, K], "bfloat16"),
    "mk0": ("sbuf", [128, K], "bfloat16"), "mk1": ("sbuf", [128, K], "bfloat16"),
    "xs0": ("sbuf", [128, K], "float16"), "xs1": ("sbuf", [128, K], "float16"),
    "ug0": ("sbuf", [128, 2 * K], "bfloat16"), "ug1": ("sbuf", [128, 2 * K], "bfloat16"),
    "sm": ("sbuf", [128, 32 * 90], "float32"), "sb": ("sbuf", [128, 32 * 90], "bfloat16"),
    "sh": ("sbuf", [128, 32 * 200], "float16"), "su": ("sbuf", [128, 32 * 40], "uint16"),
    "si": ("sbuf", [128, 32 * 12], "int32"),
    "lB1": ("sbuf", [128, K], "bfloat16"), "lB2": ("sbuf", [128, K], "bfloat16"),
    "lD1": ("sbuf", [128, K], "bfloat16"), "lD2": ("sbuf", [128, K], "bfloat16"),
    "lW1": ("sbuf", [128, 32], "uint16"), "lW2": ("sbuf", [128, 32], "uint16"),
    "lI1": ("sbuf", [128, 192], "uint16"), "lI2": ("sbuf", [128, 192], "uint16"),
    "lL1": ("sbuf", [128, 32 * 2], "float16"), "lL2": ("sbuf", [128, 32 * 5], "float16"),
    "xa": ("sbuf", [128, 96], "int32"), "xf": ("sbuf", [128, 96], "float32"), "xt": ("sbuf", [128, 96], "float32"),
    "xu": ("sbuf", [128, 96], "uint16"), "xp": ("sbuf", [128, 96], "float32"), "xy": ("sbuf", [128, 96], "float32"),
    "xd": ("sbuf", [128, 96], "float32"), "tj": ("sbuf", [128, 96], "float32"), "tm": ("sbuf", [128, 96], "float32"),
    "xh": ("sbuf", [128, 96], "bfloat16"), "xl": ("sbuf", [128, 96], "bfloat16"),
    "pi": ("sbuf", [128, 16], "int32"), "pc": ("sbuf", [128, 16], "float32"),
    "xi": ("sbuf", [128, 144], "float32"), "dd": ("sbuf", [128, 144], "float32"), "rel": ("sbuf", [128, 128], "float32"),
    "EA": ("sbuf", [128, 144], "float16"), "EB": ("sbuf", [128, 144], "bfloat16"),
    "E8": ("sbuf", [128, 144], "float16"), "EA8": ("sbuf", [128, 144], "float16"), "EB8": ("sbuf", [128, 144], "bfloat16"),
    "par": ("sbuf", [128, 64], "float32"), "pw": ("sbuf", [128, 64], "float16"), "farA": ("sbuf", [128, 64], "float16"),
    "farL": ("sbuf", [128, 64], "float16"), "farB": ("sbuf", [128, 64], "bfloat16"),
    "cl": ("sbuf", [128, 128], "float32"), "SG": ("sbuf", [128, 128], "float32"), "I32": ("sbuf", [128, 128], "float32"),
    "g0": ("sbuf", [128, 128], "float32"), "T2b": ("sbuf", [128, 128], "float32"), "T1b": ("sbuf", [128, 128], "float32"),
    "T1": ("sbuf", [128, 128], "bfloat16"), "T2": ("sbuf", [128, 128], "bfloat16"),
    "T0": ("sbuf", [128, 128], "bfloat16"), "T3": ("sbuf", [128, 128], "bfloat16"), "T4": ("sbuf", [128, 128], "bfloat16"),
    "ones": ("sbuf", [128, 256], "bfloat16"), "xg": ("sbuf", [128, K], "float16"), "xw": ("sbuf", [128, K], "uint16"),
    "I16": ("sbuf", [128, 128], "float16"), "N16": ("sbuf", [128, 128], "float16"), "K16": ("sbuf", [128, 128], "float16"),
    "W16": ("sbuf", [128, 128], "float16"),
    "cz": ("sbuf", [128, 32], "float16"), "co": ("sbuf", [128, 32], "float16"), "anz": ("sbuf", [128, 64], "float32"),
    "PLC": ("sbuf", [128, 288], "float32"), "ri": ("sbuf", [128, 32], "float32"), "rep": ("sbuf", [128, 32], "uint16"),
    "ki": ("sbuf", [128, 32], "float32"), "kk": ("sbuf", [128, 32], "float16"), "kz": ("sbuf", [128, 32], "float32"),
    "yo": ("sbuf", [128, 288], "float32"),
    "z0": ("psum", [128, 512], "float32"), "z1": ("psum", [128, 512], "float32"),
    "B0": ("psum", [128, 512], "float32"), "B1": ("psum", [128, 512], "float32"),
    "B2": ("psum", [128, 512], "float32"), "PB": ("psum", [128, 512], "float32"),
    "PL": ("psum", [128, 512], "float32"), "PT": ("psum", [128, 512], "float32"),
}
PSUM = ("z0", "z1", "B0", "B1", "B2", "PB", "PL", "PT")
NDMA, NREM = 36, 14
SEMAPHORES = ["eV", "eA", "eP", "eG"] + ["d%d" % i for i in range(NDMA)] + ["r%d" % i for i in range(NREM)] + ["l%d" % i for i in range(NREM)]

OPT = {
    "fcut": (0, 128, 256, 512), "feng": "AAA",
    "cut": (0, 256, 512),
    "xcut": (0, 256, 512),
    "dcut": (0, 256, 512), "deng": "VA", "leng": "AA", "vcut": (0, 320, 512), "veng": "AV",
    "wcut": (0, 128, 256, 512), "weng": "VAV",
    "ycut": (0, 256, 512), "yeng": "AAAA", "vclamp": (), "gate": "F", "wown": False, "ahead": (3, 6, 8), "xmode": "NNNN", "gcut": (0, 512), "geng": "AAA", "ccut": (0, 256, 512), "peo": (8, 9), "pem": (), "sp": ("B2", 64), "along": (7,), "dvV": True, "uearly": True,
    "xsplit": True, "cq": ("B2", 0, 32), "sendB": 4, "pD": "ab", "pI": "ab", "half": 1.5, "bcut": (0, 256, 512), "uq": ("B2", 416, 512),
    "zat": (("z0", 0), ("z1", 0), ("z0", 256), ("z1", 208)), "a16": "t", "feng0": "PPV", "rfirst": 4.0,
    "copy": (1, 4, 7),
    "split": (4,),
    "ugroups": ((1, 2), (3,), (4, 5), (6,), (7,), (8,)), "ueng": "AAAAAAAAA",
    "cy": 0.83e-3, "pcy": 0.46e-3, "hop": 0.14, "same": 0.2, "gat": 1.5, "afix": 0.08,
    "loads": "Fm0B1X", "mq": "A", "dfix": 0.95, "drate": 300.0, "rfix": 1.0, "rrate": 80.0, "rissue": 1.2, "seed": 1, "sweeps": 4000, "noise": 1.2, "width": 2.0, "allow": 0.05,
}


def plan(T, g, dst_addr, engines):
    ops = []
    used = {"sm": 0, "sb": 0, "sh": 0, "su": 0, "si": 0}
    CY, PCY, GAT = OPT["cy"], OPT["pcy"], OPT["gat"]

    def new(buf, blocks=1):
        a = used[buf]; used[buf] += 32 * blocks
        return (buf, a, a + 32 * blocks)

    def ap(r):
        return T[r[0]][:, r[1]:r[2]]

    def whole(n):
        return (n, 0, SCRATCH[n][1][1])

    def sub(r, a, b):
        return (r[0], r[1] + a, r[1] + b)

    def blk(r, a, n=1):
        return sub(r, 32 * a, 32 * (a + n))

    def add(eng, fn, rd, wr, cost, kind="c", kb=0.0):
        ops.append({"e": eng, "fn": fn, "rd": rd, "wr": wr, "cost": cost, "kind": kind, "kb": kb})

    def two(r):
        return SCRATCH[r[0]][2] in ("bfloat16", "float16", "uint16")

    def n_of(r):
        return r[2] - r[1]

    def ts(o, i, s1, op0, s2=None, op1=None, cols=()):
        c = max(64, n_of(o) * (0.5 if two(o) and two(i) else 1)) * CY
        if op1 is None:
            add("V", lambda: g.vector.tensor_scalar(ap(o), ap(i), s1, None, op0), [i] + list(cols), [o], c)
        else:
            add("V", lambda: g.vector.tensor_scalar(ap(o), ap(i), s1, s2, op0, op1), [i] + list(cols), [o], c)

    def tt(o, a, b, op):
        c = max(64, n_of(o) * (1 if a[0] in PSUM or b[0] in PSUM else 2)) * CY
        add("V", lambda: g.vector.tensor_tensor(ap(o), ap(a), ap(b), op), [a, b], [o], c)

    def cp(o, i):
        add("V", lambda: g.vector.tensor_copy(ap(o), ap(i)), [i], [o], max(64, n_of(o) * (0.5 if two(o) and two(i) else 1)) * CY)

    def fill(o, v):
        add("V", lambda: g.vector.memset(ap(o), v), [], [o], max(64, n_of(o) * (0.5 if two(o) else 1)) * CY)

    def gt(o, win, off, b, op):
        add("V", lambda: g.vector.tensor_tensor(ap(o), ap(win).indirect(ap(off)), ap(b), op), [win, off, b], [o],
            0.05 + GAT * n_of(o) * CY)

    def act(o, i, func=AF.Identity, bias=0.0, scale=1.0, cols=()):
        add("A", lambda: g.scalar.activation(ap(o), ap(i), func, bias=bias, scale=scale), [i] + list(cols), [o],
            max(64, n_of(o)) * CY + OPT["afix"])

    def gather(eng, o, win, off, bias=0.0, scale=1.0):
        if eng == "A":
            add("A", lambda: g.scalar.activation(ap(o), ap(win).indirect(ap(off)), AF.Identity, bias=bias, scale=scale),
                [win, off], [o], 0.065 + GAT * n_of(o) * CY)
        else:
            add("V", lambda: g.vector.tensor_scalar(ap(o), ap(win).indirect(ap(off)), scale, bias, ALU.mult, ALU.add),
                [win, off], [o], 0.05 + GAT * n_of(o) * CY)

    def pieces(cut, eng):
        return [(cut[i], cut[i + 1], eng[i]) for i in range(len(cut) - 1)]

    def mm(items, start=True, stop=True):
        def fn():
            for i, (o, l, r) in enumerate(items):
                ins = g.tensor.matmul(ap(o), T[l][:, :], ap(r), start and i == 0, stop and i == len(items) - 1)
            return ins
        add("P", fn, [whole(l) for _, l, _ in items] + [r for _, _, r in items], [o for o, _, _ in items],
            sum(max(64, n_of(r)) for _, _, r in items) * PCY)

    def to_list(o, E, x, more=(), stop=True):
        def fn():
            for j in range(16):
                ins = g.tensor.matmul(ap(o), T[E][:, 15 - j:143 - j], T[x[0]][:, x[1] + j:x[2]:16], j == 0, stop and j == 15 and not more)
            for i, (p, l, r) in enumerate(more):
                ins = g.tensor.matmul(ap(p), T[l][:, :], ap(r), False, i == len(more) - 1)
            return ins
        add("P", fn, [whole(E), x] + [whole(l) for _, l, _ in more] + [r for _, _, r in more], [o], 64 * (16 + len(more)) * PCY)

    def least(o, at, E, x, far, M, y, cap):
        def fn():
            for j in range(8):
                g.tensor.matmul(ap(at), T[E][:, 15 - j:143 - j], T[x[0]][:, x[1] + j:x[2]:8], j == 0, False)
            g.tensor.matmul(ap(at), T[far[0]][:, :], T[far[1]][:, :], False, False)
            for h in range(2):
                ins = g.tensor.matmul(T[at[0]][:, at[1] + h:at[2]:2], T[M][:, :], ap(y), False, h == 1)
            return ins
        add("P", fn, [whole(E), x, whole(far[0]), whole(far[1]), whole(M), y], [at], 64 * 11 * PCY)
        half = new("sm")
        add("V", lambda: g.vector.tensor_tensor(ap(half), T[at[0]][:, at[1]:at[2]:2], ap(cap), ALU.min), [at, cap], [half], 64 * CY)
        add("V", lambda: g.vector.tensor_tensor(ap(o), T[at[0]][:, at[1] + 1:at[2]:2], ap(half), ALU.min), [at, half], [o], 64 * CY)

    def dma(q, o, i, rd, wr, kb):
        eng = g.sync if q == "S" else (g.scalar if q == "A" else g)
        add(q, lambda: eng.dma_start(o, i), rd, wr, 0.06, kind="dma", kb=kb)

    def remote(land, src, part="ab"):
        half = len(engines) // 2
        use = (engines[:half] if "a" in part else []) + (engines[half:] if "b" in part else [])
        mask = sum(1 << e for e in use)
        add("G", lambda rs, ls: g.remote_dma(ap(land), ap(src), rs, ls, dst_addr[1], dst_addr[0], mask), [src], [land],
            OPT["rissue"], kind="rem", kb=(n_of(src) * (2 if two(src) else 4) / 8.0 + 20) * (1.0 if part == "ab" else OPT["half"]))
        ops[-1]["part"], ops[-1]["n"] = part, len(use)

    def iota(o, pattern, base, cm):
        if SCRATCH[o[0]][2] == "int32":
            add("G", lambda: g.iota(ap(o), pattern, base, cm), [], [o], 0.13 + 2 * n_of(o) * CY)
        else:
            add("G", lambda: g.iota(ap(o), pattern, base, cm, allow_small_or_imprecise_dtypes=True), [], [o], 0.13 + 2 * n_of(o) * CY)

    def col(j):
        return ("pc", j, j + 1)

    FW, XW, DTW = ("DT", 0, Z), whole("X"), whole("DT")
    for c in OPT["loads"]:
        if c == "m":
            dma(OPT["mq"], T.mi[:, :], T.m0[:, :], [], [whole("mi")], 45)
        if c == "F":
            dma("S", T.DT[:, O:Z], T.fm[:, :], [], [("DT", O, Z)], 420)
        if c == "B":
            dma("A", T.Bi[:, :], T.b0[:, :], [], [whole("Bi")], 160)
        if c in "01":
            gg = int(c)
            dma("S", T.xa[:, 48 * gg:48 * gg + 48], T.nx[16 * gg::32, :], [], [("xa", 48 * gg, 48 * gg + 48)], 55)
        if c == "X":
            dma("S", T.X[:, O:Z], T.nx[:, :], [], [("X", O, Z)], 810)
    iota(("pi", 0, 1), [[0, 1]], 0, 1)
    iota(whole("xi"), [[1, 144]], 0, 0)
    iota(whole("rel"), [[1, 128]], 0, -1)
    ts(("pi", 4, 5), ("pi", 0, 1), 112, ALU.bitwise_and)
    cp(col(0), ("pi", 4, 5))
    tt(col(1), ("pi", 0, 1), ("pi", 4, 5), ALU.subtract)
    ts(col(2), col(1), 1.0, ALU.min, -3.0 * 4096, ALU.mult)
    ts(col(3), col(2), 4096.0, ALU.add)
    ts(col(4), col(1), 15.0, ALU.is_equal, 2048.0, ALU.mult)
    ts(whole("dd"), whole("xi"), ap(col(0)), ALU.subtract, cols=[col(0)])
    ts(whole("EB"), whole("dd"), 15.0, ALU.is_equal, ap(col(3)), ALU.mult, cols=[col(3)])
    ts(whole("EA"), whole("dd"), 15.0, ALU.is_equal)
    ts(whole("cl"), ("dd", 0, 128), 0.0, ALU.max, 15.0, ALU.min)
    tt(whole("SG"), whole("cl"), ("dd", 0, 128), ALU.is_equal)
    ts(whole("I32"), whole("rel"), 0.0, ALU.is_equal)
    ts(whole("g0"), whole("rel"), 0.0, ALU.is_gt, -2.0, ALU.mult)
    tt(whole("T2b"), whole("I32"), whole("g0"), ALU.add)
    tt(whole("T2"), whole("T2b"), whole("SG"), ALU.mult)
    act(whole("T1b"), whole("T2b"), bias=-4.0, scale=512.0)
    tt(whole("T1"), whole("T1b"), whole("SG"), ALU.mult)
    if "N" in OPT["xmode"]:
        ts(whole("T0"), whole("I32"), ap(col(4)), ALU.mult, cols=[col(4)])
        ts(whole("T3"), whole("T1"), 2048.0, ALU.mult); ts(whole("T4"), whole("T2"), 2048.0, ALU.mult)
        fill(whole("ones"), 1.0)
    cp(whole("I16"), whole("I32"))
    for name, v in (("N16", -1.0), ("K16", -4096.0), ("W16", 1024.0)):
        ts(whole(name), whole("I16"), v, ALU.mult)
    ts(col(6), col(1), 15.0, ALU.not_equal, 0.5, ALU.mult)
    ts(col(7), col(6), -1.0, ALU.mult)
    ts(col(8), col(6), 3.0, ALU.mult, -1.0, ALU.add)
    for name, v in (("IB", 1.0), ("NB", -1.0)):
        act(whole(name), whole("I32"), scale=v)
    for name, j in (("IH", 6), ("NC", 7), ("IP", 8), ("H16", 8)):
        act(whole(name), whole("I32"), scale=ap(col(j)), cols=[col(j)])
    iota(whole("PLC"), [[1, 9], [0, 32]], 1, 0)
    iota(("ri", 0, 18), [[0, 9], [16, 2]], 0, 1)
    ts(("rep", 0, 18), ("ri", 0, 18), ap(col(0)), ALU.subtract, cols=[col(0)])
    iota(whole("ki"), [[16, 32]], 0, 1)
    ts(whole("kk"), whole("ki"), ap(col(0)), ALU.subtract, cols=[col(0)])
    ts(whole("kz"), whole("kk"), float(K), ALU.add)
    fill(whole("cz"), float(Z)); fill(whole("co"), float(O)); fill(("anz", 32, 64), 0.0)
    fill(("DT", 0, O), 0.0); fill(("DT", Z, R0), 0.0); fill(("X", 0, O), 0)
    fill(("W", K, 2 * K), 0.0); ops[-1]["early"] = True
    iota(whole("tj"), [[0, 2], [1, 48]], 0, 0)
    remote(whole("lB1"), whole("Bi"))
    first = len(ops) - 1
    ops[first]["rd"].append(FW if OPT["gate"] == "F" else XW); ops[first]["cost"] = OPT["rfirst"]
    ops[first]["after"] = [i for i in range(first) if ops[i]["e"] == "G"]
    for a in range(0, DW, K):
        b = min(a + K, DW)
        dma("S", T.U[:, a:b], T.W[:, K:K + b - a], [XW, ("W", K, 2 * K)], [("U", a, b)], (b - a) / 4 + 25)
    for i in range(2):
        dma("S", T.W[:, 2 * i * K:2 * i * K + K], T.wl[:, i % 2 * K:i % 2 * K + K], [XW], [("W", 2 * i * K, 2 * i * K + K)], 150)
    ts(("pi", 8, 9), ("pi", 0, 1), 31, ALU.bitwise_and)
    ts(col(5), ("pi", 8, 9), 48.0, ALU.mult)
    ts(whole("tm"), whole("tj"), ap(col(5)), ALU.add, cols=[col(5)])
    ts(whole("xp"), whole("xa"), float(O), ALU.add)
    for b in range(3):
        for gg in range(2):
            act(("xf", 32 * b + 16 * gg, 32 * b + 16 * gg + 16), ("xp", 48 * gg + 16 * b, 48 * gg + 16 * b + 16))
    add("V", lambda: g.vector.transpose(T.xt[:, :], T.xf[:, :]), [whole("xf")], [whole("xt")], 96 * CY)
    for b in range(3):
        add("V", lambda b=b: g.vector.tensor_copy(T.xu[:, b:96:3], T.xt[:, 32 * b:32 * b + 32]), [whole("xt")], [blk(whole("xu"), b)], 64 * CY)
    for i in range(3):
        if OPT["feng0"][i] == "P":
            at = (("PL", "PT", "PB")[i], 0, K)
            gather("A", ("F", K * i, K * i + K), FW, blk(whole("xu"), i))
            ops[-1]["rd"].append(whole("xu"))
            mm([(at, "IB", ("F", K * i, K * i + K)), (at, "NB", ("DT", O + K * i, O + K * i + K))])
            act(("DT", R0 + K * i, R0 + K * i + K), at)
            continue
        (cp if OPT["feng0"][i] == "V" else act)(("F", K * i, K * i + K), ("DT", O + K * i, O + K * i + K))
        gt(("DT", R0 + K * i, R0 + K * i + K), FW, blk(whole("xu"), i), ("F", K * i, K * i + K), ALU.subtract)
        ops[-1]["rd"].append(whole("xu"))
    tt(whole("xd"), whole("tm"), whole("xa"), ALU.subtract)
    act(whole("xy"), whole("xd"), scale=1.0 / 8192)
    act(whole("xh"), whole("xy"))
    tt(whole("xl"), whole("xy"), whole("xh"), ALU.subtract)
    for o in ops[-4:]:
        o["early"] = OPT["uearly"]
    for gg in range(2):
        dma("S", T.U[16 * gg + 1::32, R0:DW], T.xh[:, 48 * gg:48 * gg + 48], [whole("xh"), ("U", R0 + 4, DW)], [("U", R0 + gg, R0 + gg + 1)], 40)
        dma("S", T.U[16 * gg + 2::32, R0:DW], T.xl[:, 48 * gg:48 * gg + 48], [whole("xl"), ("U", R0 + 4, DW)], [("U", R0 + 2 + gg, R0 + 3 + gg)], 40)

    mu = new("su"); ts(mu, whole("mi"), float(O), ALU.add)
    m = new("sh"); ts(m, whole("mi"), float(O), ALU.add)
    CUT = [(i, OPT["bcut"][i], OPT["bcut"][i + 1]) for i in range(len(OPT["bcut"]) - 1)]
    FINE = [(max(i for i, c, _ in CUT if c <= a), a, b) for a, b, _ in pieces(OPT["cut"], "VVVVVV")]

    def BA(i, a, b):
        return ("B%d" % i, a - CUT[i][1], b - CUT[i][1])

    def BB(i, a, b):
        return ("B%d" % i, 256 + a - CUT[i][1], 256 + b - CUT[i][1])

    def stocks(terms, start, stop, half=True, only=None):
        for p in CUT:
            if only is None or p[0] == only:
                mm([(BA(*p), x, sub(y, p[1], p[2])) for x, _, y in terms]
                   + [(BB(*p), x, sub(y, p[1], p[2])) for _, x, y in terms if half], start, stop)

    terms = [("IB", "IH", whole("Bi"))]
    stocks(terms, True, True)
    parts, idxs, ams, OCs, bfs, tzs = [], {}, {}, {}, {}, {}
    tl = cn = clip = None
    tz = whole("cz")
    TQ, TN, TW, CN, UQ = ("PT", 0, 128), ("PT", 128, 160), ("PT", 160, 192), ("PT", 192, 256), OPT["uq"]

    wide = [0]

    def logsum(width, start=True, stop=True, now=None):
        now = sorted(parts if now is None else now, key=lambda x: -n_of(x))
        items = []
        if start:
            wide[0] = min(n_of(now[0]), 32 * width)
        for x in now:
            n = min(n_of(x), 32 * width)
            items += [(("PL", a, b), "I16", sub(x, a, b)) for a, b in ((0, min(n, wide[0])), (wide[0], n)) if a < b]
            wide[0] = max(wide[0], n)
        mm(items, start, stop)

    def repeat(o, x, y, op, pe):
        k = n_of(o) // 32
        if pe:
            at = (OPT["sp"][0], OPT["sp"][1], OPT["sp"][1] + 32 * k)
            mm([(blk(at, i), "IB" if x[0] == "sb" else "I16", x) for i in range(k)])
            tt(o, at, y, op)
        else:
            gt(o, x, ("rep", 0, 2 * k), y, op)

    def place(s, value):
        M = new("sh", s); repeat(M, value, OCs[s], ALU.mult, value[0] == "sh")
        parts.append(M)

    def below(s, tl):
        more = []
        if s >= 2:
            M4 = new("sh", s - 1)
            if s == 2:
                tt(M4, ams[0], blk(OCs[s], 1), ALU.mult)
            else:
                tt(M4, ("PL", 0, 32 * s - 32), blk(OCs[s], 1, s - 1), ALU.mult)
            more = [(blk(TQ, 0), "I16", blk(M4, i)) for i in range(s - 1)]
        mm([(blk(TQ, 0), "N16", tl)] + more)

    def partners(n, group):
        if group[0] in OPT["along"]:
            gather(OPT["ueng"][group[0]], ("st%d" % ((group[0] + 1) % 2), K, 2 * K), whole("U"), idxs[group[0]])
            return
        ug = ("ug%d" % (n % 2), 0, K * len(group))
        for i, s in enumerate(group):
            gather(OPT["ueng"][s], sub(ug, K * i, K * i + K), whole("U"), tzs[s] if s in OPT["ahead"] else idxs[s])
        uq = blk(UQ, 0, len(group))
        to_list(uq, "EB", ug, [(blk(uq, i), "I16", ams[s - 1]) for i, s in enumerate(group)
                               if s > 1 and s not in OPT["split"] + OPT["ahead"]])
        for i, s in enumerate(group):
            if s in OPT["ahead"]:
                p, dv = new("sm"), new("sh" if s in OPT["pem"] else "sm")
                tt(p, blk(uq, i), bfs[s], ALU.mult); tt(dv, p, ams[s - 1], ALU.add); place(s, dv)
            elif s == 1:
                dv = new("sh"); cp(dv, blk(uq, i)); parts.append(dv)
            else:
                dv = new("sh" if s in OPT["pem"] else "sm"); act(dv, blk(uq, i)); place(s, dv)

    for s in range(NST):
        last = s == NST - 1
        vend = s % S_ == S_ - 1 and not last
        st, lw, mk, xs, fg = ((x + str(s % 2), 0, K) for x in ("st", "lw", "mk", "xs", "fg"))
        if s >= 2:
            OCs[s] = new("sb", s); repeat(OCs[s], blk(cn, 0), ("PLC", 0, 32 * s), ALU.is_equal, s in OPT["peo"])
            if s in OPT["split"]:
                place(s, ams[s - 1])
        if s >= 1:
            if not last:
                if s - 1 not in OPT["along"]:
                    below(s, tl)
                mm([(blk(TQ, 1), "I16", m), (blk(TQ, 1), "N16", tl)])
                if not vend:
                    mm([(blk(TQ, 2), "I16", m), (blk(TQ, 3), "I16", m)])
            else:
                mm([(blk(TQ, 2), "I16", m), (blk(TQ, 2), "N16", whole("co")), (blk(TQ, 3), "I16", m)])
                ON = new("sb", 9); repeat(ON, blk(cn, 1), whole("PLC"), ALU.is_equal, 9 in OPT["peo"])
        for a, b, e in pieces(OPT["fcut"], OPT["feng"]):
            gather(e, sub(fg, a, b), FW, sub(mu, a // 16, b // 16))
        for i, a, b in FINE:
            tt(sub(st, a, b), sub(fg, a, b), BA(i, a, b), ALU.is_gt)
            tt(sub(lw, a, b), sub(fg, a, b), BB(i, a, b), ALU.is_gt)
        shift = 0.0
        if s in OPT["vclamp"]:
            for i, a, b in CUT:
                ts(("ex", a, b), BA(i, a, b), 255.0, ALU.min)
            terms = [("IB", "IH", whole("ex"))]
        elif s % S_ == 0 and s:
            for i, a, b in CUT:
                act(("ex", a, b), BA(i, a, b), AF.Relu, bias=255.0, scale=-1.0)
            terms, shift = [("NB", "NC", whole("ex"))], 255.0
            if s == S_:
                remote(whole("lB2"), whole("ex"))
        elif s == 2 * S_ - 1:
            shift = -128.0 if s - 1 in OPT["copy"] else 0.0
        elif s in OPT["copy"]:
            Bs, shift = whole("Bs%d" % (s % 2)), 128.0 if s > 1 else 0.0
            for i, a, b in CUT:
                act(sub(Bs, a, b), BA(i, a, b), bias=-shift)
            terms = [("IB", "IH", Bs)]
        ends = [(("B%d" % (i % 2), 256 * (i // 2), 256 * (i // 2) + b - a), a, b, e)
                for i, (a, b, e) in enumerate(pieces(OPT["ycut"], OPT["yeng"]))]
        if last:
            for at, a, b, _ in ends[:2]:
                mm([(at, x, sub(y, a, b)) for x, _, y in terms], True, False)
        elif not vend:
            stocks(terms, True, False)
        Cq = OPT["cq"]
        idx = idxs[s] = new("su")
        FL = new("sh", 2); bf, ok = blk(FL, 0), blk(FL, 1)
        bfs[s], tzs[s] = bf, tz
        if s - 1 in OPT["along"]:
            to_list(sub(Cq, 0, 64), "EB", whole(st[0]), [(Cq, "I16", m), (sub(Cq, 32, 64), "I16", ams[s - 2])])
        else:
            to_list(Cq, "EB", st, [(Cq, "I16", m)])
        tt(idx, Cq, tz, ALU.min)
        tt(ok, Cq, m, ALU.is_equal)
        if s - 1 in OPT["along"]:
            dv = new("sm"); (cp if OPT["dvV"] else act)(dv, sub(Cq, 32, 64)); place(s - 1, dv)
            if not last:
                logsum(s - 1); below(s, tl)
        if s:
            ts(bf, idx, float(Z), ALU.is_gt)
        for i, (_, a, b) in enumerate(FINE):
            z = (OPT["zat"][i][0], OPT["zat"][i][1], OPT["zat"][i][1] + b - a)
            if OPT["xmode"][i] == "R" or s == 0:
                mm([(z, "T1", sub(st, a, b)), (z, "T2", sub(lw, a, b))])
                act(sub(mk, a, b), z, AF.Relu, bias=ap(col(4)), scale=2048.0, cols=[col(4)])
                gt(sub(xs, a, b), XW, sub(mu, a // 16, b // 16), sub(mk, a, b), ALU.min)
            else:
                if i == 0:
                    for c, d, e in pieces(OPT["gcut"], OPT["geng"]):
                        gather(e, ("xg", c, d), XW, sub(mu, c // 16, d // 16), bias=0.0 if last else float(O))
                if not lifted:
                    mm([(z, "T0", ("ones", 0, b - a))], stop=False)
                mm([(z, "T3", sub(st, a, b)), (z, "T4", sub(lw, a, b))], start=lifted)
                tt(("xw", a, b), z, ("xg", a, b), ALU.min)
                if b in OPT["ccut"]:
                    c = OPT["ccut"][OPT["ccut"].index(b) - 1]
                    cp(sub(xs, c, b), ("xw", c, b))
        PA = ("PB", 64, 96)
        msg = new("su", 6) if vend else None
        mn = new("sm" if last else "sh"); mun = blk(msg, 0) if vend else new("su")
        if s == 0:
            to_list(PA, "EA", xs)
            ts(mun, PA, float(O), ALU.add)
            ts(mn, PA, float(O), ALU.add)
            tln = ams[0] = new("sh"); tt(tln, ok, m, ALU.mult)
            tzn = new("sm"); ts(tzn, tln, float(Z), ALU.add)
            parts.append(tln)
            cnn = new("sb", 2); cp(blk(cnn, 0), ok); ts(blk(cnn, 1), ok, 1.0, ALU.add)
        else:
            if vend:
                w = new("sh"); tt(w, bf, m, ALU.mult); tt(blk(msg, 2), ok, m, ALU.mult)
            else:
                wa = new("sm" if (last and 9 not in OPT["pem"]) or s + 1 in OPT["split"] else "sh", 2); w, ams[s] = blk(wa, 0), blk(wa, 1)
                tt(wa, blk(TQ, 2, 2), FL, ALU.mult)
            more = [(PA, "K16", bf)]
            if OPT["xsplit"]:
                to_list(PA, "EA", xs, stop=False)
                mm(more, start=False)
            else:
                to_list(PA, "EA", xs, more)
            tt(mn if last else mun, PA, w, ALU.max)
            if not (last or vend):
                (act if "m" in OPT["a16"] else cp)(mn, mun)
            tt(("anz", 0, 32), ok, blk(cn, 1), ALU.mult)
            if last:
                mm([(blk(CN, 0), "IB", blk(cn, 0)), (blk(CN, 0), "N16", bf)])
                cnn = new("sm"); tt(cnn, blk(CN, 0), ("anz", 0, 32), ALU.max)
            else:
                mm([(CN, "IB", cn), (blk(CN, 0), "N16", bf), (blk(CN, 1), "I16", ok)])
                cnn = blk(msg, 3, 2) if vend else new("sb", 2)
                tt(cnn, CN, whole("anz"), ALU.max)
                pr = new("sh", 2); tt(pr, blk(TQ, 0, 2), FL, ALU.mult)
                three = [tl, blk(pr, 0), blk(pr, 1)]
                if vend:
                    mm([(TW, "W16", x) for x in three] + [(TW, "I16", whole("kk"))])
                mm([(TN, "I16", x) for x in three])
                tln = blk(msg, 1) if vend else new("sh")
                (act if "t" in OPT["a16"] else cp)(tln, TN)
                if not vend:
                    tzn = new("su" if s + 1 in OPT["ahead"] else "sm"); act(tzn, TN, bias=float(Z))
        dg = whole("dh" if shift == 255.0 else "dg%d" % (s % 3))
        terms = terms + [("I16", "H16", dg) if shift == 255.0 else ("IB", "IP" if shift > 0 else "IH", dg)]
        lifted = any(x in ("IP", "H16") for _, x, _ in terms)
        for a, b, e in pieces(OPT["vcut"], OPT["veng"]) if vend else pieces(OPT["ycut" if last else "dcut"], OPT["leng" if last else "deng"]):
            gather(e, sub(dg, a, b), DTW if s else ("DT", 0, R0), sub(idx, a // 16, b // 16), bias=shift, scale=-1.0)
        if last:
            for i, (at, a, b, _) in enumerate(ends):
                mm([(at, x, sub(y, a, b)) for x, _, y in (terms[-1:] if i < 2 else terms)], i >= 2, True)
                if i >= 2:
                    ops[-1]["rd"].append(ends[i - 2][0])
        elif not vend:
            stocks(terms[-1:], False, True)
        if s < S_ - 1:
            remote(whole("lE%d" % s), dg)
        if S_ <= s < 2 * S_ - 1:
            remote(whole("lH" if s == S_ else "lE2"), dg)
        if vend:
            v = s // S_ + 1
            lB, lD, lI, lL = (whole(x + str(v)) for x in ("lB", "lD", "lI", "lL"))
            ti = new("si"); tt(ti, TW, whole("kz"), ALU.max)
            x = new("si"); ts(x, ti, 4 * K - 1, ALU.bitwise_and)
            if clip is None:
                e0, e1, lo, hi = new("sm"), new("sm"), new("sm"), new("sm")
                ts(e0, x, float(K), ALU.is_lt, float(K), ALU.mult); tt(lo, e0, whole("kk"), ALU.add)
                ts(e1, x, 2.0 * K, ALU.is_lt, float(K), ALU.mult); tt(hi, e1, whole("kz"), ALU.add)
                clip = (lo, hi)
                cp(blk(msg, 5), x)
            else:
                x1 = new("sm")
                tt(x1, x, clip[0], ALU.max); tt(blk(msg, 5), x1, clip[1], ALU.min)
            remote(lD, dg, OPT["pD"])
            remote(lI, msg, OPT["pI"])
        for n, group in enumerate(OPT["ugroups"]):
            if group[-1] == s:
                if last:
                    M5 = new("sh", 9); repeat(M5, ams[s], ON, ALU.mult, 9 in OPT["pem"])
                    logsum(9, stop=False, now=parts[:-1])
                    for x in (parts[-1], M5):
                        logsum(9, start=False, stop=False, now=[x])
                    del parts[:]
                partners(n, group)
        if last:
            for at, a, b, e in ends:
                part = ("Bf", a, b)
                (act if e == "A" else cp)(part, at)
                dma("S", T.yb[:, a:b], ap(part), [part], [], (b - a) / 2 + 32)
            logsum(9, start=False)
            ts(whole("yo"), ("PL", 0, 288), -float(O), ALU.add, -1.0, ALU.max)
            yc = new("sm"); act(yc, cnn, bias=-1.0)
            dma("S", T.yc[:, :], ap(yc), [yc], [], 48)
            dma("A", T.yl[:, :], T.yo[:, :], [whole("yo")], [], 176)
            dma("S", T.ym[:, :], ap(mn), [mn], [], 48)
            break
        if vend:
            logsum(s)
            lg = new("sh", s); cp(lg, ("PL", 0, 32 * s))
            remote(lL, lg)
            parts[:] = [lL]
            mun = blk(lI, 0)
            ta = new("sh", 3); cp(ta, blk(lI, 0, 3)); mn, tln, ams[s] = blk(ta, 0), blk(ta, 1), blk(ta, 2)
            tzn = new("su" if s + 1 in OPT["ahead"] else "sm"); ts(tzn, blk(lI, 1), float(Z), ALU.add)
            cnn = new("sb", 2); cp(cnn, blk(lI, 3, 2))
            for a, b, e in pieces(OPT["wcut"], OPT["weng"]):
                gather(e, ("wg", a, b), whole("W"), sub(blk(lI, 5), a // 16, b // 16))
            come = [lB] + ([whole("lE0"), whole("lE1")] if v == 1 else [whole("lH"), whole("lE2")]) + [lD, whole("wg")]
            for i, x in enumerate(come):
                stocks([{"lB2": ("NB", "NC"), "lH": ("I16", "H16")}.get(x[0], ("IB", "IH")) + (x,)], i == 0, x == come[-1])
            lifted = whole("lH") in come
        if 2 <= s < NST - 2 and s not in OPT["along"]:
            logsum(s)
        m, mu, tl, tz, cn = mn, mun, tln, tzn, cnn
    return ops


def depend(ops):
    def meet(a, b):
        return a[0] == b[0] and a[1] < b[2] and b[1] < a[2]
    deps = []
    for i, o in enumerate(ops):
        d = {}
        for j in range(i):
            p = ops[j]
            if any(meet(a, b) for a in o["rd"] + o["wr"] for b in p["wr"]):
                d[j] = "done"
            elif any(meet(a, b) for a in o["wr"] for b in p["rd"]):
                d[j] = "left" if p["kind"] == "rem" else "done"
        for j in o.get("after", ()):
            d.setdefault(j, "issued")
        deps.append(d)
    return deps


def banks(o):
    return {r[0] for r in o["rd"] + o["wr"] if r[0] in PSUM}


def timing(ops, deps):
    HOP, SAME = OPT["hop"], OPT["same"]
    span, uses, lag = [], [], []
    for i, o in enumerate(ops):
        c, u = o["cost"], [(o["e"], 0.0, o["cost"], 0.0)] + [(k, 0.0, o["cost"], HOP) for k in banks(o)]
        if o["kind"] != "c":
            fix, rate = (OPT["dfix"], OPT["drate"]) if o["kind"] == "dma" else (OPT["rfix"], OPT["rrate"])
            u += [(k, c + fix, o["kb"] / rate, 0.0) for k in o.get("part", ["dma"])]; c += fix + o["kb"] / rate
        span.append(c); uses.append(u)
        lag.append({j: HOP if ops[j]["e"] != o["e"] or ops[j]["kind"] != "c" else (0.0 if o["e"] == "P" else SAME) for j in deps[i]})
        for j, how in deps[i].items():
            if how == "issued":
                lag[i][j] = ops[j]["cost"] - span[j]
    return span, uses, lag


def sweep(ops, span, uses, before, key):
    n = len(ops)
    after = [[] for _ in ops]
    for i in range(n):
        for j in before[i]:
            after[j].append(i)
    left = [len(d) for d in before]; start = [0.0] * n; taken = {}
    cand = [(key[i], i) for i in range(n) if left[i] == 0]
    while cand:
        c = min(cand); cand.remove(c); i = c[1]; e = ops[i]["e"]
        t = max([start[j] + span[j] + d for j, d in before[i].items()] + [0.0])
        busy = []
        for k, off, ln, pad in uses[i]:
            for a, b, f in reversed(taken.get(k, ())):
                if a < t + off - 4.5:
                    break
                if b + pad - off > t and not (pad and f == e):
                    busy.append((a - pad - off - ln, b + pad - off))
        for a, b in sorted(busy):
            if a < t - 1e-9 and t < b:
                t = b
        start[i] = t
        for k, off, ln, pad in uses[i]:
            row = taken.setdefault(k, []); q = len(row)
            while q and row[q - 1][0] > t + off:
                q -= 1
            row.insert(q, (t + off, t + off + ln, e))
        for k in after[i]:
            left[k] -= 1
            if left[k] == 0:
                cand.append((key[k], k))
    return start, max(start[i] + span[i] for i in range(n))


def schedule(ops, deps):
    n = len(ops)
    span, uses, lag = timing(ops, deps)
    back = [{} for _ in ops]
    for i in range(n):
        for j, d in lag[i].items():
            back[j][i] = d
    mirror = [[(k, span[i] - off - ln, ln, pad) for k, off, ln, pad in uses[i]] for i in range(n)]
    loads = [i for i in range(n) if ops[i]["kind"] == "dma" and not deps[i]]
    early = [i for i in range(n) if ops[i].get("early") or (ops[i]["kind"] == "dma" and ops[i]["wr"])]
    tail = [0.0] * n
    for i in range(n - 1, -1, -1):
        tail[i] = span[i] + max([tail[k] + d for k, d in back[i].items()] + [0.0])
    key, best, top, x = [-t for t in tail], None, None, OPT["seed"]
    for it in range(OPT["sweeps"]):
        for i in early:
            key[i] = i - 1000.0
        start, end = sweep(ops, span, uses, lag, key)
        if top is None or end <= top[1]:
            top = (start, end)
        if best is None or end <= best[1] + OPT["allow"] * (1.0 - it / OPT["sweeps"]):
            best = (start, end)
        noise = []
        x = (x * 1103515245 + 12345) % 2147483648
        mid = best[1] * x / 2147483648.0
        for i in range(n):
            x = (x * 1103515245 + 12345) % 2147483648
            noise.append(OPT["noise"] * (x / 2147483648.0 - 0.5) if abs(best[0][i] - mid) < OPT["width"] and x % 8192 < 2048 else 0.0)
        late, _ = sweep(ops, span, mirror, back, [noise[i] - best[0][i] - span[i] for i in range(n)])
        key = [-late[i] - span[i] for i in range(n)]
    return sorted(range(n), key=lambda i: (i not in loads, top[0][i], i)), top[1]


MADE = {}


def rank_program(g, core, T, topo):
    rank = T.rank_of(core)
    if rank is None:
        return
    dst = T.cores[(rank + 1) % len(T.cores)]
    ops = plan(T, g, topo.addr(dst, core), topo.engines(core, dst))
    if not MADE:
        deps = depend(ops)
        seq, MADE["time"] = schedule(ops, deps)
        latest = {}
        for i in seq:
            for k in banks(ops[i]):
                for e, j in latest.setdefault(k, {}).items():
                    if e != ops[i]["e"]:
                        deps[i][j] = "done"
                latest[k][ops[i]["e"]] = i
        MADE["deps"], MADE["seq"] = deps, seq
    deps, seq = MADE["deps"], MADE["seq"]
    pos = {i: k for k, i in enumerate(seq)}
    queue = {"V": g.vector, "A": g.scalar, "P": g.tensor, "G": g, "S": g.sync}
    count = {e: 0 for e in "VAPG"}
    know = {e: {} for e in "VAPGS"}
    token = {}; clock = {}; nd = 0; nr = 0; total = {}
    for i in seq:
        o = ops[i]; e = o["e"]; kn = know[e]
        need = {}
        for j, how in deps[i].items():
            if how == "issued" or (e == "P" and ops[j]["e"] == "P"):
                continue
            sem, val = token[(j, how)]
            if kn.get(sem, 0) < val and need.get(sem, (0, 0))[0] < val:
                need[sem] = (val, j)
        for sem, (val, j) in sorted(need.items(), key=lambda x: -pos[x[1][1]]):
            if kn.get(sem, 0) >= val:
                continue
            queue[e].wait_ge(T.sem[sem], val)
            kn[sem] = val
            if not sem.startswith("r"):
                for s2, v2 in clock[j].items():
                    if kn.get(s2, 0) < v2:
                        kn[s2] = v2
        clock[i] = dict(kn)
        if o["kind"] == "dma":
            sem = "d%d" % nd; nd += 1
            o["fn"]().then_inc(T.sem[sem], 16); token[(i, "done")] = (sem, 16); total[sem] = 16
        elif o["kind"] == "rem":
            rs, ls = "r%d" % nr, "l%d" % nr; nr += 1
            o["fn"](T.sem[rs], T.sem[ls]); neng = o["n"]
            token[(i, "done")] = (rs, neng); token[(i, "left")] = (ls, neng); total[rs] = neng; total[ls] = neng
        else:
            count[e] += 1
            o["fn"]().then_inc(T.sem["e" + e], 1); token[(i, "done")] = ("e" + e, count[e]); total["e" + e] = count[e]
    for sem, val in total.items():
        g.wait_ge(T.sem[sem], val)
